import numpy as np
import ml_dtypes


def mxq(x, axis, fmt="e4m3"):
    dtype, down = {"e4m3": (ml_dtypes.float8_e4m3fn, 7), "e5m2": (ml_dtypes.float8_e5m2, 14)}[fmt]
    v = np.moveaxis(np.asarray(x, np.float32).astype(ml_dtypes.bfloat16).astype(np.float64), axis, -1)
    blocks = v.reshape(v.shape[:-1] + (-1, 32))
    amax = np.abs(blocks).max(-1, keepdims=True)
    byte = np.maximum(np.where(amax > 0, np.frexp(amax)[1] - 1 + 127, 0) - down, 1)
    scale = np.exp2(byte - 127.0)
    codes = (blocks / scale).astype(np.float32).astype(dtype).astype(np.float64)
    return np.moveaxis((codes * scale).reshape(v.shape), -1, axis)


WIDE = False


def mx_kscale(k):
    if not WIDE:
        return np.ones(k)
    levels = np.array([30, -30])
    if k % 512:
        return np.exp2(np.random.permutation(np.resize(levels, k // 32))).repeat(32)
    a = np.empty((k // 512, 16))
    for p in range(k // 512):
        a[p, :8] = np.random.permutation(np.resize(levels, 8))
        for g in range(8):
            far = levels[np.abs(levels - a[p, g]) >= 10]
            a[p, g + 8] = far[np.random.randint(len(far))]
    return np.exp2(a.ravel()).repeat(32)


BF16 = ml_dtypes.bfloat16


def bf(x):
    return np.asarray(x, np.float32).astype(BF16)


def f64(x):
    return np.asarray(x).astype(np.float64)


E2M1 = np.array([0.0, 0.5, 1.0, 1.5, 2.0, 3.0, 4.0, 6.0, -0.0, -0.5, -1.0, -1.5, -2.0, -3.0, -4.0, -6.0])


def pack_weight(w, fmt):
    k, n = w.shape
    w = f64(bf(w)).reshape(k // 32, 32, n)
    amax = np.abs(w).max(1)
    if fmt == "e4m3":
        byte = np.frexp(amax)[1] - 1 + 127 - 7
    else:
        mant, ex = np.frexp(amax / 6.0)
        byte = np.where(mant > 0.5, ex, ex - 1) + 127
    byte = np.clip(np.where(amax > 0, byte, 1), 1, 254)
    scaled = (w * np.exp2(127.0 - byte)[:, None, :]).reshape(k, n).astype(np.float32)
    by_word = np.ascontiguousarray(scaled.reshape(k // 512, 128, 4, n).transpose(0, 1, 3, 2))
    if fmt == "e4m3":
        words = by_word.astype(ml_dtypes.float8_e4m3fn).view(np.uint8)
    else:
        c = by_word.astype(ml_dtypes.float4_e2m1fn).view(np.uint8) & 0xF
        words = c[..., 0::2] | (c[..., 1::2] << 4)
    return np.ascontiguousarray(words), np.ascontiguousarray(byte.astype(np.uint8).reshape(k // 512, 16, n))


def unpack_weight(words, scales, fmt):
    g, p, n, _ = words.shape
    if fmt == "e4m3":
        vals = np.ascontiguousarray(words).view(ml_dtypes.float8_e4m3fn).astype(np.float64)
    else:
        nib = np.empty((g, p, n, 4), np.uint8)
        nib[..., 0::2] = words & 0xF
        nib[..., 1::2] = words >> 4
        vals = E2M1[nib]
    vals = vals * np.repeat(np.exp2(scales.astype(np.float64) - 127.0), 8, axis=1)[..., None]
    return vals.transpose(0, 1, 3, 2).reshape(g * 512, n)
def pack4(w):
    words, scales = pack_weight(w, "e2m1")
    return words.reshape(words.shape[0], 128, -1), scales


def unpack4(words, scales):
    return unpack_weight(words.reshape(words.shape[0], 128, -1, 2), scales, "e2m1")


M, K, N = 512, 1024, 2048


def setup_inputs():
    s = mx_kscale(K)
    t = mx_kscale(N)
    u = np.random.standard_normal((M, K))
    gain = (1 + 0.1 * np.random.standard_normal(K)) * s
    w = np.random.standard_normal((K, N)) / np.sqrt(K) / s[:, None] / t
    c = (1 + 0.1 * np.random.standard_normal(N)) * t
    teacher = np.random.standard_normal((K, N)) / np.sqrt(K) / s[:, None]
    words, scales = pack4(teacher)
    return {"u": bf(u), "gain": bf(gain), "w": bf(w), "c": bf(c),
            "teacher_words": words, "teacher_scales": scales}


def reference(u, gain, w, c, teacher_words, teacher_scales):
    gain, w, c = f64(gain), f64(w), f64(c)
    x = mxq(f64(u) * gain, 1, "e4m3")
    zt = x @ unpack4(teacher_words, teacher_scales)
    zs = (x @ mxq(w, 0, "e4m3")) * c
    d = (zs - zt) * c
    dx = mxq(d, 1, "e5m2") @ mxq(w, 1, "e4m3").T
    du = dx * gain
    return zs, zt, du

@@ -1,0 +1,376 @@
+from contextlib import ExitStack
+
+import concourse.mybir as mybir
+from concourse.masks import make_identity
+
+M, K, N = 512, 1024, 2048
+FLOPS = 3 * 2 * M * K * N
+F32 = mybir.dt.float32
+BF16 = mybir.dt.bfloat16
+U32 = mybir.dt.uint32
+I32 = mybir.dt.int32
+U8 = mybir.dt.uint8
+E4M3 = mybir.dt.float8_e4m3fn_x4
+E5M2 = mybir.dt.float8_e5m2_x4
+E2M1 = mybir.dt.float4_e2m1fn_x4
+MULT = mybir.AluOpType.mult
+SUB = mybir.AluOpType.subtract
+
+P = 128
+MT = M // P
+KG = K // 512
+NG = N // 512
+K_ENG = {0: 1, 1: 1, 2: 1}
+K_AT = {0: [4, 5, 6, 7], 1: [8, 9], 2: [10, 11], 3: [12, 13], 4: [14, 15]}
+QK_AT = {0: [(1, 0)], 1: [(1, 1)], 2: [(2, 0)], 3: [(2, 1)], 4: [(3, 0)], 5: [(3, 1)]}
+N_AT = {0: [4], 1: [5], 2: [6, 7], 3: [8, 9], 4: [10, 11], 5: [12, 13], 6: [14, 15]}
+QN_AT = {2: [(1, 0)], 3: [(1, 1)], 4: [(2, 0)], 5: [(2, 1)], 6: [(3, 0)], 7: [(3, 1)]}
+
+
+def tile_teacher_student_logits_s9_kernel(tc, u, gain, w, c, teacher_words, teacher_scales, zs_out, zt_out, du_out):
+    nc = tc.nc
+    with ExitStack() as ctx:
+        keep = ctx.enter_context(tc.tile_pool(name="keep", bufs=1))
+        work = ctx.enter_context(tc.tile_pool(name="work", bufs=3))
+        psum = ctx.enter_context(tc.psum_pool(name="psum", bufs=2))
+        ident = keep.tile([P, P], F32, name="ident", align_bytes=64)
+        ident_b = keep.tile([P, P], BF16, name="ident_b", align_bytes=64)
+        rows = keep.tile([P, 512], BF16, name="rows", align_bytes=64)
+        cg = keep.tile([P, 6, 4], BF16, name="cg", align_bytes=64)
+        gain_bc = keep.tile([P, KG * 512], BF16, name="gain_bc", align_bytes=64)
+        c_bc = keep.tile([P, NG * 512], BF16, name="c_bc", align_bytes=64)
+        x_codes = keep.tile([P, MT, KG * P], U32, name="x_codes", align_bytes=64)
+        x_scales = keep.tile([P, MT, KG * P], U8, name="x_scales", align_bytes=64)
+        t_words = keep.tile([P, KG, 2 * N], U8, name="t_words", align_bytes=64)
+        t_scales = keep.tile([P, KG, N], U8, name="t_scales", align_bytes=64)
+        w_raw = keep.tile([P, NG, KG, 4, 512], BF16, name="w_raw", align_bytes=64)
+        wk_codes = keep.tile([P, NG, KG, 512], U32, name="wk_codes", align_bytes=64)
+        wk_scales = keep.tile([P, NG, KG, 512], U8, name="wk_scales", align_bytes=64)
+        wn_codes = keep.tile([P, NG, KG, 512], U32, name="wn_codes", align_bytes=64)
+        wn_scales = keep.tile([P, NG, KG, 512], U8, name="wn_scales", align_bytes=64)
+        d_codes = keep.tile([P, NG, MT, P], U32, name="d_codes", align_bytes=64)
+        d_scales = keep.tile([P, NG, MT, P], U8, name="d_scales", align_bytes=64)
+        u_sb = keep.tile([P, MT, K], BF16, name="u_sb", align_bytes=64)
+
+        make_identity(nc, ident[:])
+        nc.vector.memset(rows[:], 0.0)
+        nc.vector.memset(t_scales[:].rearrange("p g n -> p (g n)").bitcast(I32), 0)
+        nc.scalar.dma_start(out=rows[0:4, :], in_=c.rearrange("(g n) -> g n", g=4))
+        nc.scalar.dma_start(out=rows[4:6, :], in_=gain.rearrange("(g n) -> g n", g=2))
+        nc.vector.tensor_copy(out=ident_b[:], in_=ident[:])
+
+        def load_u(m):
+            nc.sync.dma_start(out=u_sb[:, m, :], in_=u[m * P : (m + 1) * P, :])
+
+        def load_w(g, kg):
+            nc.sync.dma_start(
+                out=w_raw[:, g, kg, :, :],
+                in_=w[512 * kg : 512 * (kg + 1), 512 * g : 512 * (g + 1)].rearrange("(p j) n -> p j n", j=4),
+            )
+
+        def load_teacher(half):
+            cols = slice(half * N, (half + 1) * N)
+            nc.sync.dma_start(
+                out=t_words[:, :, cols].bitcast(I32),
+                in_=teacher_words.rearrange("g p n -> p g n")[:, :, cols].bitcast(I32),
+            )
+
+        def load_teacher_scales():
+            for q in range(4):
+                nc.sync.dma_start(
+                    out=t_scales[32 * q : 32 * q + 4, :, :].bitcast(I32),
+                    in_=teacher_scales[:, 4 * q : 4 * q + 4, :].rearrange("g r n -> r g n").bitcast(I32),
+                )
+
+        load_w(0, 0)
+        load_u(0)
+        load_w(0, 1)
+        load_u(1)
+        load_teacher_scales()
+        load_teacher(0)
+        load_u(2)
+        load_u(3)
+        load_w(1, 0)
+        load_w(1, 1)
+        load_teacher(1)
+        load_w(2, 0)
+        load_w(2, 1)
+        load_w(3, 0)
+        load_w(3, 1)
+
+        def make_cg():
+            ps = psum.tile([P, 4, P], BF16, name="ps_rows", tag="e")
+            for t in range(4):
+                nc.tensor.transpose(ps[:, t, :], rows[:, t:512:4], ident_b[:])
+            nc.vector.tensor_copy(out=cg[:], in_=ps[:, :, 0:6].rearrange("p t r -> p r t"))
+
+        def broadcast_rows(first, dst, tag):
+            ps = psum.tile([P, 2, 4, P], BF16, name="ps_bc", tag=tag)
+            for r in range(2):
+                for t in range(4):
+                    nc.tensor.transpose(ps[:, r, t, :], cg[:, first + r, t : t + 1].to_broadcast([P, P]), ident_b[:])
+            nc.scalar.copy(out=dst.rearrange("p (r q t) -> p r q t", r=2, t=4), in_=ps[:].rearrange("p r t q -> p r q t"))
+
+        x_bf = {}
+        x_grp = {}
+
+        def x_mul(m):
+            x_bf[m] = work.tile([P, K], BF16, name="x_bf", align_bytes=64)
+            nc.vector.tensor_tensor(out=x_bf[m][:], in0=u_sb[:, m, :], in1=gain_bc[:], op=MULT)
+
+        def x_turn(m, eng):
+            ps = psum.tile([P, KG * 2, P], F32, name="ps_x", tag="e")
+            words = x_bf[m][:].bitcast(F32)
+            for kg in range(KG):
+                for e in range(2):
+                    nc.tensor.transpose(ps[:, 2 * kg + e, :], words[:, 256 * kg + e : 256 * (kg + 1) : 2], ident[:])
+            x_grp[m] = work.tile([P, KG * P * 4], BF16, name="x_grp", align_bytes=64)
+            for_out = x_grp[m][:].bitcast(F32).rearrange("p (g m e) -> p g m e", g=KG, e=2)
+            for_in = ps[:].rearrange("p (g e) m -> p g m e", e=2)
+            if eng == 0:
+                nc.scalar.copy(out=for_out, in_=for_in)
+            else:
+                nc.vector.tensor_copy(out=for_out, in_=for_in)
+
+        def x_quant(m):
+            nc.vector.quantize_mx(out=x_codes[:, m, :].bitcast(E4M3), scales=x_scales[:, m, :], in_=x_grp[m][:])
+
+        wk_grp = {}
+        wn_grp = {}
+
+        def w_inter(g, kg, a, b, eng):
+            if (g, kg) not in wk_grp:
+                wk_grp[g, kg] = work.tile([P, 2048], BF16, name="wk_grp", align_bytes=64)
+            dst = wk_grp[g, kg][:, 4 * a : 4 * b].rearrange("p (n i j) -> p n j i", j=4, i=4)
+            src = w_raw[:, g, kg, :, a:b].rearrange("p j (n i) -> p n j i", i=4)
+            if eng == 0:
+                nc.scalar.copy(out=dst, in_=src)
+            elif eng == 2:
+                nc.gpsimd.tensor_scalar(out=dst, in0=src, scalar1=1.0, scalar2=0.0, op0=MULT, op1=mybir.AluOpType.add)
+            else:
+                nc.vector.tensor_copy(out=dst, in_=src)
+
+        def wk_quant(g, kg):
+            nc.vector.quantize_mx(out=wk_codes[:, g, kg, :].bitcast(E4M3), scales=wk_scales[:, g, kg, :], in_=wk_grp[g, kg][:])
+
+        def w_turn(g, kg, h):
+            ps = psum.tile([P, 4, P], F32, name="ps_w", tag="w")
+            for j in range(2):
+                words = w_raw[:, g, kg, 2 * h + j, :].bitcast(F32)
+                for e in range(2):
+                    nc.tensor.transpose(ps[:, 2 * j + e, :], words[:, e:256:2], ident[:])
+            return ps
+
+        def w_out(g, kg, h, ps):
+            if (g, kg) not in wn_grp:
+                wn_grp[g, kg] = work.tile([P, 2048], BF16, name="wn_grp", align_bytes=64)
+            dst = wn_grp[g, kg][:].bitcast(F32)[:, 512 * h : 512 * (h + 1)]
+            nc.scalar.copy(
+                out=dst.rearrange("q (j p e) -> q j p e", j=2, e=2), in_=ps[:].rearrange("q (j e) p -> q j p e", e=2)
+            )
+
+        def wn_quant(g, kg):
+            nc.vector.quantize_mx(out=wn_codes[:, g, kg, :].bitcast(E4M3), scales=wn_scales[:, g, kg, :], in_=wn_grp[g, kg][:])
+
+        def mx_student(g, m):
+            ps = psum.tile([P, 512], F32, name="ps_s", tag="s")
+            for kg in range(KG):
+                nc.tensor.matmul_mx(
+                    out=ps[:],
+                    lhsT=x_codes[:, m, kg * P : (kg + 1) * P].bitcast(E4M3),
+                    lhsT_scale=x_scales[:, m, kg * P : (kg + 1) * P],
+                    rhs=wk_codes[:, g, kg, :].bitcast(E4M3),
+                    rhs_scale=wk_scales[:, g, kg, :],
+                    start=(kg == 0),
+                    stop=(kg == KG - 1),
+                )
+            return ps
+
+        def mx_teacher(g, m):
+            ps = psum.tile([P, 512], F32, name="ps_t", tag="t")
+            for kg in range(KG):
+                nc.tensor.matmul_mx(
+                    out=ps[:],
+                    lhsT=x_codes[:, m, kg * P : (kg + 1) * P].bitcast(E4M3),
+                    lhsT_scale=x_scales[:, m, kg * P : (kg + 1) * P],
+                    rhs=t_words[:, kg, 1024 * g : 1024 * (g + 1)].bitcast(E2M1),
+                    rhs_scale=t_scales[:, kg, 512 * g : 512 * (g + 1)],
+                    start=(kg == 0),
+                    stop=(kg == KG - 1),
+                )
+            return ps
+
+        zs = {}
+        zt = {}
+        es = {}
+        dp = {}
+        eps = {}
+        dg = {}
+
+        def out_slice(o, g, m):
+            return o[m * P : (m + 1) * P, 512 * g : 512 * (g + 1)]
+
+        def do_zt(b, ps):
+            g, m = divmod(b, MT)
+            zt[b] = work.tile([P, 512], F32, name="zt", bufs=6)
+            nc.scalar.copy(out=zt[b][:], in_=ps[:])
+            nc.sync.dma_start(out=out_slice(zt_out, g, m), in_=zt[b][:])
+
+        def do_zs(b, ps):
+            g, m = divmod(b, MT)
+            zs[b] = work.tile([P, 512], F32, name="zs", bufs=6)
+            nc.vector.tensor_tensor(out=zs[b][:], in0=ps[:], in1=c_bc[:, 512 * g : 512 * (g + 1)], op=MULT)
+            nc.sync.dma_start(out=out_slice(zs_out, g, m), in_=zs[b][:])
+
+        def do_e(b):
+            es[b] = work.tile([P, 512], F32, name="es", bufs=4)
+            nc.vector.tensor_tensor(out=es[b][:], in0=zs[b][:], in1=zt[b][:], op=SUB)
+
+        def do_d(b, eng):
+            g = b // MT
+            dp[b] = work.tile([P, 512], BF16, name="dp", bufs=4, align_bytes=64)
+            eng.tensor_tensor(
+                out=dp[b][:].rearrange("m (u p e) -> m p u e", u=2, e=2),
+                in0=es[b][:].rearrange("m (p u e) -> m p u e", u=2, e=2),
+                in1=c_bc[:, 512 * g : 512 * (g + 1)].rearrange("m (p u e) -> m p u e", u=2, e=2),
+                op=MULT,
+            )
+
+        def d_turn(i):
+            eps[i] = psum.tile([P, 4, P], F32, name="ps_e", tag="e")
+            for b in (0, 1):
+                words = dp[2 * i + b][:].bitcast(F32)
+                for half in range(2):
+                    nc.tensor.transpose(eps[i][:, 2 * b + half, :], words[:, P * half : P * (half + 1)], ident[:])
+
+        def d_out(i):
+            dg[i] = work.tile([P, 2 * P * 4], BF16, name="dg", align_bytes=64)
+            nc.scalar.copy(
+                out=dg[i][:].bitcast(F32).rearrange("p (b m u) -> p b m u", b=2, u=2),
+                in_=eps[i][:].rearrange("p (b u) m -> p b m u", u=2),
+            )
+
+        def d_quant(i):
+            g, m = divmod(2 * i, MT)
+            nc.vector.quantize_mx(
+                out=d_codes[:, g, m : m + 2, :].rearrange("p m n -> p (m n)").bitcast(E5M2),
+                scales=d_scales[:, g, m : m + 2, :].rearrange("p m n -> p (m n)"),
+                in_=dg[i][:],
+            )
+
+        dx = {}
+
+        def mx_back(m, kg, groups, tag):
+            if (m, kg) not in dx:
+                dx[m, kg] = psum.tile([P, 512], F32, name="ps_dx", tag=tag)
+            for g in groups:
+                nc.tensor.matmul_mx(
+                    out=dx[m, kg][:],
+                    lhsT=d_codes[:, g, m, :].bitcast(E5M2),
+                    lhsT_scale=d_scales[:, g, m, :],
+                    rhs=wn_codes[:, g, kg, :].bitcast(E4M3),
+                    rhs_scale=wn_scales[:, g, kg, :],
+                    start=(g == 0),
+                    stop=(g == NG - 1),
+                )
+
+        def do_du(m, kg):
+            du = work.tile([P, 512], F32, name="du", bufs=8)
+            nc.vector.tensor_tensor(
+                out=du[:].rearrange("m (p j) -> m p j", j=4),
+                in0=dx[m, kg][:].rearrange("m (j p) -> m p j", j=4),
+                in1=gain_bc[:, 512 * kg : 512 * (kg + 1)].rearrange("m (p j) -> m p j", j=4),
+                op=MULT,
+            )
+            nc.sync.dma_start(out=du_out[m * P : (m + 1) * P, 512 * kg : 512 * (kg + 1)], in_=du[:])
+
+        def chunk(k):
+            g, rest = divmod(k, 4)
+            kg, h = divmod(rest, 2)
+            return g, kg, h
+
+        def prep_k(k):
+            g, kg, h = chunk(k)
+            w_inter(g, kg, 256 * h, 256 * h + 256, K_ENG.get(k, 0))
+
+        def prep_n(k):
+            g, kg, h = chunk(k)
+            w_out(g, kg, h, w_turn(g, kg, h))
+
+        make_cg()
+        broadcast_rows(4, gain_bc[:], "w")
+        prep_k(0)
+        x_mul(0)
+        x_turn(0, 0)
+        prep_k(1)
+        prep_k(2)
+        prep_k(3)
+        prep_n(0)
+        x_mul(1)
+        x_quant(0)
+        wk_quant(0, 0)
+        prep_n(1)
+        x_turn(1, 0)
+        wk_quant(0, 1)
+        broadcast_rows(0, c_bc[:, 0:1024], "e")
+        x_quant(1)
+        x_mul(2)
+
+        for i in range(8):
+            pair = (2 * i, 2 * i + 1)
+            for b in pair:
+                g, m = divmod(b, MT)
+                ps_s = mx_student(g, m)
+                ps_t = mx_teacher(g, m)
+                do_zt(b, ps_t)
+                do_zs(b, ps_s)
+                if b == 0:
+                    prep_n(2)
+                    prep_n(3)
+                    x_turn(2, 0)
+                    x_mul(3)
+                    wn_quant(0, 0)
+                if b == 1:
+                    x_turn(3, 0)
+                    x_quant(2)
+                    wn_quant(0, 1)
+                    broadcast_rows(2, c_bc[:, 1024:2048], "e")
+                    x_quant(3)
+            if i >= 1:
+                d_turn(i - 1)
+                d_out(i - 1)
+            do_e(pair[0])
+            do_e(pair[1])
+            for k in K_AT.get(i, []):
+                prep_k(k)
+            for k in N_AT.get(i, []):
+                prep_n(k)
+            for a in QK_AT.get(i, []):
+                wk_quant(*a)
+            do_d(pair[0], nc.vector)
+            do_d(pair[1], nc.vector)
+            if i >= 1:
+                d_quant(i - 1)
+            for a in QN_AT.get(i, []):
+                wn_quant(*a)
+            if i == 6:
+                mx_back(0, 0, (0, 1, 2), "w")
+                mx_back(0, 1, (0, 1, 2), "w")
+
+        d_turn(7)
+        d_out(7)
+        mx_back(0, 0, (3,), "w")
+        mx_back(0, 1, (3,), "w")
+        mx_back(1, 0, (0, 1, 2, 3), "s")
+        mx_back(1, 1, (0, 1, 2, 3), "s")
+        do_du(0, 0)
+        d_quant(7)
+        do_du(0, 1)
+        do_du(1, 0)
+        do_du(1, 1)
+        for kg in range(KG):
+            mx_back(2, kg, (0, 1, 2, 3), "t")
+            do_du(2, kg)
+        for kg in range(KG):
+            mx_back(3, kg, (0, 1, 2, 3), "w")
+            do_du(3, kg)

@@ -17,360 +17,355 @@ MULT = mybir.AluOpType.mult
 SUB = mybir.AluOpType.subtract
 
 P = 128
+G = 512
 MT = M // P
-KG = K // 512
-NG = N // 512
-K_ENG = {0: 1, 1: 1, 2: 1}
-K_AT = {0: [4, 5, 6, 7], 1: [8, 9], 2: [10, 11], 3: [12, 13], 4: [14, 15]}
-QK_AT = {0: [(1, 0)], 1: [(1, 1)], 2: [(2, 0)], 3: [(2, 1)], 4: [(3, 0)], 5: [(3, 1)]}
-N_AT = {0: [4], 1: [5], 2: [6, 7], 3: [8, 9], 4: [10, 11], 5: [12, 13], 6: [14, 15]}
-QN_AT = {2: [(1, 0)], 3: [(1, 1)], 4: [(2, 0)], 5: [(2, 1)], 6: [(3, 0)], 7: [(3, 1)]}
+KG = K // G
+NG = N // G
+PAIRS = NG * MT // 2
+HEAD_SPLIT = 320
+LOOP_SPLIT = 192
+D_SPLIT = 704
 
 
 def tile_teacher_student_logits_s9_kernel(tc, u, gain, w, c, teacher_words, teacher_scales, zs_out, zt_out, du_out):
     nc = tc.nc
     with ExitStack() as ctx:
         keep = ctx.enter_context(tc.tile_pool(name="keep", bufs=1))
-        work = ctx.enter_context(tc.tile_pool(name="work", bufs=3))
-        psum = ctx.enter_context(tc.psum_pool(name="psum", bufs=2))
-        ident = keep.tile([P, P], F32, name="ident", align_bytes=64)
-        ident_b = keep.tile([P, P], BF16, name="ident_b", align_bytes=64)
-        rows = keep.tile([P, 512], BF16, name="rows", align_bytes=64)
-        cg = keep.tile([P, 6, 4], BF16, name="cg", align_bytes=64)
-        gain_bc = keep.tile([P, KG * 512], BF16, name="gain_bc", align_bytes=64)
-        c_bc = keep.tile([P, NG * 512], BF16, name="c_bc", align_bytes=64)
-        x_codes = keep.tile([P, MT, KG * P], U32, name="x_codes", align_bytes=64)
-        x_scales = keep.tile([P, MT, KG * P], U8, name="x_scales", align_bytes=64)
-        t_words = keep.tile([P, KG, 2 * N], U8, name="t_words", align_bytes=64)
-        t_scales = keep.tile([P, KG, N], U8, name="t_scales", align_bytes=64)
-        w_raw = keep.tile([P, NG, KG, 4, 512], BF16, name="w_raw", align_bytes=64)
-        wk_codes = keep.tile([P, NG, KG, 512], U32, name="wk_codes", align_bytes=64)
-        wk_scales = keep.tile([P, NG, KG, 512], U8, name="wk_scales", align_bytes=64)
-        wn_codes = keep.tile([P, NG, KG, 512], U32, name="wn_codes", align_bytes=64)
-        wn_scales = keep.tile([P, NG, KG, 512], U8, name="wn_scales", align_bytes=64)
-        d_codes = keep.tile([P, NG, MT, P], U32, name="d_codes", align_bytes=64)
-        d_scales = keep.tile([P, NG, MT, P], U8, name="d_scales", align_bytes=64)
-        u_sb = keep.tile([P, MT, K], BF16, name="u_sb", align_bytes=64)
+        work = ctx.enter_context(tc.tile_pool(name="work", bufs=2))
+        psum = ctx.enter_context(tc.psum_pool(name="psum", bufs=1))
+        ctx.enter_context(tc.manual_schedule())
 
-        make_identity(nc, ident[:])
-        nc.vector.memset(rows[:], 0.0)
+        def kept(name, shape, dtype):
+            return keep.tile(shape, dtype, name=name, align_bytes=64)
+
+        def operand(name, width):
+            return kept(name + "_codes", [P, width], U32), kept(name + "_scales", [P, width], U8)
+
+        ident = kept("ident", [P, P], F32)
+        gain_t = kept("gain_t", [P, KG, 4], BF16)
+        c_t = kept("c_t", [P, N // P], BF16)
+        gain_all = kept("gain_all", [P, K], BF16)
+        c_all = kept("c_all", [P, N], BF16)
+        c_sorted = kept("c_sorted", [P, N], BF16)
+        t_scales = kept("t_scales", [P, KG, N], U8)
+        t_first = kept("t_first", [P, KG, 2 * G], U8)
+        t_rest = kept("t_rest", [P, KG, 2 * (N - G)], U8)
+        u_sb = [kept("u%d" % m, [P, K], BF16) for m in range(MT)]
+        w_raw = {(g, kg): kept("w%d%d" % (g, kg), [P, 4, G], BF16) for g in range(NG) for kg in range(KG)}
+        x_q = [operand("x%d" % m, KG * P) for m in range(MT)]
+        wk_q = {key: operand("wk%d%d" % key, G) for key in w_raw}
+        wn_q = {key: operand("wn%d%d" % key, G) for key in w_raw}
+        d_q = [operand("d%d" % i, 2 * P) for i in range(PAIRS)]
+
+        def quantize(dst, src, fmt):
+            nc.vector.quantize_mx(out=dst[0][:].bitcast(fmt), scales=dst[1][:], in_=src[:])
+
+        nc.scalar.dma_start(out=gain_t[:], in_=gain.rearrange("(g p t) -> p g t", g=KG, t=4))
+        nc.scalar.dma_start(out=c_t[:], in_=c.rearrange("(p i) -> p i", p=P))
         nc.vector.memset(t_scales[:].rearrange("p g n -> p (g n)").bitcast(I32), 0)
-        nc.scalar.dma_start(out=rows[0:4, :], in_=c.rearrange("(g n) -> g n", g=4))
-        nc.scalar.dma_start(out=rows[4:6, :], in_=gain.rearrange("(g n) -> g n", g=2))
-        nc.vector.tensor_copy(out=ident_b[:], in_=ident[:])
+        make_identity(nc, ident[:])
 
         def load_u(m):
-            nc.sync.dma_start(out=u_sb[:, m, :], in_=u[m * P : (m + 1) * P, :])
+            nc.sync.dma_start(out=u_sb[m][:], in_=u[m * P : (m + 1) * P, :])
 
-        def load_w(g, kg):
-            nc.sync.dma_start(
-                out=w_raw[:, g, kg, :, :],
-                in_=w[512 * kg : 512 * (kg + 1), 512 * g : 512 * (g + 1)].rearrange("(p j) n -> p j n", j=4),
-            )
-
-        def load_teacher(half):
-            cols = slice(half * N, (half + 1) * N)
-            nc.sync.dma_start(
-                out=t_words[:, :, cols].bitcast(I32),
-                in_=teacher_words.rearrange("g p n -> p g n")[:, :, cols].bitcast(I32),
-            )
-
-        def load_teacher_scales():
-            for q in range(4):
+        def load_w(g):
+            for kg in range(KG):
                 nc.sync.dma_start(
-                    out=t_scales[32 * q : 32 * q + 4, :, :].bitcast(I32),
-                    in_=teacher_scales[:, 4 * q : 4 * q + 4, :].rearrange("g r n -> r g n").bitcast(I32),
+                    out=w_raw[g, kg][:],
+                    in_=w[G * kg : G * (kg + 1), G * g : G * (g + 1)].rearrange("(p j) n -> p j n", j=4),
                 )
 
-        load_w(0, 0)
+        def load_teacher(dst, first, last):
+            words = teacher_words.rearrange("g p n -> p g n")[:, :, 2 * first : 2 * last]
+            nc.sync.dma_start(out=dst[:].bitcast(I32), in_=words.bitcast(I32))
+
         load_u(0)
-        load_w(0, 1)
+        load_w(0)
         load_u(1)
-        load_teacher_scales()
-        load_teacher(0)
+        for q in range(4):
+            nc.sync.dma_start(
+                out=t_scales[32 * q : 32 * q + 4, :, :].bitcast(I32),
+                in_=teacher_scales[:, 4 * q : 4 * q + 4, :].rearrange("g r n -> r g n").bitcast(I32),
+            )
+        load_teacher(t_first, 0, G)
         load_u(2)
         load_u(3)
-        load_w(1, 0)
-        load_w(1, 1)
-        load_teacher(1)
-        load_w(2, 0)
-        load_w(2, 1)
-        load_w(3, 0)
-        load_w(3, 1)
+        load_w(1)
+        load_teacher(t_rest, G, N)
+        load_w(2)
+        load_w(3)
 
-        def make_cg():
-            ps = psum.tile([P, 4, P], BF16, name="ps_rows", tag="e")
-            for t in range(4):
-                nc.tensor.transpose(ps[:, t, :], rows[:, t:512:4], ident_b[:])
-            nc.vector.tensor_copy(out=cg[:], in_=ps[:, :, 0:6].rearrange("p t r -> p r t"))
+        def spread(words, tag):
+            ps = psum.tile([P, 4, P], F32, name="ps_spread", tag=tag)
+            for j in range(4):
+                nc.tensor.transpose(ps[:, j, :], words[:, j : j + 1].to_broadcast([P, P]), ident[:])
+            return ps
 
-        def broadcast_rows(first, dst, tag):
-            ps = psum.tile([P, 2, 4, P], BF16, name="ps_bc", tag=tag)
-            for r in range(2):
-                for t in range(4):
-                    nc.tensor.transpose(ps[:, r, t, :], cg[:, first + r, t : t + 1].to_broadcast([P, P]), ident_b[:])
-            nc.scalar.copy(out=dst.rearrange("p (r q t) -> p r q t", r=2, t=4), in_=ps[:].rearrange("p r t q -> p r q t"))
+        def spread_c(h, tag):
+            ps = spread(c_t[:].bitcast(F32)[:, 4 * h : 4 * h + 4], tag)
+            dst = c_all[:].bitcast(F32).rearrange("q (p j) -> q p j", j=8)[:, :, 4 * h : 4 * h + 4]
+            nc.scalar.copy(out=dst, in_=ps[:].rearrange("q j p -> q p j"))
 
-        x_bf = {}
-        x_grp = {}
+        def sort_c():
+            nc.vector.tensor_copy(
+                out=c_sorted[:].bitcast(F32).rearrange("q (g u p) -> q g u p", g=NG, u=2),
+                in_=c_all[:].bitcast(F32).rearrange("q (g p u) -> q g u p", g=NG, u=2),
+            )
 
-        def x_mul(m):
-            x_bf[m] = work.tile([P, K], BF16, name="x_bf", align_bytes=64)
-            nc.vector.tensor_tensor(out=x_bf[m][:], in0=u_sb[:, m, :], in1=gain_bc[:], op=MULT)
+        def spread_gain(tag):
+            ps = spread(gain_t[:].rearrange("p g t -> p (g t)").bitcast(F32), tag)
+            nc.scalar.copy(
+                out=gain_all[:].bitcast(F32).rearrange("q (g p u) -> q g p u", g=KG, u=2),
+                in_=ps[:].rearrange("q (g u) p -> q g p u", u=2),
+            )
 
-        def x_turn(m, eng):
-            ps = psum.tile([P, KG * 2, P], F32, name="ps_x", tag="e")
-            words = x_bf[m][:].bitcast(F32)
+        x_ps, x_grp = {}, {}
+
+        def x_turn(m, tag):
+            x_ps[m] = psum.tile([P, KG * 2, P], F32, name="ps_x", tag=tag)
+            words = u_sb[m][:].bitcast(F32)
             for kg in range(KG):
-                for e in range(2):
-                    nc.tensor.transpose(ps[:, 2 * kg + e, :], words[:, 256 * kg + e : 256 * (kg + 1) : 2], ident[:])
-            x_grp[m] = work.tile([P, KG * P * 4], BF16, name="x_grp", align_bytes=64)
-            for_out = x_grp[m][:].bitcast(F32).rearrange("p (g m e) -> p g m e", g=KG, e=2)
-            for_in = ps[:].rearrange("p (g e) m -> p g m e", e=2)
-            if eng == 0:
-                nc.scalar.copy(out=for_out, in_=for_in)
-            else:
-                nc.vector.tensor_copy(out=for_out, in_=for_in)
+                for half in range(2):
+                    nc.tensor.transpose(x_ps[m][:, 2 * kg + half, :], words[:, 256 * kg + half : 256 * (kg + 1) : 2], ident[:])
+
+        def x_scale(m):
+            x_grp[m] = work.tile([P, K], BF16, name="x_grp", align_bytes=64)
+            for kg in range(KG):
+                turned = x_ps[m][:, 2 * kg : 2 * kg + 2, :].bitcast(BF16)
+                nc.vector.tensor_tensor(
+                    out=x_grp[m][:, G * kg : G * (kg + 1)].rearrange("p (m u e) -> p m u e", u=2, e=2),
+                    in0=turned.rearrange("p u (m e) -> p m u e", e=2),
+                    in1=gain_t[:, kg, :].rearrange("p (u e) -> p u e", e=2).unsqueeze(1).to_broadcast([P, P, 2, 2]),
+                    op=MULT,
+                )
 
         def x_quant(m):
-            nc.vector.quantize_mx(out=x_codes[:, m, :].bitcast(E4M3), scales=x_scales[:, m, :], in_=x_grp[m][:])
+            quantize(x_q[m], x_grp[m], E4M3)
 
         wk_grp = {}
+
+        def wk_views(key, first, last):
+            if key not in wk_grp:
+                wk_grp[key] = work.tile([P, 4 * G], BF16, name="wk_grp", bufs=3, align_bytes=64)
+            dst = wk_grp[key][:, 4 * first : 4 * last].rearrange("p (n i j) -> p n j i", j=4, i=4)
+            src = w_raw[key][:, :, first:last].rearrange("p j (n i) -> p n j i", i=4)
+            return dst, src
+
+        def wk_vector(key, split):
+            dst, src = wk_views(key, 0, split)
+            nc.vector.tensor_copy(out=dst, in_=src)
+
+        def wk_scalar(key, split):
+            dst, src = wk_views(key, split, G)
+            nc.scalar.copy(out=dst, in_=src)
+
+        def wk_quant(key):
+            quantize(wk_q[key], wk_grp[key], E4M3)
+
         wn_grp = {}
 
-        def w_inter(g, kg, a, b, eng):
-            if (g, kg) not in wk_grp:
-                wk_grp[g, kg] = work.tile([P, 2048], BF16, name="wk_grp", align_bytes=64)
-            dst = wk_grp[g, kg][:, 4 * a : 4 * b].rearrange("p (n i j) -> p n j i", j=4, i=4)
-            src = w_raw[:, g, kg, :, a:b].rearrange("p j (n i) -> p n j i", i=4)
-            if eng == 0:
-                nc.scalar.copy(out=dst, in_=src)
-            elif eng == 2:
-                nc.gpsimd.tensor_scalar(out=dst, in0=src, scalar1=1.0, scalar2=0.0, op0=MULT, op1=mybir.AluOpType.add)
-            else:
-                nc.vector.tensor_copy(out=dst, in_=src)
+        def wn_turn(key):
+            wn_grp[key] = work.tile([P, 4 * G], BF16, name="wn_grp", bufs=3, align_bytes=64)
+            for h in range(2):
+                ps = psum.tile([P, 4, P], F32, name="ps_w", tag="w%d" % h)
+                for j in range(2):
+                    words = w_raw[key][:, 2 * h + j, :].bitcast(F32)
+                    for half in range(2):
+                        nc.tensor.transpose(ps[:, 2 * j + half, :], words[:, half:256:2], ident[:])
+                dst = wn_grp[key][:].bitcast(F32)[:, G * h : G * (h + 1)]
+                nc.scalar.copy(
+                    out=dst.rearrange("q (j p u) -> q j p u", j=2, u=2), in_=ps[:].rearrange("q (j u) p -> q j p u", u=2)
+                )
 
-        def wk_quant(g, kg):
-            nc.vector.quantize_mx(out=wk_codes[:, g, kg, :].bitcast(E4M3), scales=wk_scales[:, g, kg, :], in_=wk_grp[g, kg][:])
+        def wn_quant(key):
+            quantize(wn_q[key], wn_grp[key], E4M3)
 
-        def w_turn(g, kg, h):
-            ps = psum.tile([P, 4, P], F32, name="ps_w", tag="w")
-            for j in range(2):
-                words = w_raw[:, g, kg, 2 * h + j, :].bitcast(F32)
-                for e in range(2):
-                    nc.tensor.transpose(ps[:, 2 * j + e, :], words[:, e:256:2], ident[:])
-            return ps
+        ps_s, ps_t, zs, diff, d_bf, d_grp = {}, {}, {}, {}, {}, {}
 
-        def w_out(g, kg, h, ps):
-            if (g, kg) not in wn_grp:
-                wn_grp[g, kg] = work.tile([P, 2048], BF16, name="wn_grp", align_bytes=64)
-            dst = wn_grp[g, kg][:].bitcast(F32)[:, 512 * h : 512 * (h + 1)]
-            nc.scalar.copy(
-                out=dst.rearrange("q (j p e) -> q j p e", j=2, e=2), in_=ps[:].rearrange("q (j e) p -> q j p e", e=2)
-            )
-
-        def wn_quant(g, kg):
-            nc.vector.quantize_mx(out=wn_codes[:, g, kg, :].bitcast(E4M3), scales=wn_scales[:, g, kg, :], in_=wn_grp[g, kg][:])
-
-        def mx_student(g, m):
-            ps = psum.tile([P, 512], F32, name="ps_s", tag="s")
+        def logits(ps, m, codes, scales):
             for kg in range(KG):
                 nc.tensor.matmul_mx(
                     out=ps[:],
-                    lhsT=x_codes[:, m, kg * P : (kg + 1) * P].bitcast(E4M3),
-                    lhsT_scale=x_scales[:, m, kg * P : (kg + 1) * P],
-                    rhs=wk_codes[:, g, kg, :].bitcast(E4M3),
-                    rhs_scale=wk_scales[:, g, kg, :],
+                    lhsT=x_q[m][0][:, kg * P : (kg + 1) * P].bitcast(E4M3),
+                    lhsT_scale=x_q[m][1][:, kg * P : (kg + 1) * P],
+                    rhs=codes(kg),
+                    rhs_scale=scales(kg),
                     start=(kg == 0),
                     stop=(kg == KG - 1),
                 )
-            return ps
 
-        def mx_teacher(g, m):
-            ps = psum.tile([P, 512], F32, name="ps_t", tag="t")
-            for kg in range(KG):
-                nc.tensor.matmul_mx(
-                    out=ps[:],
-                    lhsT=x_codes[:, m, kg * P : (kg + 1) * P].bitcast(E4M3),
-                    lhsT_scale=x_scales[:, m, kg * P : (kg + 1) * P],
-                    rhs=t_words[:, kg, 1024 * g : 1024 * (g + 1)].bitcast(E2M1),
-                    rhs_scale=t_scales[:, kg, 512 * g : 512 * (g + 1)],
-                    start=(kg == 0),
-                    stop=(kg == KG - 1),
-                )
-            return ps
-
-        zs = {}
-        zt = {}
-        es = {}
-        dp = {}
-        eps = {}
-        dg = {}
-
-        def out_slice(o, g, m):
-            return o[m * P : (m + 1) * P, 512 * g : 512 * (g + 1)]
-
-        def do_zt(b, ps):
+        def mx_student(b):
             g, m = divmod(b, MT)
-            zt[b] = work.tile([P, 512], F32, name="zt", bufs=6)
-            nc.scalar.copy(out=zt[b][:], in_=ps[:])
-            nc.sync.dma_start(out=out_slice(zt_out, g, m), in_=zt[b][:])
+            ps_s[b] = psum.tile([P, G], F32, name="ps_s", tag="s%d" % (b % 2))
+            logits(ps_s[b], m, lambda kg: wk_q[g, kg][0][:].bitcast(E4M3), lambda kg: wk_q[g, kg][1][:])
 
-        def do_zs(b, ps):
+        def mx_teacher(b):
             g, m = divmod(b, MT)
-            zs[b] = work.tile([P, 512], F32, name="zs", bufs=6)
-            nc.vector.tensor_tensor(out=zs[b][:], in0=ps[:], in1=c_bc[:, 512 * g : 512 * (g + 1)], op=MULT)
-            nc.sync.dma_start(out=out_slice(zs_out, g, m), in_=zs[b][:])
+            ps_t[b] = psum.tile([P, G], F32, name="ps_t", tag="t%d" % (b % 2))
+            words, g0 = (t_first, 0) if g == 0 else (t_rest, 1)
+            cols = slice(2 * G * (g - g0), 2 * G * (g - g0 + 1))
+            logits(ps_t[b], m, lambda kg: words[:, kg, cols].bitcast(E2M1), lambda kg: t_scales[:, kg, G * g : G * (g + 1)])
 
-        def do_e(b):
-            es[b] = work.tile([P, 512], F32, name="es", bufs=4)
-            nc.vector.tensor_tensor(out=es[b][:], in0=zs[b][:], in1=zt[b][:], op=SUB)
+        def out_block(out, b):
+            g, m = divmod(b, MT)
+            return out[m * P : (m + 1) * P, G * g : G * (g + 1)]
 
-        def do_d(b, eng):
+        def zs_out_of_psum(b):
             g = b // MT
-            dp[b] = work.tile([P, 512], BF16, name="dp", bufs=4, align_bytes=64)
-            eng.tensor_tensor(
-                out=dp[b][:].rearrange("m (u p e) -> m p u e", u=2, e=2),
-                in0=es[b][:].rearrange("m (p u e) -> m p u e", u=2, e=2),
-                in1=c_bc[:, 512 * g : 512 * (g + 1)].rearrange("m (p u e) -> m p u e", u=2, e=2),
-                op=MULT,
-            )
+            zs[b] = work.tile([P, G], F32, name="zs", bufs=8)
+            nc.vector.tensor_tensor(out=zs[b][:], in0=ps_s[b][:], in1=c_all[:, G * g : G * (g + 1)], op=MULT)
+            nc.sync.dma_start(out=out_block(zs_out, b), in_=zs[b][:])
+
+        def zt_out_of_psum(b):
+            zt = work.tile([P, G], F32, name="zt", bufs=8)
+            nc.scalar.copy(out=zt[:], in_=ps_t[b][:])
+            nc.sync.dma_start(out=out_block(zt_out, b), in_=zt[:])
+
+        def subtract(i):
+            diff[i] = work.tile([P, 2 * G], F32, name="diff", align_bytes=64)
+            for h in range(2):
+                nc.vector.tensor_tensor(
+                    out=diff[i][:, G * h : G * (h + 1)].rearrange("m (u p e) -> m u p e", u=2, e=2),
+                    in0=zs[2 * i + h][:].rearrange("m (p u e) -> m u p e", u=2, e=2),
+                    in1=ps_t[2 * i + h][:].rearrange("m (p u e) -> m u p e", u=2, e=2),
+                    op=SUB,
+                )
+
+        def d_scale(eng, i, first, last):
+            if i not in d_bf:
+                d_bf[i] = work.tile([P, 2 * G], BF16, name="d_bf", align_bytes=64)
+            g = i // 2
+            for h in range(2):
+                a, b = max(first, G * h), min(last, G * (h + 1))
+                if a < b:
+                    eng.tensor_tensor(
+                        out=d_bf[i][:, a:b], in0=diff[i][:, a:b], in1=c_sorted[:, G * (g - h) + a : G * (g - h) + b], op=MULT
+                    )
 
         def d_turn(i):
-            eps[i] = psum.tile([P, 4, P], F32, name="ps_e", tag="e")
-            for b in (0, 1):
-                words = dp[2 * i + b][:].bitcast(F32)
-                for half in range(2):
-                    nc.tensor.transpose(eps[i][:, 2 * b + half, :], words[:, P * half : P * (half + 1)], ident[:])
-
-        def d_out(i):
-            dg[i] = work.tile([P, 2 * P * 4], BF16, name="dg", align_bytes=64)
+            ps = psum.tile([P, 4, P], F32, name="ps_d", tag="d")
+            words = d_bf[i][:].bitcast(F32)
+            for j in range(4):
+                nc.tensor.transpose(ps[:, j, :], words[:, P * j : P * (j + 1)], ident[:])
+            d_grp[i] = work.tile([P, 2 * G], BF16, name="d_grp", align_bytes=64)
             nc.scalar.copy(
-                out=dg[i][:].bitcast(F32).rearrange("p (b m u) -> p b m u", b=2, u=2),
-                in_=eps[i][:].rearrange("p (b u) m -> p b m u", u=2),
+                out=d_grp[i][:].bitcast(F32).rearrange("p (h m u) -> p h m u", h=2, u=2),
+                in_=ps[:].rearrange("p (h u) m -> p h m u", u=2),
             )
 
         def d_quant(i):
-            g, m = divmod(2 * i, MT)
-            nc.vector.quantize_mx(
-                out=d_codes[:, g, m : m + 2, :].rearrange("p m n -> p (m n)").bitcast(E5M2),
-                scales=d_scales[:, g, m : m + 2, :].rearrange("p m n -> p (m n)"),
-                in_=dg[i][:],
-            )
+            quantize(d_q[i], d_grp[i], E5M2)
 
         dx = {}
 
         def mx_back(m, kg, groups, tag):
             if (m, kg) not in dx:
-                dx[m, kg] = psum.tile([P, 512], F32, name="ps_dx", tag=tag)
+                dx[m, kg] = psum.tile([P, G], F32, name="ps_dx", tag=tag)
             for g in groups:
+                codes, scales = d_q[2 * g + m // 2]
+                cols = slice(P * (m % 2), P * (m % 2 + 1))
                 nc.tensor.matmul_mx(
                     out=dx[m, kg][:],
-                    lhsT=d_codes[:, g, m, :].bitcast(E5M2),
-                    lhsT_scale=d_scales[:, g, m, :],
-                    rhs=wn_codes[:, g, kg, :].bitcast(E4M3),
-                    rhs_scale=wn_scales[:, g, kg, :],
+                    lhsT=codes[:, cols].bitcast(E5M2),
+                    lhsT_scale=scales[:, cols],
+                    rhs=wn_q[g, kg][0][:].bitcast(E4M3),
+                    rhs_scale=wn_q[g, kg][1][:],
                     start=(g == 0),
                     stop=(g == NG - 1),
                 )
 
-        def do_du(m, kg):
-            du = work.tile([P, 512], F32, name="du", bufs=8)
+        def du_out_of_psum(m, kg):
+            du = work.tile([P, G], F32, name="du", bufs=8)
             nc.vector.tensor_tensor(
                 out=du[:].rearrange("m (p j) -> m p j", j=4),
                 in0=dx[m, kg][:].rearrange("m (j p) -> m p j", j=4),
-                in1=gain_bc[:, 512 * kg : 512 * (kg + 1)].rearrange("m (p j) -> m p j", j=4),
+                in1=gain_all[:, G * kg : G * (kg + 1)].rearrange("m (p j) -> m p j", j=4),
                 op=MULT,
             )
-            nc.sync.dma_start(out=du_out[m * P : (m + 1) * P, 512 * kg : 512 * (kg + 1)], in_=du[:])
+            nc.sync.dma_start(out=du_out[m * P : (m + 1) * P, G * kg : G * (kg + 1)], in_=du[:])
 
-        def chunk(k):
-            g, rest = divmod(k, 4)
-            kg, h = divmod(rest, 2)
-            return g, kg, h
-
-        def prep_k(k):
-            g, kg, h = chunk(k)
-            w_inter(g, kg, 256 * h, 256 * h + 256, K_ENG.get(k, 0))
-
-        def prep_n(k):
-            g, kg, h = chunk(k)
-            w_out(g, kg, h, w_turn(g, kg, h))
-
-        make_cg()
-        broadcast_rows(4, gain_bc[:], "w")
-        prep_k(0)
-        x_mul(0)
-        x_turn(0, 0)
-        prep_k(1)
-        prep_k(2)
-        prep_k(3)
-        prep_n(0)
-        x_mul(1)
+        x_turn(0, "x")
+        x_scale(0)
+        wk_vector((0, 0), HEAD_SPLIT)
+        wk_scalar((0, 0), HEAD_SPLIT)
+        spread_c(0, "w0")
         x_quant(0)
-        wk_quant(0, 0)
-        prep_n(1)
-        x_turn(1, 0)
-        wk_quant(0, 1)
-        broadcast_rows(0, c_bc[:, 0:1024], "e")
+        wk_vector((0, 1), HEAD_SPLIT)
+        wk_scalar((0, 1), HEAD_SPLIT)
+        spread_c(1, "w1")
+        wk_quant((0, 0))
+        x_turn(1, "d")
+        x_scale(1)
+        wk_quant((0, 1))
         x_quant(1)
-        x_mul(2)
 
-        for i in range(8):
-            pair = (2 * i, 2 * i + 1)
-            for b in pair:
-                g, m = divmod(b, MT)
-                ps_s = mx_student(g, m)
-                ps_t = mx_teacher(g, m)
-                do_zt(b, ps_t)
-                do_zs(b, ps_s)
-                if b == 0:
-                    prep_n(2)
-                    prep_n(3)
-                    x_turn(2, 0)
-                    x_mul(3)
-                    wn_quant(0, 0)
-                if b == 1:
-                    x_turn(3, 0)
-                    x_quant(2)
-                    wn_quant(0, 1)
-                    broadcast_rows(2, c_bc[:, 1024:2048], "e")
-                    x_quant(3)
+        def wk_key(i):
+            return (i // 2 + 1, i % 2)
+
+        last = PAIRS - 1
+        for i in range(PAIRS):
+            a, b = 2 * i, 2 * i + 1
+            prepares = i < PAIRS - 2
+            mx_student(a)
+            mx_student(b)
+            if i >= 1:
+                if prepares:
+                    wk_scalar(wk_key(i), LOOP_SPLIT)
+                subtract(i - 1)
+                d_scale(nc.gpsimd, i - 1, 0, D_SPLIT)
+            mx_teacher(a)
+            mx_teacher(b)
+            zs_out_of_psum(a)
+            zt_out_of_psum(a)
+            zs_out_of_psum(b)
+            zt_out_of_psum(b)
+            if i == 0:
+                x_turn(2, "x")
+                x_turn(3, "d")
+                sort_c()
+                x_scale(2)
+                x_scale(3)
+                wk_scalar(wk_key(0), 0)
+                x_quant(2)
+                x_quant(3)
+            else:
+                d_scale(nc.vector, i - 1, D_SPLIT, 2 * G)
+            if i < last:
+                wn_turn(divmod(i, 2))
+            if i == last - 1:
+                wn_turn(divmod(last, 2))
+            if i == 2:
+                spread_gain("x")
             if i >= 1:
                 d_turn(i - 1)
-                d_out(i - 1)
-            do_e(pair[0])
-            do_e(pair[1])
-            for k in K_AT.get(i, []):
-                prep_k(k)
-            for k in N_AT.get(i, []):
-                prep_n(k)
-            for a in QK_AT.get(i, []):
-                wk_quant(*a)
-            do_d(pair[0], nc.vector)
-            do_d(pair[1], nc.vector)
+            if prepares:
+                wk_quant(wk_key(i))
             if i >= 1:
-                d_quant(i - 1)
-            for a in QN_AT.get(i, []):
-                wn_quant(*a)
-            if i == 6:
-                mx_back(0, 0, (0, 1, 2), "w")
-                mx_back(0, 1, (0, 1, 2), "w")
+                wn_quant(divmod(i - 1, 2))
+            if i == last:
+                wn_quant(divmod(last, 2))
+            if i >= 2:
+                d_quant(i - 2)
+            if i + 1 < PAIRS - 2:
+                wk_vector(wk_key(i + 1), LOOP_SPLIT)
 
-        d_turn(7)
-        d_out(7)
-        mx_back(0, 0, (3,), "w")
-        mx_back(0, 1, (3,), "w")
-        mx_back(1, 0, (0, 1, 2, 3), "s")
-        mx_back(1, 1, (0, 1, 2, 3), "s")
-        do_du(0, 0)
-        d_quant(7)
-        do_du(0, 1)
-        do_du(1, 0)
-        do_du(1, 1)
+        subtract(last)
         for kg in range(KG):
-            mx_back(2, kg, (0, 1, 2, 3), "t")
-            do_du(2, kg)
+            mx_back(0, kg, range(NG - 1), "w%d" % kg)
+        d_quant(last - 1)
+        d_scale(nc.gpsimd, last, 0, G // 2)
+        d_scale(nc.vector, last, G // 2, 2 * G)
         for kg in range(KG):
-            mx_back(3, kg, (0, 1, 2, 3), "w")
-            do_du(3, kg)
+            mx_back(0, kg, [NG - 1], "w%d" % kg)
+        mx_back(1, 0, range(NG), "s0")
+        d_turn(last)
+        mx_back(1, 1, range(NG), "s1")
+        du_out_of_psum(0, 0)
+        d_quant(last)
+        du_out_of_psum(0, 1)
+        du_out_of_psum(1, 0)
+        du_out_of_psum(1, 1)
+        for m, bank in ((2, "t"), (3, "w")):
+            for kg in range(KG):
+                mx_back(m, kg, range(NG), bank + str(kg))
+                du_out_of_psum(m, kg)

@@ -22,9 +22,9 @@ MT = M // P
 KG = K // G
 NG = N // G
 PAIRS = NG * MT // 2
-HEAD_SPLIT = 320
-LOOP_SPLIT = 192
-D_SPLIT = 704
+HEAD_SPLIT = 256
+LOOP_SPLIT = 128
+D_SPLIT = 512
 
 
 def tile_teacher_student_logits_s9_kernel(tc, u, gain, w, c, teacher_words, teacher_scales, zs_out, zt_out, du_out):
@@ -68,8 +68,8 @@ def tile_teacher_student_logits_s9_kernel(tc, u, gain, w, c, teacher_words, teac
         def load_u(m):
             nc.sync.dma_start(out=u_sb[m][:], in_=u[m * P : (m + 1) * P, :])
 
-        def load_w(g):
-            for kg in range(KG):
+        def load_w(g, groups=range(KG)):
+            for kg in groups:
                 nc.sync.dma_start(
                     out=w_raw[g, kg][:],
                     in_=w[G * kg : G * (kg + 1), G * g : G * (g + 1)].rearrange("(p j) n -> p j n", j=4),
@@ -80,8 +80,9 @@ def tile_teacher_student_logits_s9_kernel(tc, u, gain, w, c, teacher_words, teac
             nc.sync.dma_start(out=dst[:].bitcast(I32), in_=words.bitcast(I32))
 
         load_u(0)
-        load_w(0)
+        load_w(0, [0])
         load_u(1)
+        load_w(0, [1])
         for q in range(4):
             nc.sync.dma_start(
                 out=t_scales[32 * q : 32 * q + 4, :, :].bitcast(I32),
@@ -101,8 +102,10 @@ def tile_teacher_student_logits_s9_kernel(tc, u, gain, w, c, teacher_words, teac
                 nc.tensor.transpose(ps[:, j, :], words[:, j : j + 1].to_broadcast([P, P]), ident[:])
             return ps
 
-        def spread_c(h, tag):
-            ps = spread(c_t[:].bitcast(F32)[:, 4 * h : 4 * h + 4], tag)
+        def c_turn(h, tag):
+            return spread(c_t[:].bitcast(F32)[:, 4 * h : 4 * h + 4], tag)
+
+        def c_copy(h, ps):
             dst = c_all[:].bitcast(F32).rearrange("q (p j) -> q p j", j=8)[:, :, 4 * h : 4 * h + 4]
             nc.scalar.copy(out=dst, in_=ps[:].rearrange("q j p -> q p j"))
 
@@ -164,26 +167,31 @@ def tile_teacher_student_logits_s9_kernel(tc, u, gain, w, c, teacher_words, teac
 
         wn_grp = {}
 
-        def wn_turn(key):
-            wn_grp[key] = work.tile([P, 4 * G], BF16, name="wn_grp", bufs=3, align_bytes=64)
-            for h in range(2):
-                ps = psum.tile([P, 4, P], F32, name="ps_w", tag="w%d" % h)
-                for j in range(2):
-                    words = w_raw[key][:, 2 * h + j, :].bitcast(F32)
-                    for half in range(2):
-                        nc.tensor.transpose(ps[:, 2 * j + half, :], words[:, half:256:2], ident[:])
-                dst = wn_grp[key][:].bitcast(F32)[:, G * h : G * (h + 1)]
-                nc.scalar.copy(
-                    out=dst.rearrange("q (j p u) -> q j p u", j=2, u=2), in_=ps[:].rearrange("q (j u) p -> q j p u", u=2)
-                )
+        wn_ps = {}
+
+        def wn_turn(key, h, bank="w"):
+            wn_ps[key, h] = psum.tile([P, 4, P], F32, name="ps_w", tag=bank + str(h))
+            for j in range(2):
+                words = w_raw[key][:, 2 * h + j, :].bitcast(F32)
+                for half in range(2):
+                    nc.tensor.transpose(wn_ps[key, h][:, 2 * j + half, :], words[:, half:256:2], ident[:])
+
+        def wn_copy(key, h):
+            if h == 0:
+                wn_grp[key] = work.tile([P, 4 * G], BF16, name="wn_grp", bufs=3, align_bytes=64)
+            dst = wn_grp[key][:].bitcast(F32)[:, G * h : G * (h + 1)]
+            nc.scalar.copy(
+                out=dst.rearrange("q (j p u) -> q j p u", j=2, u=2),
+                in_=wn_ps[key, h][:].rearrange("q (j u) p -> q j p u", u=2),
+            )
 
         def wn_quant(key):
             quantize(wn_q[key], wn_grp[key], E4M3)
 
         ps_s, ps_t, zs, diff, d_bf, d_grp = {}, {}, {}, {}, {}, {}
 
-        def logits(ps, m, codes, scales):
-            for kg in range(KG):
+        def logits(ps, m, codes, scales, groups):
+            for kg in groups:
                 nc.tensor.matmul_mx(
                     out=ps[:],
                     lhsT=x_q[m][0][:, kg * P : (kg + 1) * P].bitcast(E4M3),
@@ -194,17 +202,18 @@ def tile_teacher_student_logits_s9_kernel(tc, u, gain, w, c, teacher_words, teac
                     stop=(kg == KG - 1),
                 )
 
-        def mx_student(b):
+        def mx_student(b, groups=range(KG)):
             g, m = divmod(b, MT)
-            ps_s[b] = psum.tile([P, G], F32, name="ps_s", tag="s%d" % (b % 2))
-            logits(ps_s[b], m, lambda kg: wk_q[g, kg][0][:].bitcast(E4M3), lambda kg: wk_q[g, kg][1][:])
+            if b not in ps_s:
+                ps_s[b] = psum.tile([P, G], F32, name="ps_s", tag="s%d" % (b % 2))
+            logits(ps_s[b], m, lambda kg: wk_q[g, kg][0][:].bitcast(E4M3), lambda kg: wk_q[g, kg][1][:], groups)
 
         def mx_teacher(b):
             g, m = divmod(b, MT)
             ps_t[b] = psum.tile([P, G], F32, name="ps_t", tag="t%d" % (b % 2))
             words, g0 = (t_first, 0) if g == 0 else (t_rest, 1)
             cols = slice(2 * G * (g - g0), 2 * G * (g - g0 + 1))
-            logits(ps_t[b], m, lambda kg: words[:, kg, cols].bitcast(E2M1), lambda kg: t_scales[:, kg, G * g : G * (g + 1)])
+            logits(ps_t[b], m, lambda kg: words[:, kg, cols].bitcast(E2M1), lambda kg: t_scales[:, kg, G * g : G * (g + 1)], range(KG))
 
         def out_block(out, b):
             g, m = divmod(b, MT)
@@ -284,88 +293,118 @@ def tile_teacher_student_logits_s9_kernel(tc, u, gain, w, c, teacher_words, teac
             )
             nc.sync.dma_start(out=du_out[m * P : (m + 1) * P, G * kg : G * (kg + 1)], in_=du[:])
 
+        def unit(i):
+            return (i // 2 + 1, i % 2)
+
         x_turn(0, "x")
+        c_ps = [c_turn(h, "t%d" % h) for h in range(2)]
+        x_turn(1, "d")
         x_scale(0)
         wk_vector((0, 0), HEAD_SPLIT)
         wk_scalar((0, 0), HEAD_SPLIT)
-        spread_c(0, "w0")
+        c_copy(0, c_ps[0])
         x_quant(0)
+        wk_quant((0, 0))
+        x_scale(1)
         wk_vector((0, 1), HEAD_SPLIT)
         wk_scalar((0, 1), HEAD_SPLIT)
-        spread_c(1, "w1")
-        wk_quant((0, 0))
-        x_turn(1, "d")
-        x_scale(1)
-        wk_quant((0, 1))
+        c_copy(1, c_ps[1])
         x_quant(1)
-
-        def wk_key(i):
-            return (i // 2 + 1, i % 2)
+        wk_quant((0, 1))
+        sort_c()
+        for h in range(2):
+            wn_turn((0, 0), h)
+            wn_copy((0, 0), h)
+        wn_turn((0, 1), 0, "t")
+        wn_copy((0, 1), 0)
+        mx_student(0)
+        mx_student(1)
+        wn_turn((0, 1), 1, "t")
+        wn_copy((0, 1), 1)
+        x_turn(2, "x")
+        x_turn(3, "d")
+        wn_quant((0, 0))
+        zs_out_of_psum(0)
+        zs_out_of_psum(1)
+        x_scale(2)
+        x_scale(3)
+        mx_teacher(0)
+        mx_teacher(1)
+        wk_vector(unit(0), HEAD_SPLIT)
+        wk_scalar(unit(0), HEAD_SPLIT)
+        zt_out_of_psum(0)
+        zt_out_of_psum(1)
+        x_quant(2)
+        x_quant(3)
+        wn_quant((0, 1))
+        for h in range(2):
+            wn_turn(unit(0), h)
+            wn_copy(unit(0), h)
+        wk_quant(unit(0))
+        wk_vector(unit(1), LOOP_SPLIT)
 
         last = PAIRS - 1
-        for i in range(PAIRS):
+        for i in range(1, PAIRS):
             a, b = 2 * i, 2 * i + 1
             prepares = i < PAIRS - 2
             mx_student(a)
             mx_student(b)
-            if i >= 1:
-                if prepares:
-                    wk_scalar(wk_key(i), LOOP_SPLIT)
-                subtract(i - 1)
-                d_scale(nc.gpsimd, i - 1, 0, D_SPLIT)
+            if prepares:
+                wk_scalar(unit(i), LOOP_SPLIT)
+                wn_turn(unit(i), 0)
+                wn_copy(unit(i), 0)
+            if i == last - 1:
+                mx_back(0, 0, (0, 1), "w0")
+                mx_back(1, 0, (0, 1), "x")
+            if i == last:
+                mx_back(0, 1, (0, 1), "w1")
+            subtract(i - 1)
+            d_scale(nc.gpsimd, i - 1, 0, D_SPLIT)
             mx_teacher(a)
             mx_teacher(b)
             zs_out_of_psum(a)
             zt_out_of_psum(a)
             zs_out_of_psum(b)
             zt_out_of_psum(b)
-            if i == 0:
-                x_turn(2, "x")
-                x_turn(3, "d")
-                sort_c()
-                x_scale(2)
-                x_scale(3)
-                wk_scalar(wk_key(0), 0)
-                x_quant(2)
-                x_quant(3)
-            else:
-                d_scale(nc.vector, i - 1, D_SPLIT, 2 * G)
-            if i < last:
-                wn_turn(divmod(i, 2))
-            if i == last - 1:
-                wn_turn(divmod(last, 2))
-            if i == 2:
-                spread_gain("x")
-            if i >= 1:
-                d_turn(i - 1)
+            d_scale(nc.vector, i - 1, D_SPLIT, 2 * G)
             if prepares:
-                wk_quant(wk_key(i))
-            if i >= 1:
-                wn_quant(divmod(i - 1, 2))
-            if i == last:
-                wn_quant(divmod(last, 2))
+                wn_turn(unit(i), 1)
+                wn_copy(unit(i), 1)
+            if i == 1:
+                spread_gain("x")
+            d_turn(i - 1)
+            if prepares:
+                wk_quant(unit(i))
+            if i <= PAIRS - 2:
+                wn_quant(unit(i - 1))
             if i >= 2:
                 d_quant(i - 2)
             if i + 1 < PAIRS - 2:
-                wk_vector(wk_key(i + 1), LOOP_SPLIT)
+                wk_vector(unit(i + 1), LOOP_SPLIT)
 
+        banks = {(0, 0): "w0", (0, 1): "w1", (1, 0): "x", (1, 1): "s0", (2, 0): "s1", (2, 1): "t0", (3, 0): "t1", (3, 1): "w0"}
+        early, late = [(0, 0), (0, 1), (1, 0), (1, 1)], [(2, 0), (2, 1), (3, 0), (3, 1)]
+        for key in early[:3]:
+            mx_back(*key, (2,), banks[key])
         subtract(last)
-        for kg in range(KG):
-            mx_back(0, kg, range(NG - 1), "w%d" % kg)
         d_quant(last - 1)
-        d_scale(nc.gpsimd, last, 0, G // 2)
-        d_scale(nc.vector, last, G // 2, 2 * G)
-        for kg in range(KG):
-            mx_back(0, kg, [NG - 1], "w%d" % kg)
-        mx_back(1, 0, range(NG), "s0")
+        d_scale(nc.vector, last, 0, 2 * G)
+        mx_back(1, 1, (0, 1, 2), banks[1, 1])
+        mx_back(2, 0, (0, 1, 2), banks[2, 0])
+        for key in early[:2]:
+            mx_back(*key, (3,), banks[key])
         d_turn(last)
-        mx_back(1, 1, range(NG), "s1")
+        for key in early[2:]:
+            mx_back(*key, (3,), banks[key])
         du_out_of_psum(0, 0)
-        d_quant(last)
         du_out_of_psum(0, 1)
+        mx_back(2, 1, (0, 1, 2), banks[2, 1])
+        mx_back(3, 0, (0, 1, 2), banks[3, 0])
         du_out_of_psum(1, 0)
+        d_quant(last)
         du_out_of_psum(1, 1)
-        for m, bank in ((2, "t"), (3, "w")):
-            for kg in range(KG):
-                mx_back(m, kg, range(NG), bank + str(kg))
-                du_out_of_psum(m, kg)
+        for key in late[:3]:
+            mx_back(*key, (3,), banks[key])
+            du_out_of_psum(*key)
+        mx_back(3, 1, range(NG), banks[3, 1])
+        du_out_of_psum(3, 1)

@@ -23,7 +23,7 @@ KG = K // G
 NG = N // G
 PAIRS = NG * MT // 2
 HEAD_SPLIT = 256
-LOOP_SPLIT = 128
+LOOP_SPLIT = 144
 D_SPLIT = 512
 
 
@@ -110,13 +110,12 @@ def tile_teacher_student_logits_s9_kernel(tc, u, gain, w, c, teacher_words, teac
             nc.scalar.copy(out=dst, in_=ps[:].rearrange("q j p -> q p j"))
 
         def sort_c():
-            nc.vector.tensor_copy(
+            nc.scalar.copy(
                 out=c_sorted[:].bitcast(F32).rearrange("q (g u p) -> q g u p", g=NG, u=2),
                 in_=c_all[:].bitcast(F32).rearrange("q (g p u) -> q g u p", g=NG, u=2),
             )
 
-        def spread_gain(tag):
-            ps = spread(gain_t[:].rearrange("p g t -> p (g t)").bitcast(F32), tag)
+        def gain_copy(ps):
             nc.scalar.copy(
                 out=gain_all[:].bitcast(F32).rearrange("q (g p u) -> q g p u", g=KG, u=2),
                 in_=ps[:].rearrange("q (g u) p -> q g p u", u=2),
@@ -169,8 +168,8 @@ def tile_teacher_student_logits_s9_kernel(tc, u, gain, w, c, teacher_words, teac
 
         wn_ps = {}
 
-        def wn_turn(key, h, bank="w"):
-            wn_ps[key, h] = psum.tile([P, 4, P], F32, name="ps_w", tag=bank + str(h))
+        def wn_turn(key, h, bank):
+            wn_ps[key, h] = psum.tile([P, 4, P], F32, name="ps_w", tag=bank)
             for j in range(2):
                 words = w_raw[key][:, 2 * h + j, :].bitcast(F32)
                 for half in range(2):
@@ -298,11 +297,13 @@ def tile_teacher_student_logits_s9_kernel(tc, u, gain, w, c, teacher_words, teac
 
         x_turn(0, "x")
         c_ps = [c_turn(h, "t%d" % h) for h in range(2)]
+        gain_ps = spread(gain_t[:].rearrange("p g t -> p (g t)").bitcast(F32), "s1")
         x_turn(1, "d")
         x_scale(0)
         wk_vector((0, 0), HEAD_SPLIT)
         wk_scalar((0, 0), HEAD_SPLIT)
         c_copy(0, c_ps[0])
+        gain_copy(gain_ps)
         x_quant(0)
         wk_quant((0, 0))
         x_scale(1)
@@ -311,53 +312,52 @@ def tile_teacher_student_logits_s9_kernel(tc, u, gain, w, c, teacher_words, teac
         c_copy(1, c_ps[1])
         x_quant(1)
         wk_quant((0, 1))
-        sort_c()
         for h in range(2):
-            wn_turn((0, 0), h)
+            wn_turn((0, 0), h, "w%d" % h)
             wn_copy((0, 0), h)
-        wn_turn((0, 1), 0, "t")
+        wn_turn((0, 1), 0, "t0")
         wn_copy((0, 1), 0)
+        sort_c()
         mx_student(0)
-        mx_student(1)
-        wn_turn((0, 1), 1, "t")
-        wn_copy((0, 1), 1)
         x_turn(2, "x")
+        mx_student(1)
         x_turn(3, "d")
+        wn_turn((0, 1), 1, "t1")
         wn_quant((0, 0))
+        wk_scalar(unit(0), HEAD_SPLIT)
+        wn_copy((0, 1), 1)
         zs_out_of_psum(0)
-        zs_out_of_psum(1)
         x_scale(2)
+        zs_out_of_psum(1)
         x_scale(3)
         mx_teacher(0)
         mx_teacher(1)
         wk_vector(unit(0), HEAD_SPLIT)
-        wk_scalar(unit(0), HEAD_SPLIT)
         zt_out_of_psum(0)
         zt_out_of_psum(1)
         x_quant(2)
         x_quant(3)
         wn_quant((0, 1))
         for h in range(2):
-            wn_turn(unit(0), h)
+            wn_turn(unit(0), h, "w%d" % h)
             wn_copy(unit(0), h)
         wk_quant(unit(0))
         wk_vector(unit(1), LOOP_SPLIT)
 
-        last = PAIRS - 1
-        for i in range(1, PAIRS):
+        banks = {(0, 0): "w1", (0, 1): "x", (1, 0): "w0", (1, 1): "s0", (2, 0): "s1", (2, 1): "t0", (3, 0): "t1", (3, 1): "d"}
+
+        def back(key, groups):
+            mx_back(*key, groups, banks[key])
+
+        for i in range(1, PAIRS - 2):
             a, b = 2 * i, 2 * i + 1
-            prepares = i < PAIRS - 2
             mx_student(a)
             mx_student(b)
-            if prepares:
-                wk_scalar(unit(i), LOOP_SPLIT)
-                wn_turn(unit(i), 0)
-                wn_copy(unit(i), 0)
-            if i == last - 1:
-                mx_back(0, 0, (0, 1), "w0")
-                mx_back(1, 0, (0, 1), "x")
-            if i == last:
-                mx_back(0, 1, (0, 1), "w1")
+            if i in (3, 5):
+                back((0, 1), [i // 2 - 1])
+            wk_scalar(unit(i), LOOP_SPLIT)
+            wn_turn(unit(i), 0, "w0")
+            wn_copy(unit(i), 0)
             subtract(i - 1)
             d_scale(nc.gpsimd, i - 1, 0, D_SPLIT)
             mx_teacher(a)
@@ -367,44 +367,64 @@ def tile_teacher_student_logits_s9_kernel(tc, u, gain, w, c, teacher_words, teac
             zs_out_of_psum(b)
             zt_out_of_psum(b)
             d_scale(nc.vector, i - 1, D_SPLIT, 2 * G)
-            if prepares:
-                wn_turn(unit(i), 1)
-                wn_copy(unit(i), 1)
-            if i == 1:
-                spread_gain("x")
+            wn_turn(unit(i), 1, "w1")
+            wn_copy(unit(i), 1)
             d_turn(i - 1)
-            if prepares:
-                wk_quant(unit(i))
-            if i <= PAIRS - 2:
-                wn_quant(unit(i - 1))
+            wk_quant(unit(i))
+            wn_quant(unit(i - 1))
             if i >= 2:
                 d_quant(i - 2)
             if i + 1 < PAIRS - 2:
                 wk_vector(unit(i + 1), LOOP_SPLIT)
 
-        banks = {(0, 0): "w0", (0, 1): "w1", (1, 0): "x", (1, 1): "s0", (2, 0): "s1", (2, 1): "t0", (3, 0): "t1", (3, 1): "w0"}
-        early, late = [(0, 0), (0, 1), (1, 0), (1, 1)], [(2, 0), (2, 1), (3, 0), (3, 1)]
-        for key in early[:3]:
-            mx_back(*key, (2,), banks[key])
-        subtract(last)
-        d_quant(last - 1)
-        d_scale(nc.vector, last, 0, 2 * G)
-        mx_back(1, 1, (0, 1, 2), banks[1, 1])
-        mx_back(2, 0, (0, 1, 2), banks[2, 0])
-        for key in early[:2]:
-            mx_back(*key, (3,), banks[key])
-        d_turn(last)
-        for key in early[2:]:
-            mx_back(*key, (3,), banks[key])
+        mx_student(12)
+        mx_student(13)
+        back((1, 0), (0, 1))
+        subtract(5)
+        d_scale(nc.gpsimd, 5, 0, D_SPLIT)
+        mx_teacher(12)
+        mx_teacher(13)
+        back((0, 0), (0, 1))
+        zs_out_of_psum(12)
+        zt_out_of_psum(12)
+        zs_out_of_psum(13)
+        zt_out_of_psum(13)
+        d_scale(nc.vector, 5, D_SPLIT, 2 * G)
+        mx_student(14)
+        mx_student(15)
+        d_turn(5)
+        d_quant(4)
+        wn_quant(unit(5))
+        for key in ((0, 0), (0, 1)):
+            back(key, (2,))
+        subtract(6)
+        d_scale(nc.gpsimd, 6, 0, 2 * G)
+        mx_teacher(14)
+        mx_teacher(15)
+        zs_out_of_psum(14)
+        zs_out_of_psum(15)
+        subtract(7)
+        zt_out_of_psum(14)
+        zt_out_of_psum(15)
+        back((1, 0), (2,))
+        back((1, 1), (0, 1, 2))
+        d_quant(5)
+        d_scale(nc.vector, 7, 0, 2 * G)
+        d_turn(6)
+        d_quant(6)
+        back((2, 0), (0, 1, 2))
+        back((2, 1), (0,))
+        d_turn(7)
+        for key in ((0, 0), (0, 1), (1, 0), (1, 1)):
+            back(key, (3,))
         du_out_of_psum(0, 0)
-        du_out_of_psum(0, 1)
-        mx_back(2, 1, (0, 1, 2), banks[2, 1])
-        mx_back(3, 0, (0, 1, 2), banks[3, 0])
-        du_out_of_psum(1, 0)
-        d_quant(last)
-        du_out_of_psum(1, 1)
-        for key in late[:3]:
-            mx_back(*key, (3,), banks[key])
+        d_quant(7)
+        for key in ((0, 1), (1, 0), (1, 1)):
             du_out_of_psum(*key)
-        mx_back(3, 1, range(NG), banks[3, 1])
-        du_out_of_psum(3, 1)
+        back((2, 1), (1, 2))
+        for key in ((2, 0), (2, 1)):
+            back(key, (3,))
+            du_out_of_psum(*key)
+        for key in ((3, 0), (3, 1)):
+            back(key, range(NG))
+            du_out_of_psum(*key)

@@ -14,6 +14,7 @@ E4M3 = mybir.dt.float8_e4m3fn_x4
 E5M2 = mybir.dt.float8_e5m2_x4
 E2M1 = mybir.dt.float4_e2m1fn_x4
 MULT = mybir.AluOpType.mult
+ADD = mybir.AluOpType.add
 SUB = mybir.AluOpType.subtract
 
 P = 128
@@ -24,7 +25,9 @@ NG = N // G
 PAIRS = NG * MT // 2
 HEAD_SPLIT = 256
 LOOP_SPLIT = 144
-D_SPLIT = 512
+D_SPLIT = 288
+D_SPLIT_LATE = 448
+D_SPLIT_LAST = 832
 
 
 def tile_teacher_student_logits_s9_kernel(tc, u, gain, w, c, teacher_words, teacher_scales, zs_out, zt_out, du_out):
@@ -144,11 +147,16 @@ def tile_teacher_student_logits_s9_kernel(tc, u, gain, w, c, teacher_words, teac
         def x_quant(m):
             quantize(x_q[m], x_grp[m], E4M3)
 
+        def staging(key, shift):
+            step = 2 * key[0] + key[1] + shift
+            tag = "stage%d" % (step % 3) if step > 0 or shift == 0 else "first%d" % (step % 3)
+            return keep.tile([P, 4 * G], BF16, name="staged", tag=tag, align_bytes=64)
+
         wk_grp = {}
 
         def wk_views(key, first, last):
             if key not in wk_grp:
-                wk_grp[key] = work.tile([P, 4 * G], BF16, name="wk_grp", bufs=3, align_bytes=64)
+                wk_grp[key] = staging(key, -2)
             dst = wk_grp[key][:, 4 * first : 4 * last].rearrange("p (n i j) -> p n j i", j=4, i=4)
             src = w_raw[key][:, :, first:last].rearrange("p j (n i) -> p n j i", i=4)
             return dst, src
@@ -160,6 +168,10 @@ def tile_teacher_student_logits_s9_kernel(tc, u, gain, w, c, teacher_words, teac
         def wk_scalar(key, split):
             dst, src = wk_views(key, split, G)
             nc.scalar.copy(out=dst, in_=src)
+
+        def wk_gpsimd(key, split):
+            dst, src = [view.rearrange("p n j i -> p n i j") for view in wk_views(key, 0, split)]
+            nc.gpsimd.tensor_scalar(out=dst, in0=src, scalar1=1.0, scalar2=0.0, op0=MULT, op1=ADD)
 
         def wk_quant(key):
             quantize(wk_q[key], wk_grp[key], E4M3)
@@ -177,7 +189,7 @@ def tile_teacher_student_logits_s9_kernel(tc, u, gain, w, c, teacher_words, teac
 
         def wn_copy(key, h):
             if h == 0:
-                wn_grp[key] = work.tile([P, 4 * G], BF16, name="wn_grp", bufs=3, align_bytes=64)
+                wn_grp[key] = staging(key, 0)
             dst = wn_grp[key][:].bitcast(F32)[:, G * h : G * (h + 1)]
             nc.scalar.copy(
                 out=dst.rearrange("q (j p u) -> q j p u", j=2, u=2),
@@ -241,7 +253,7 @@ def tile_teacher_student_logits_s9_kernel(tc, u, gain, w, c, teacher_words, teac
 
         def d_scale(eng, i, first, last):
             if i not in d_bf:
-                d_bf[i] = work.tile([P, 2 * G], BF16, name="d_bf", align_bytes=64)
+                d_bf[i] = work.tile([P, 2 * G], BF16, name="d_bf", bufs=3, align_bytes=64)
             g = i // 2
             for h in range(2):
                 a, b = max(first, G * h), min(last, G * (h + 1))
@@ -250,12 +262,15 @@ def tile_teacher_student_logits_s9_kernel(tc, u, gain, w, c, teacher_words, teac
                         out=d_bf[i][:, a:b], in0=diff[i][:, a:b], in1=c_sorted[:, G * (g - h) + a : G * (g - h) + b], op=MULT
                     )
 
-        def d_turn(i):
-            ps = psum.tile([P, 4, P], F32, name="ps_d", tag="d")
+        def d_turn(i, bank):
+            ps = psum.tile([P, 4, P], F32, name="ps_d", tag=bank)
             words = d_bf[i][:].bitcast(F32)
             for j in range(4):
                 nc.tensor.transpose(ps[:, j, :], words[:, P * j : P * (j + 1)], ident[:])
-            d_grp[i] = work.tile([P, 2 * G], BF16, name="d_grp", align_bytes=64)
+            return ps
+
+        def d_copy(i, ps):
+            d_grp[i] = work.tile([P, 2 * G], BF16, name="d_grp", bufs=3, align_bytes=64)
             nc.scalar.copy(
                 out=d_grp[i][:].bitcast(F32).rearrange("p (h m u) -> p h m u", h=2, u=2),
                 in_=ps[:].rearrange("p (h u) m -> p h m u", u=2),
@@ -337,24 +352,24 @@ def tile_teacher_student_logits_s9_kernel(tc, u, gain, w, c, teacher_words, teac
         zt_out_of_psum(1)
         x_quant(2)
         x_quant(3)
-        wn_quant((0, 1))
         for h in range(2):
             wn_turn(unit(0), h, "w%d" % h)
             wn_copy(unit(0), h)
         wk_quant(unit(0))
-        wk_vector(unit(1), LOOP_SPLIT)
+        wn_quant((0, 1))
+        mx_student(2)
+        mx_student(3)
 
-        banks = {(0, 0): "w1", (0, 1): "x", (1, 0): "w0", (1, 1): "s0", (2, 0): "s1", (2, 1): "t0", (3, 0): "t1", (3, 1): "d"}
+        banks = {(0, 0): "w1", (0, 1): "x", (1, 0): "w0", (1, 1): "s0", (2, 0): "t0", (2, 1): "t1", (3, 0): "s1", (3, 1): "d"}
 
         def back(key, groups):
             mx_back(*key, groups, banks[key])
 
         for i in range(1, PAIRS - 2):
             a, b = 2 * i, 2 * i + 1
-            mx_student(a)
-            mx_student(b)
             if i in (3, 5):
                 back((0, 1), [i // 2 - 1])
+            wk_gpsimd(unit(i), LOOP_SPLIT)
             wk_scalar(unit(i), LOOP_SPLIT)
             wn_turn(unit(i), 0, "w0")
             wn_copy(unit(i), 0)
@@ -369,19 +384,17 @@ def tile_teacher_student_logits_s9_kernel(tc, u, gain, w, c, teacher_words, teac
             d_scale(nc.vector, i - 1, D_SPLIT, 2 * G)
             wn_turn(unit(i), 1, "w1")
             wn_copy(unit(i), 1)
-            d_turn(i - 1)
+            d_copy(i - 1, d_turn(i - 1, "d"))
             wk_quant(unit(i))
-            wn_quant(unit(i - 1))
             if i >= 2:
                 d_quant(i - 2)
-            if i + 1 < PAIRS - 2:
-                wk_vector(unit(i + 1), LOOP_SPLIT)
+            wn_quant(unit(i - 1))
+            mx_student(a + 2)
+            mx_student(b + 2)
 
-        mx_student(12)
-        mx_student(13)
         back((1, 0), (0, 1))
         subtract(5)
-        d_scale(nc.gpsimd, 5, 0, D_SPLIT)
+        d_scale(nc.gpsimd, 5, 0, D_SPLIT_LATE)
         mx_teacher(12)
         mx_teacher(13)
         back((0, 0), (0, 1))
@@ -389,16 +402,15 @@ def tile_teacher_student_logits_s9_kernel(tc, u, gain, w, c, teacher_words, teac
         zt_out_of_psum(12)
         zs_out_of_psum(13)
         zt_out_of_psum(13)
-        d_scale(nc.vector, 5, D_SPLIT, 2 * G)
+        d_scale(nc.vector, 5, D_SPLIT_LATE, 2 * G)
         mx_student(14)
         mx_student(15)
-        d_turn(5)
         d_quant(4)
         wn_quant(unit(5))
-        for key in ((0, 0), (0, 1)):
+        for key in ((0, 0), (0, 1), (1, 0)):
             back(key, (2,))
         subtract(6)
-        d_scale(nc.gpsimd, 6, 0, 2 * G)
+        d_scale(nc.gpsimd, 6, 0, D_SPLIT_LAST)
         mx_teacher(14)
         mx_teacher(15)
         zs_out_of_psum(14)
@@ -406,15 +418,17 @@ def tile_teacher_student_logits_s9_kernel(tc, u, gain, w, c, teacher_words, teac
         subtract(7)
         zt_out_of_psum(14)
         zt_out_of_psum(15)
-        back((1, 0), (2,))
         back((1, 1), (0, 1, 2))
-        d_quant(5)
+        d_scale(nc.vector, 6, D_SPLIT_LAST, 2 * G)
         d_scale(nc.vector, 7, 0, 2 * G)
-        d_turn(6)
+        turned = [d_turn(5, "s1"), d_turn(6, "d")]
+        d_copy(6, turned[1])
+        d_copy(5, turned[0])
         d_quant(6)
-        back((2, 0), (0, 1, 2))
+        d_quant(5)
+        back((2, 0), (0, 1))
         back((2, 1), (0,))
-        d_turn(7)
+        d_copy(7, d_turn(7, "d"))
         for key in ((0, 0), (0, 1), (1, 0), (1, 1)):
             back(key, (3,))
         du_out_of_psum(0, 0)
@@ -422,9 +436,10 @@ def tile_teacher_student_logits_s9_kernel(tc, u, gain, w, c, teacher_words, teac
         for key in ((0, 1), (1, 0), (1, 1)):
             du_out_of_psum(*key)
         back((2, 1), (1, 2))
-        for key in ((2, 0), (2, 1)):
-            back(key, (3,))
-            du_out_of_psum(*key)
+        back((2, 0), (2, 3))
+        du_out_of_psum(2, 0)
+        back((2, 1), (3,))
+        du_out_of_psum(2, 1)
         for key in ((3, 0), (3, 1)):
             back(key, range(NG))
             du_out_of_psum(*key)

@@ -23,7 +23,8 @@ MT = M // P
 KG = K // G
 NG = N // G
 PAIRS = NG * MT // 2
-HEAD_SPLIT = 256
+HEAD_SPLIT = 320
+THIRD = 128
 LOOP_SPLIT = 144
 D_SPLIT = 288
 D_SPLIT_LATE = 448
@@ -113,7 +114,7 @@ def tile_teacher_student_logits_s9_kernel(tc, u, gain, w, c, teacher_words, teac
             nc.scalar.copy(out=dst, in_=ps[:].rearrange("q j p -> q p j"))
 
         def sort_c():
-            nc.scalar.copy(
+            nc.vector.tensor_copy(
                 out=c_sorted[:].bitcast(F32).rearrange("q (g u p) -> q g u p", g=NG, u=2),
                 in_=c_all[:].bitcast(F32).rearrange("q (g p u) -> q g u p", g=NG, u=2),
             )
@@ -318,36 +319,35 @@ def tile_teacher_student_logits_s9_kernel(tc, u, gain, w, c, teacher_words, teac
         wk_vector((0, 0), HEAD_SPLIT)
         wk_scalar((0, 0), HEAD_SPLIT)
         c_copy(0, c_ps[0])
-        gain_copy(gain_ps)
+        c_copy(1, c_ps[1])
         x_quant(0)
         wk_quant((0, 0))
         x_scale(1)
         wk_vector((0, 1), HEAD_SPLIT)
         wk_scalar((0, 1), HEAD_SPLIT)
-        c_copy(1, c_ps[1])
+        gain_copy(gain_ps)
         x_quant(1)
         wk_quant((0, 1))
+        sort_c()
         for h in range(2):
             wn_turn((0, 0), h, "w%d" % h)
             wn_copy((0, 0), h)
-        wn_turn((0, 1), 0, "t0")
-        wn_copy((0, 1), 0)
-        sort_c()
+        for h in range(2):
+            wn_turn((0, 1), h, "t%d" % h)
+            wn_copy((0, 1), h)
         mx_student(0)
-        x_turn(2, "x")
         mx_student(1)
+        x_turn(2, "x")
         x_turn(3, "d")
-        wn_turn((0, 1), 1, "t1")
         wn_quant((0, 0))
-        wk_scalar(unit(0), HEAD_SPLIT)
-        wn_copy((0, 1), 1)
         zs_out_of_psum(0)
-        x_scale(2)
         zs_out_of_psum(1)
+        x_scale(2)
         x_scale(3)
         mx_teacher(0)
         mx_teacher(1)
-        wk_vector(unit(0), HEAD_SPLIT)
+        wk_scalar(unit(0), THIRD)
+        wk_vector(unit(0), THIRD)
         zt_out_of_psum(0)
         zt_out_of_psum(1)
         x_quant(2)
@@ -371,8 +371,6 @@ def tile_teacher_student_logits_s9_kernel(tc, u, gain, w, c, teacher_words, teac
                 back((0, 1), [i // 2 - 1])
             wk_gpsimd(unit(i), LOOP_SPLIT)
             wk_scalar(unit(i), LOOP_SPLIT)
-            wn_turn(unit(i), 0, "w0")
-            wn_copy(unit(i), 0)
             subtract(i - 1)
             d_scale(nc.gpsimd, i - 1, 0, D_SPLIT)
             mx_teacher(a)
@@ -382,8 +380,9 @@ def tile_teacher_student_logits_s9_kernel(tc, u, gain, w, c, teacher_words, teac
             zs_out_of_psum(b)
             zt_out_of_psum(b)
             d_scale(nc.vector, i - 1, D_SPLIT, 2 * G)
-            wn_turn(unit(i), 1, "w1")
-            wn_copy(unit(i), 1)
+            for h in range(2):
+                wn_turn(unit(i), h, "w%d" % h)
+                wn_copy(unit(i), h)
             d_copy(i - 1, d_turn(i - 1, "d"))
             wk_quant(unit(i))
             if i >= 2:

@@ -14,7 +14,6 @@ E4M3 = mybir.dt.float8_e4m3fn_x4
 E5M2 = mybir.dt.float8_e5m2_x4
 E2M1 = mybir.dt.float4_e2m1fn_x4
 MULT = mybir.AluOpType.mult
-ADD = mybir.AluOpType.add
 SUB = mybir.AluOpType.subtract
 
 P = 128
@@ -25,9 +24,8 @@ NG = N // G
 PAIRS = NG * MT // 2
 HEAD_SPLIT = 320
 THIRD = 128
-LOOP_SPLIT = 144
-D_SPLIT = 288
-D_SPLIT_LATE = 448
+LOOP_SPLIT = 112
+D_SPLIT = 448
 D_SPLIT_LAST = 832
 
 
@@ -148,16 +146,11 @@ def tile_teacher_student_logits_s9_kernel(tc, u, gain, w, c, teacher_words, teac
         def x_quant(m):
             quantize(x_q[m], x_grp[m], E4M3)
 
-        def staging(key, shift):
-            step = 2 * key[0] + key[1] + shift
-            tag = "stage%d" % (step % 3) if step > 0 or shift == 0 else "first%d" % (step % 3)
-            return keep.tile([P, 4 * G], BF16, name="staged", tag=tag, align_bytes=64)
-
         wk_grp = {}
 
         def wk_views(key, first, last):
             if key not in wk_grp:
-                wk_grp[key] = staging(key, -2)
+                wk_grp[key] = work.tile([P, 4 * G], BF16, name="wk_grp", bufs=3, align_bytes=64)
             dst = wk_grp[key][:, 4 * first : 4 * last].rearrange("p (n i j) -> p n j i", j=4, i=4)
             src = w_raw[key][:, :, first:last].rearrange("p j (n i) -> p n j i", i=4)
             return dst, src
@@ -169,10 +162,6 @@ def tile_teacher_student_logits_s9_kernel(tc, u, gain, w, c, teacher_words, teac
         def wk_scalar(key, split):
             dst, src = wk_views(key, split, G)
             nc.scalar.copy(out=dst, in_=src)
-
-        def wk_gpsimd(key, split):
-            dst, src = [view.rearrange("p n j i -> p n i j") for view in wk_views(key, 0, split)]
-            nc.gpsimd.tensor_scalar(out=dst, in0=src, scalar1=1.0, scalar2=0.0, op0=MULT, op1=ADD)
 
         def wk_quant(key):
             quantize(wk_q[key], wk_grp[key], E4M3)
@@ -190,7 +179,7 @@ def tile_teacher_student_logits_s9_kernel(tc, u, gain, w, c, teacher_words, teac
 
         def wn_copy(key, h):
             if h == 0:
-                wn_grp[key] = staging(key, 0)
+                wn_grp[key] = work.tile([P, 4 * G], BF16, name="wn_grp", bufs=3, align_bytes=64)
             dst = wn_grp[key][:].bitcast(F32)[:, G * h : G * (h + 1)]
             nc.scalar.copy(
                 out=dst.rearrange("q (j p u) -> q j p u", j=2, u=2),
@@ -357,6 +346,7 @@ def tile_teacher_student_logits_s9_kernel(tc, u, gain, w, c, teacher_words, teac
             wn_copy(unit(0), h)
         wk_quant(unit(0))
         wn_quant((0, 1))
+        wk_vector(unit(1), LOOP_SPLIT)
         mx_student(2)
         mx_student(3)
 
@@ -369,8 +359,9 @@ def tile_teacher_student_logits_s9_kernel(tc, u, gain, w, c, teacher_words, teac
             a, b = 2 * i, 2 * i + 1
             if i in (3, 5):
                 back((0, 1), [i // 2 - 1])
-            wk_gpsimd(unit(i), LOOP_SPLIT)
             wk_scalar(unit(i), LOOP_SPLIT)
+            wn_turn(unit(i), 0, "w0")
+            wn_copy(unit(i), 0)
             subtract(i - 1)
             d_scale(nc.gpsimd, i - 1, 0, D_SPLIT)
             mx_teacher(a)
@@ -380,20 +371,21 @@ def tile_teacher_student_logits_s9_kernel(tc, u, gain, w, c, teacher_words, teac
             zs_out_of_psum(b)
             zt_out_of_psum(b)
             d_scale(nc.vector, i - 1, D_SPLIT, 2 * G)
-            for h in range(2):
-                wn_turn(unit(i), h, "w%d" % h)
-                wn_copy(unit(i), h)
+            wn_turn(unit(i), 1, "w1")
+            wn_copy(unit(i), 1)
             d_copy(i - 1, d_turn(i - 1, "d"))
             wk_quant(unit(i))
             if i >= 2:
                 d_quant(i - 2)
             wn_quant(unit(i - 1))
+            if i + 1 < PAIRS - 2:
+                wk_vector(unit(i + 1), LOOP_SPLIT)
             mx_student(a + 2)
             mx_student(b + 2)
 
         back((1, 0), (0, 1))
         subtract(5)
-        d_scale(nc.gpsimd, 5, 0, D_SPLIT_LATE)
+        d_scale(nc.gpsimd, 5, 0, D_SPLIT)
         mx_teacher(12)
         mx_teacher(13)
         back((0, 0), (0, 1))
@@ -401,7 +393,7 @@ def tile_teacher_student_logits_s9_kernel(tc, u, gain, w, c, teacher_words, teac
         zt_out_of_psum(12)
         zs_out_of_psum(13)
         zt_out_of_psum(13)
-        d_scale(nc.vector, 5, D_SPLIT_LATE, 2 * G)
+        d_scale(nc.vector, 5, D_SPLIT, 2 * G)
         mx_student(14)
         mx_student(15)
         d_quant(4)

@@ -23,7 +23,7 @@ KG = K // G
 NG = N // G
 PAIRS = NG * MT // 2
 HEAD_SPLIT = 320
-THIRD = 128
+THIRD = 192
 LOOP_SPLIT = 112
 D_SPLIT = 448
 D_SPLIT_LAST = 832
@@ -49,9 +49,9 @@ def tile_teacher_student_logits_s9_kernel(tc, u, gain, w, c, teacher_words, teac
         gain_all = kept("gain_all", [P, K], BF16)
         c_all = kept("c_all", [P, N], BF16)
         c_sorted = kept("c_sorted", [P, N], BF16)
-        t_scales = kept("t_scales", [P, KG, N], U8)
-        t_first = kept("t_first", [P, KG, 2 * G], U8)
-        t_rest = kept("t_rest", [P, KG, 2 * (N - G)], U8)
+        t_parts = [(0, G), (G, N)]
+        t_words = [kept("t_words%d" % a, [P, KG, 2 * (b - a)], U8) for a, b in t_parts]
+        t_scales = [kept("t_scales%d" % a, [P, KG, b - a], U8) for a, b in t_parts]
         u_sb = [kept("u%d" % m, [P, K], BF16) for m in range(MT)]
         w_raw = {(g, kg): kept("w%d%d" % (g, kg), [P, 4, G], BF16) for g in range(NG) for kg in range(KG)}
         x_q = [operand("x%d" % m, KG * P) for m in range(MT)]
@@ -64,7 +64,8 @@ def tile_teacher_student_logits_s9_kernel(tc, u, gain, w, c, teacher_words, teac
 
         nc.scalar.dma_start(out=gain_t[:], in_=gain.rearrange("(g p t) -> p g t", g=KG, t=4))
         nc.scalar.dma_start(out=c_t[:], in_=c.rearrange("(p i) -> p i", p=P))
-        nc.vector.memset(t_scales[:].rearrange("p g n -> p (g n)").bitcast(I32), 0)
+        for plane in t_scales:
+            nc.vector.memset(plane[:].rearrange("p g n -> p (g n)").bitcast(I32), 0)
         make_identity(nc, ident[:])
 
         def load_u(m):
@@ -77,25 +78,27 @@ def tile_teacher_student_logits_s9_kernel(tc, u, gain, w, c, teacher_words, teac
                     in_=w[G * kg : G * (kg + 1), G * g : G * (g + 1)].rearrange("(p j) n -> p j n", j=4),
                 )
 
-        def load_teacher(dst, first, last):
+        def load_teacher(part):
+            first, last = t_parts[part]
+            for q in range(4):
+                nc.sync.dma_start(
+                    out=t_scales[part][32 * q : 32 * q + 4, :, :].bitcast(I32),
+                    in_=teacher_scales[:, 4 * q : 4 * q + 4, first:last].rearrange("g r n -> r g n").bitcast(I32),
+                )
             words = teacher_words.rearrange("g p n -> p g n")[:, :, 2 * first : 2 * last]
-            nc.sync.dma_start(out=dst[:].bitcast(I32), in_=words.bitcast(I32))
+            nc.sync.dma_start(out=t_words[part][:].bitcast(I32), in_=words.bitcast(I32))
 
         load_u(0)
-        load_w(0, [0])
+        load_w(0)
         load_u(1)
-        load_w(0, [1])
-        for q in range(4):
-            nc.sync.dma_start(
-                out=t_scales[32 * q : 32 * q + 4, :, :].bitcast(I32),
-                in_=teacher_scales[:, 4 * q : 4 * q + 4, :].rearrange("g r n -> r g n").bitcast(I32),
-            )
-        load_teacher(t_first, 0, G)
+        load_w(1, [0])
         load_u(2)
         load_u(3)
-        load_w(1)
-        load_teacher(t_rest, G, N)
-        load_w(2)
+        load_teacher(0)
+        load_w(1, [1])
+        load_w(2, [0])
+        load_teacher(1)
+        load_w(2, [1])
         load_w(3)
 
         def spread(words, tag):
@@ -212,9 +215,11 @@ def tile_teacher_student_logits_s9_kernel(tc, u, gain, w, c, teacher_words, teac
         def mx_teacher(b):
             g, m = divmod(b, MT)
             ps_t[b] = psum.tile([P, G], F32, name="ps_t", tag="t%d" % (b % 2))
-            words, g0 = (t_first, 0) if g == 0 else (t_rest, 1)
-            cols = slice(2 * G * (g - g0), 2 * G * (g - g0 + 1))
-            logits(ps_t[b], m, lambda kg: words[:, kg, cols].bitcast(E2M1), lambda kg: t_scales[:, kg, G * g : G * (g + 1)], range(KG))
+            part = min(g, 1)
+            first = G * (g - part)
+            words = t_words[part][:, :, 2 * first : 2 * (first + G)]
+            scales = t_scales[part][:, :, first : first + G]
+            logits(ps_t[b], m, lambda kg: words[:, kg, :].bitcast(E2M1), lambda kg: scales[:, kg, :], range(KG))
 
         def out_block(out, b):
             g, m = divmod(b, MT)
@@ -303,7 +308,6 @@ def tile_teacher_student_logits_s9_kernel(tc, u, gain, w, c, teacher_words, teac
         x_turn(0, "x")
         c_ps = [c_turn(h, "t%d" % h) for h in range(2)]
         gain_ps = spread(gain_t[:].rearrange("p g t -> p (g t)").bitcast(F32), "s1")
-        x_turn(1, "d")
         x_scale(0)
         wk_vector((0, 0), HEAD_SPLIT)
         wk_scalar((0, 0), HEAD_SPLIT)
@@ -311,41 +315,43 @@ def tile_teacher_student_logits_s9_kernel(tc, u, gain, w, c, teacher_words, teac
         c_copy(1, c_ps[1])
         x_quant(0)
         wk_quant((0, 0))
-        x_scale(1)
         wk_vector((0, 1), HEAD_SPLIT)
         wk_scalar((0, 1), HEAD_SPLIT)
         gain_copy(gain_ps)
-        x_quant(1)
-        wk_quant((0, 1))
-        sort_c()
         for h in range(2):
             wn_turn((0, 0), h, "w%d" % h)
             wn_copy((0, 0), h)
-        for h in range(2):
-            wn_turn((0, 1), h, "t%d" % h)
-            wn_copy((0, 1), h)
+        wn_turn((0, 1), 0, "t0")
+        x_turn(1, "d")
+        wn_turn((0, 1), 1, "t1")
+        wn_copy((0, 1), 0)
+        wn_copy((0, 1), 1)
+        sort_c()
+        wk_quant((0, 1))
+        x_scale(1)
+        wk_vector(unit(0), THIRD)
+        x_quant(1)
+        wn_quant((0, 0))
         mx_student(0)
         mx_student(1)
+        wk_scalar(unit(0), THIRD)
         x_turn(2, "x")
         x_turn(3, "d")
-        wn_quant((0, 0))
         zs_out_of_psum(0)
         zs_out_of_psum(1)
         x_scale(2)
         x_scale(3)
         mx_teacher(0)
         mx_teacher(1)
-        wk_scalar(unit(0), THIRD)
-        wk_vector(unit(0), THIRD)
         zt_out_of_psum(0)
         zt_out_of_psum(1)
+        wn_quant((0, 1))
         x_quant(2)
         x_quant(3)
         for h in range(2):
             wn_turn(unit(0), h, "w%d" % h)
             wn_copy(unit(0), h)
         wk_quant(unit(0))
-        wn_quant((0, 1))
         wk_vector(unit(1), LOOP_SPLIT)
         mx_student(2)
         mx_student(3)

@@ -14,6 +14,7 @@ E4M3 = mybir.dt.float8_e4m3fn_x4
 E5M2 = mybir.dt.float8_e5m2_x4
 E2M1 = mybir.dt.float4_e2m1fn_x4
 MULT = mybir.AluOpType.mult
+ADD = mybir.AluOpType.add
 SUB = mybir.AluOpType.subtract
 
 P = 128
@@ -23,10 +24,8 @@ KG = K // G
 NG = N // G
 PAIRS = NG * MT // 2
 HEAD_SPLIT = 320
-THIRD = 192
-LOOP_SPLIT = 112
-D_SPLIT = 448
-D_SPLIT_LAST = 832
+LOOP_SPLIT = 104
+D_SPLIT = 512
 
 
 def tile_teacher_student_logits_s9_kernel(tc, u, gain, w, c, teacher_words, teacher_scales, zs_out, zt_out, du_out):
@@ -100,6 +99,7 @@ def tile_teacher_student_logits_s9_kernel(tc, u, gain, w, c, teacher_words, teac
         load_teacher(1)
         load_w(2, [1])
         load_w(3)
+        nc.sync.dma_start(out=gain_all[:], in_=gain.partition_broadcast(P))
 
         def spread(words, tag):
             ps = psum.tile([P, 4, P], F32, name="ps_spread", tag=tag)
@@ -118,12 +118,6 @@ def tile_teacher_student_logits_s9_kernel(tc, u, gain, w, c, teacher_words, teac
             nc.vector.tensor_copy(
                 out=c_sorted[:].bitcast(F32).rearrange("q (g u p) -> q g u p", g=NG, u=2),
                 in_=c_all[:].bitcast(F32).rearrange("q (g p u) -> q g u p", g=NG, u=2),
-            )
-
-        def gain_copy(ps):
-            nc.scalar.copy(
-                out=gain_all[:].bitcast(F32).rearrange("q (g p u) -> q g p u", g=KG, u=2),
-                in_=ps[:].rearrange("q (g u) p -> q g p u", u=2),
             )
 
         x_ps, x_grp = {}, {}
@@ -149,11 +143,16 @@ def tile_teacher_student_logits_s9_kernel(tc, u, gain, w, c, teacher_words, teac
         def x_quant(m):
             quantize(x_q[m], x_grp[m], E4M3)
 
+        def staging(key, shift):
+            step = 2 * key[0] + key[1] + shift
+            tag = "stage%d" % (step % 3) if step > 0 or shift == 0 else "first%d" % (step % 3)
+            return keep.tile([P, 4 * G], BF16, name="staged", tag=tag, align_bytes=64)
+
         wk_grp = {}
 
         def wk_views(key, first, last):
             if key not in wk_grp:
-                wk_grp[key] = work.tile([P, 4 * G], BF16, name="wk_grp", bufs=3, align_bytes=64)
+                wk_grp[key] = staging(key, -2)
             dst = wk_grp[key][:, 4 * first : 4 * last].rearrange("p (n i j) -> p n j i", j=4, i=4)
             src = w_raw[key][:, :, first:last].rearrange("p j (n i) -> p n j i", i=4)
             return dst, src
@@ -165,6 +164,10 @@ def tile_teacher_student_logits_s9_kernel(tc, u, gain, w, c, teacher_words, teac
         def wk_scalar(key, split):
             dst, src = wk_views(key, split, G)
             nc.scalar.copy(out=dst, in_=src)
+
+        def wk_gpsimd(key, split):
+            dst, src = [view.rearrange("p n j i -> p n i j") for view in wk_views(key, 0, split)]
+            nc.gpsimd.tensor_scalar(out=dst, in0=src, scalar1=1.0, scalar2=0.0, op0=MULT, op1=ADD)
 
         def wk_quant(key):
             quantize(wk_q[key], wk_grp[key], E4M3)
@@ -182,7 +185,7 @@ def tile_teacher_student_logits_s9_kernel(tc, u, gain, w, c, teacher_words, teac
 
         def wn_copy(key, h):
             if h == 0:
-                wn_grp[key] = work.tile([P, 4 * G], BF16, name="wn_grp", bufs=3, align_bytes=64)
+                wn_grp[key] = staging(key, 0)
             dst = wn_grp[key][:].bitcast(F32)[:, G * h : G * (h + 1)]
             nc.scalar.copy(
                 out=dst.rearrange("q (j p u) -> q j p u", j=2, u=2),
@@ -307,7 +310,6 @@ def tile_teacher_student_logits_s9_kernel(tc, u, gain, w, c, teacher_words, teac
 
         x_turn(0, "x")
         c_ps = [c_turn(h, "t%d" % h) for h in range(2)]
-        gain_ps = spread(gain_t[:].rearrange("p g t -> p (g t)").bitcast(F32), "s1")
         x_scale(0)
         wk_vector((0, 0), HEAD_SPLIT)
         wk_scalar((0, 0), HEAD_SPLIT)
@@ -317,7 +319,6 @@ def tile_teacher_student_logits_s9_kernel(tc, u, gain, w, c, teacher_words, teac
         wk_quant((0, 0))
         wk_vector((0, 1), HEAD_SPLIT)
         wk_scalar((0, 1), HEAD_SPLIT)
-        gain_copy(gain_ps)
         for h in range(2):
             wn_turn((0, 0), h, "w%d" % h)
             wn_copy((0, 0), h)
@@ -329,12 +330,11 @@ def tile_teacher_student_logits_s9_kernel(tc, u, gain, w, c, teacher_words, teac
         sort_c()
         wk_quant((0, 1))
         x_scale(1)
-        wk_vector(unit(0), THIRD)
         x_quant(1)
         wn_quant((0, 0))
         mx_student(0)
         mx_student(1)
-        wk_scalar(unit(0), THIRD)
+        wk_scalar(unit(0), 0)
         x_turn(2, "x")
         x_turn(3, "d")
         zs_out_of_psum(0)
@@ -345,14 +345,13 @@ def tile_teacher_student_logits_s9_kernel(tc, u, gain, w, c, teacher_words, teac
         mx_teacher(1)
         zt_out_of_psum(0)
         zt_out_of_psum(1)
-        wn_quant((0, 1))
         x_quant(2)
         x_quant(3)
         for h in range(2):
             wn_turn(unit(0), h, "w%d" % h)
             wn_copy(unit(0), h)
         wk_quant(unit(0))
-        wk_vector(unit(1), LOOP_SPLIT)
+        wn_quant((0, 1))
         mx_student(2)
         mx_student(3)
 
@@ -365,6 +364,7 @@ def tile_teacher_student_logits_s9_kernel(tc, u, gain, w, c, teacher_words, teac
             a, b = 2 * i, 2 * i + 1
             if i in (3, 5):
                 back((0, 1), [i // 2 - 1])
+            wk_gpsimd(unit(i), LOOP_SPLIT)
             wk_scalar(unit(i), LOOP_SPLIT)
             wn_turn(unit(i), 0, "w0")
             wn_copy(unit(i), 0)
@@ -384,8 +384,6 @@ def tile_teacher_student_logits_s9_kernel(tc, u, gain, w, c, teacher_words, teac
             if i >= 2:
                 d_quant(i - 2)
             wn_quant(unit(i - 1))
-            if i + 1 < PAIRS - 2:
-                wk_vector(unit(i + 1), LOOP_SPLIT)
             mx_student(a + 2)
             mx_student(b + 2)
 
@@ -407,36 +405,37 @@ def tile_teacher_student_logits_s9_kernel(tc, u, gain, w, c, teacher_words, teac
         for key in ((0, 0), (0, 1), (1, 0)):
             back(key, (2,))
         subtract(6)
-        d_scale(nc.gpsimd, 6, 0, D_SPLIT_LAST)
+        d_scale(nc.gpsimd, 6, 0, D_SPLIT)
         mx_teacher(14)
         mx_teacher(15)
         zs_out_of_psum(14)
-        zs_out_of_psum(15)
-        subtract(7)
         zt_out_of_psum(14)
+        zs_out_of_psum(15)
         zt_out_of_psum(15)
+        d_scale(nc.vector, 6, D_SPLIT, 2 * G)
+        subtract(7)
         back((1, 1), (0, 1, 2))
-        d_scale(nc.vector, 6, D_SPLIT_LAST, 2 * G)
-        d_scale(nc.vector, 7, 0, 2 * G)
-        turned = [d_turn(5, "s1"), d_turn(6, "d")]
-        d_copy(6, turned[1])
-        d_copy(5, turned[0])
+        d_copy(6, d_turn(6, "d"))
+        d_copy(5, d_turn(5, "s1"))
+        d_scale(nc.vector, 7, 0, G)
         d_quant(6)
+        d_scale(nc.vector, 7, G, 2 * G)
         d_quant(5)
         back((2, 0), (0, 1))
-        back((2, 1), (0,))
-        d_copy(7, d_turn(7, "d"))
-        for key in ((0, 0), (0, 1), (1, 0), (1, 1)):
+        back((2, 1), (0, 1))
+        for key in ((0, 0), (0, 1), (1, 0)):
             back(key, (3,))
-        du_out_of_psum(0, 0)
+        d_copy(7, d_turn(7, "d"))
+        for key in ((0, 0), (0, 1), (1, 0)):
+            du_out_of_psum(*key)
+        back((1, 1), (3,))
+        back((2, 0), (2,))
+        back((2, 1), (2,))
+        back((3, 0), (0, 1, 2))
         d_quant(7)
-        for key in ((0, 1), (1, 0), (1, 1)):
+        du_out_of_psum(1, 1)
+        for key in ((2, 0), (2, 1), (3, 0)):
+            back(key, (3,))
             du_out_of_psum(*key)
-        back((2, 1), (1, 2))
-        back((2, 0), (2, 3))
-        du_out_of_psum(2, 0)
-        back((2, 1), (3,))
-        du_out_of_psum(2, 1)
-        for key in ((3, 0), (3, 1)):
-            back(key, range(NG))
-            du_out_of_psum(*key)
+        back((3, 1), range(NG))
+        du_out_of_psum(3, 1)

@@ -24,8 +24,9 @@ KG = K // G
 NG = N // G
 PAIRS = NG * MT // 2
 HEAD_SPLIT = 320
-LOOP_SPLIT = 104
-D_SPLIT = 512
+SECOND = 256
+THIRD = 320
+LOOP_SPLIT = 96
 
 
 def tile_teacher_student_logits_s9_kernel(tc, u, gain, w, c, teacher_words, teacher_scales, zs_out, zt_out, du_out):
@@ -88,11 +89,12 @@ def tile_teacher_student_logits_s9_kernel(tc, u, gain, w, c, teacher_words, teac
             nc.sync.dma_start(out=t_words[part][:].bitcast(I32), in_=words.bitcast(I32))
 
         load_u(0)
-        load_w(0)
+        load_w(0, [0])
         load_u(1)
-        load_w(1, [0])
+        load_w(0, [1])
         load_u(2)
         load_u(3)
+        load_w(1, [0])
         load_teacher(0)
         load_w(1, [1])
         load_w(2, [0])
@@ -115,7 +117,7 @@ def tile_teacher_student_logits_s9_kernel(tc, u, gain, w, c, teacher_words, teac
             nc.scalar.copy(out=dst, in_=ps[:].rearrange("q j p -> q p j"))
 
         def sort_c():
-            nc.vector.tensor_copy(
+            nc.scalar.copy(
                 out=c_sorted[:].bitcast(F32).rearrange("q (g u p) -> q g u p", g=NG, u=2),
                 in_=c_all[:].bitcast(F32).rearrange("q (g p u) -> q g u p", g=NG, u=2),
             )
@@ -145,7 +147,7 @@ def tile_teacher_student_logits_s9_kernel(tc, u, gain, w, c, teacher_words, teac
 
         def staging(key, shift):
             step = 2 * key[0] + key[1] + shift
-            tag = "stage%d" % (step % 3) if step > 0 or shift == 0 else "first%d" % (step % 3)
+            tag = "stage%d" % (step % 3) if step >= 0 else "first%d" % (step % 3)
             return keep.tile([P, 4 * G], BF16, name="staged", tag=tag, align_bytes=64)
 
         wk_grp = {}
@@ -239,32 +241,26 @@ def tile_teacher_student_logits_s9_kernel(tc, u, gain, w, c, teacher_words, teac
             nc.scalar.copy(out=zt[:], in_=ps_t[b][:])
             nc.sync.dma_start(out=out_block(zt_out, b), in_=zt[:])
 
-        def subtract(i):
-            diff[i] = work.tile([P, 2 * G], F32, name="diff", align_bytes=64)
-            for h in range(2):
-                nc.vector.tensor_tensor(
-                    out=diff[i][:, G * h : G * (h + 1)].rearrange("m (u p e) -> m u p e", u=2, e=2),
-                    in0=zs[2 * i + h][:].rearrange("m (p u e) -> m u p e", u=2, e=2),
-                    in1=ps_t[2 * i + h][:].rearrange("m (p u e) -> m u p e", u=2, e=2),
-                    op=SUB,
-                )
+        def subtract(b):
+            diff[b] = work.tile([P, G], F32, name="diff", bufs=4, align_bytes=64)
+            nc.vector.tensor_tensor(
+                out=diff[b][:].rearrange("m (u p e) -> m u p e", u=2, e=2),
+                in0=zs[b][:].rearrange("m (p u e) -> m u p e", u=2, e=2),
+                in1=ps_t[b][:].rearrange("m (p u e) -> m u p e", u=2, e=2),
+                op=SUB,
+            )
 
-        def d_scale(eng, i, first, last):
-            if i not in d_bf:
-                d_bf[i] = work.tile([P, 2 * G], BF16, name="d_bf", bufs=3, align_bytes=64)
-            g = i // 2
-            for h in range(2):
-                a, b = max(first, G * h), min(last, G * (h + 1))
-                if a < b:
-                    eng.tensor_tensor(
-                        out=d_bf[i][:, a:b], in0=diff[i][:, a:b], in1=c_sorted[:, G * (g - h) + a : G * (g - h) + b], op=MULT
-                    )
+        def d_scale(eng, b, tile=None):
+            g = b // MT
+            d_bf[b] = work.tile([P, G], BF16, name="d_bf", bufs=6, align_bytes=64) if tile is None else tile
+            eng.tensor_tensor(out=d_bf[b][:, 0:G], in0=diff[b][:], in1=c_sorted[:, G * g : G * (g + 1)], op=MULT)
 
         def d_turn(i, bank):
             ps = psum.tile([P, 4, P], F32, name="ps_d", tag=bank)
-            words = d_bf[i][:].bitcast(F32)
-            for j in range(4):
-                nc.tensor.transpose(ps[:, j, :], words[:, P * j : P * (j + 1)], ident[:])
+            for h in range(2):
+                words = d_bf[2 * i + h][:, 0:G].bitcast(F32)
+                for half in range(2):
+                    nc.tensor.transpose(ps[:, 2 * h + half, :], words[:, P * half : P * (half + 1)], ident[:])
             return ps
 
         def d_copy(i, ps):
@@ -311,45 +307,46 @@ def tile_teacher_student_logits_s9_kernel(tc, u, gain, w, c, teacher_words, teac
         x_turn(0, "x")
         c_ps = [c_turn(h, "t%d" % h) for h in range(2)]
         x_scale(0)
+        c_copy(0, c_ps[0])
         wk_vector((0, 0), HEAD_SPLIT)
         wk_scalar((0, 0), HEAD_SPLIT)
-        c_copy(0, c_ps[0])
         c_copy(1, c_ps[1])
         x_quant(0)
         wk_quant((0, 0))
-        wk_vector((0, 1), HEAD_SPLIT)
-        wk_scalar((0, 1), HEAD_SPLIT)
-        for h in range(2):
-            wn_turn((0, 0), h, "w%d" % h)
-            wn_copy((0, 0), h)
-        wn_turn((0, 1), 0, "t0")
+        wn_turn((0, 0), 0, "w0")
         x_turn(1, "d")
-        wn_turn((0, 1), 1, "t1")
-        wn_copy((0, 1), 0)
-        wn_copy((0, 1), 1)
-        sort_c()
-        wk_quant((0, 1))
+        wn_turn((0, 0), 1, "w1")
+        wn_copy((0, 0), 0)
         x_scale(1)
+        wk_vector((0, 1), SECOND)
+        wk_scalar((0, 1), SECOND)
+        wn_copy((0, 0), 1)
         x_quant(1)
-        wn_quant((0, 0))
-        mx_student(0)
-        mx_student(1)
-        wk_scalar(unit(0), 0)
+        wk_quant((0, 1))
+        for h in range(2):
+            wn_turn((0, 1), h, "t%d" % h)
+            wn_copy((0, 1), h)
         x_turn(2, "x")
         x_turn(3, "d")
-        zs_out_of_psum(0)
-        zs_out_of_psum(1)
+        mx_student(0)
+        mx_student(1)
+        wn_quant((0, 0))
+        sort_c()
+        wk_gpsimd(unit(0), THIRD)
+        wk_scalar(unit(0), THIRD)
         x_scale(2)
         x_scale(3)
+        zs_out_of_psum(0)
+        zs_out_of_psum(1)
+        for h in range(2):
+            wn_turn(unit(0), h, "w%d" % h)
+            wn_copy(unit(0), h)
         mx_teacher(0)
         mx_teacher(1)
         zt_out_of_psum(0)
         zt_out_of_psum(1)
         x_quant(2)
         x_quant(3)
-        for h in range(2):
-            wn_turn(unit(0), h, "w%d" % h)
-            wn_copy(unit(0), h)
         wk_quant(unit(0))
         wn_quant((0, 1))
         mx_student(2)
@@ -368,15 +365,16 @@ def tile_teacher_student_logits_s9_kernel(tc, u, gain, w, c, teacher_words, teac
             wk_scalar(unit(i), LOOP_SPLIT)
             wn_turn(unit(i), 0, "w0")
             wn_copy(unit(i), 0)
-            subtract(i - 1)
-            d_scale(nc.gpsimd, i - 1, 0, D_SPLIT)
+            subtract(a - 2)
+            subtract(b - 2)
+            d_scale(nc.gpsimd, a - 2)
             mx_teacher(a)
             mx_teacher(b)
             zs_out_of_psum(a)
             zt_out_of_psum(a)
             zs_out_of_psum(b)
             zt_out_of_psum(b)
-            d_scale(nc.vector, i - 1, D_SPLIT, 2 * G)
+            d_scale(nc.vector, b - 2)
             wn_turn(unit(i), 1, "w1")
             wn_copy(unit(i), 1)
             d_copy(i - 1, d_turn(i - 1, "d"))
@@ -388,8 +386,9 @@ def tile_teacher_student_logits_s9_kernel(tc, u, gain, w, c, teacher_words, teac
             mx_student(b + 2)
 
         back((1, 0), (0, 1))
-        subtract(5)
-        d_scale(nc.gpsimd, 5, 0, D_SPLIT)
+        subtract(10)
+        subtract(11)
+        d_scale(nc.gpsimd, 10)
         mx_teacher(12)
         mx_teacher(13)
         back((0, 0), (0, 1))
@@ -397,45 +396,49 @@ def tile_teacher_student_logits_s9_kernel(tc, u, gain, w, c, teacher_words, teac
         zt_out_of_psum(12)
         zs_out_of_psum(13)
         zt_out_of_psum(13)
-        d_scale(nc.vector, 5, D_SPLIT, 2 * G)
         mx_student(14)
         mx_student(15)
         d_quant(4)
         wn_quant(unit(5))
+        d_scale(nc.gpsimd, 11, staging(unit(5), 0))
         for key in ((0, 0), (0, 1), (1, 0)):
             back(key, (2,))
-        subtract(6)
-        d_scale(nc.gpsimd, 6, 0, D_SPLIT)
+        subtract(12)
+        subtract(13)
+        d_scale(nc.gpsimd, 12)
         mx_teacher(14)
         mx_teacher(15)
         zs_out_of_psum(14)
-        zt_out_of_psum(14)
         zs_out_of_psum(15)
+        subtract(14)
         zt_out_of_psum(15)
-        d_scale(nc.vector, 6, D_SPLIT, 2 * G)
-        subtract(7)
+        zt_out_of_psum(14)
+        d_scale(nc.vector, 13)
+        subtract(15)
         back((1, 1), (0, 1, 2))
+        turned = d_turn(5, "s1")
         d_copy(6, d_turn(6, "d"))
-        d_copy(5, d_turn(5, "s1"))
-        d_scale(nc.vector, 7, 0, G)
+        d_copy(5, turned)
+        d_scale(nc.vector, 14)
+        d_scale(nc.vector, 15)
         d_quant(6)
-        d_scale(nc.vector, 7, G, 2 * G)
         d_quant(5)
         back((2, 0), (0, 1))
         back((2, 1), (0, 1))
-        for key in ((0, 0), (0, 1), (1, 0)):
-            back(key, (3,))
         d_copy(7, d_turn(7, "d"))
-        for key in ((0, 0), (0, 1), (1, 0)):
+        for key in ((0, 0), (0, 1), (1, 0), (1, 1)):
+            back(key, (3,))
+        du_out_of_psum(0, 0)
+        d_quant(7)
+        for key in ((0, 1), (1, 0), (1, 1)):
             du_out_of_psum(*key)
-        back((1, 1), (3,))
         back((2, 0), (2,))
         back((2, 1), (2,))
-        back((3, 0), (0, 1, 2))
-        d_quant(7)
-        du_out_of_psum(1, 1)
-        for key in ((2, 0), (2, 1), (3, 0)):
+        back((3, 0), (0,))
+        for key in ((2, 0), (2, 1)):
             back(key, (3,))
             du_out_of_psum(*key)
+        back((3, 0), (1, 2, 3))
+        du_out_of_psum(3, 0)
         back((3, 1), range(NG))
         du_out_of_psum(3, 1)

@@ -23,10 +23,11 @@ MT = M // P
 KG = K // G
 NG = N // G
 PAIRS = NG * MT // 2
-HEAD_SPLIT = 320
-SECOND = 256
-THIRD = 320
-LOOP_SPLIT = 96
+H0 = 256
+H1 = 320
+H2 = 160
+GS = 352
+SA = 256
 
 
 def tile_teacher_student_logits_s9_kernel(tc, u, gain, w, c, teacher_words, teacher_scales, zs_out, zt_out, du_out):
@@ -45,9 +46,8 @@ def tile_teacher_student_logits_s9_kernel(tc, u, gain, w, c, teacher_words, teac
 
         ident = kept("ident", [P, P], F32)
         gain_t = kept("gain_t", [P, KG, 4], BF16)
-        c_t = kept("c_t", [P, N // P], BF16)
+        c_t = kept("c_t", [P, NG, 4], BF16)
         gain_all = kept("gain_all", [P, K], BF16)
-        c_all = kept("c_all", [P, N], BF16)
         c_sorted = kept("c_sorted", [P, N], BF16)
         t_parts = [(0, G), (G, N)]
         t_words = [kept("t_words%d" % a, [P, KG, 2 * (b - a)], U8) for a, b in t_parts]
@@ -62,45 +62,51 @@ def tile_teacher_student_logits_s9_kernel(tc, u, gain, w, c, teacher_words, teac
         def quantize(dst, src, fmt):
             nc.vector.quantize_mx(out=dst[0][:].bitcast(fmt), scales=dst[1][:], in_=src[:])
 
-        nc.scalar.dma_start(out=gain_t[:], in_=gain.rearrange("(g p t) -> p g t", g=KG, t=4))
-        nc.scalar.dma_start(out=c_t[:], in_=c.rearrange("(p i) -> p i", p=P))
-        for plane in t_scales:
-            nc.vector.memset(plane[:].rearrange("p g n -> p (g n)").bitcast(I32), 0)
-        make_identity(nc, ident[:])
-
         def load_u(m):
             nc.sync.dma_start(out=u_sb[m][:], in_=u[m * P : (m + 1) * P, :])
 
-        def load_w(g, groups=range(KG)):
-            for kg in groups:
-                nc.sync.dma_start(
-                    out=w_raw[g, kg][:],
-                    in_=w[G * kg : G * (kg + 1), G * g : G * (g + 1)].rearrange("(p j) n -> p j n", j=4),
-                )
+        def load_w(n):
+            g, kg = tile_key(n)
+            nc.sync.dma_start(
+                out=w_raw[g, kg][:],
+                in_=w[G * kg : G * (kg + 1), G * g : G * (g + 1)].rearrange("(p j) n -> p j n", j=4),
+            )
 
-        def load_teacher(part):
+        def load_scales(queue, part):
             first, last = t_parts[part]
             for q in range(4):
-                nc.sync.dma_start(
+                queue.dma_start(
                     out=t_scales[part][32 * q : 32 * q + 4, :, :].bitcast(I32),
                     in_=teacher_scales[:, 4 * q : 4 * q + 4, first:last].rearrange("g r n -> r g n").bitcast(I32),
                 )
+
+        def load_words(part):
+            first, last = t_parts[part]
             words = teacher_words.rearrange("g p n -> p g n")[:, :, 2 * first : 2 * last]
             nc.sync.dma_start(out=t_words[part][:].bitcast(I32), in_=words.bitcast(I32))
 
+        def tile_key(n):
+            return divmod(n, KG)
+
+        for plane in t_scales:
+            nc.vector.memset(plane[:].rearrange("p g n -> p (g n)").bitcast(I32), 0)
+        make_identity(nc, ident[:])
+        nc.scalar.dma_start(out=gain_t[:], in_=gain.rearrange("(g p t) -> p g t", g=KG, t=4))
+        nc.scalar.dma_start(out=c_t[:], in_=c.rearrange("(g p e) -> p g e", g=NG, e=4))
         load_u(0)
-        load_w(0, [0])
+        load_w(0)
         load_u(1)
-        load_w(0, [1])
+        load_words(0)
+        load_scales(nc.sync, 0)
         load_u(2)
+        load_w(1)
         load_u(3)
-        load_w(1, [0])
-        load_teacher(0)
-        load_w(1, [1])
-        load_w(2, [0])
-        load_teacher(1)
-        load_w(2, [1])
+        load_w(2)
         load_w(3)
+        load_scales(nc.sync, 1)
+        load_words(1)
+        for n in range(4, 8):
+            load_w(n)
         nc.sync.dma_start(out=gain_all[:], in_=gain.partition_broadcast(P))
 
         def spread(words, tag):
@@ -110,17 +116,10 @@ def tile_teacher_student_logits_s9_kernel(tc, u, gain, w, c, teacher_words, teac
             return ps
 
         def c_turn(h, tag):
-            return spread(c_t[:].bitcast(F32)[:, 4 * h : 4 * h + 4], tag)
+            return spread(c_t[:].rearrange("p g e -> p (g e)").bitcast(F32)[:, 4 * h : 4 * h + 4], tag)
 
         def c_copy(h, ps):
-            dst = c_all[:].bitcast(F32).rearrange("q (p j) -> q p j", j=8)[:, :, 4 * h : 4 * h + 4]
-            nc.scalar.copy(out=dst, in_=ps[:].rearrange("q j p -> q p j"))
-
-        def sort_c():
-            nc.scalar.copy(
-                out=c_sorted[:].bitcast(F32).rearrange("q (g u p) -> q g u p", g=NG, u=2),
-                in_=c_all[:].bitcast(F32).rearrange("q (g p u) -> q g u p", g=NG, u=2),
-            )
+            nc.scalar.copy(out=c_sorted[:].bitcast(F32)[:, G * h : G * (h + 1)], in_=ps[:].rearrange("q j p -> q (j p)"))
 
         x_ps, x_grp = {}, {}
 
@@ -131,8 +130,8 @@ def tile_teacher_student_logits_s9_kernel(tc, u, gain, w, c, teacher_words, teac
                 for half in range(2):
                     nc.tensor.transpose(x_ps[m][:, 2 * kg + half, :], words[:, 256 * kg + half : 256 * (kg + 1) : 2], ident[:])
 
-        def x_scale(m):
-            x_grp[m] = work.tile([P, K], BF16, name="x_grp", align_bytes=64)
+        def x_scale(m, tag):
+            x_grp[m] = staging(tag)[:, 0:K]
             for kg in range(KG):
                 turned = x_ps[m][:, 2 * kg : 2 * kg + 2, :].bitcast(BF16)
                 nc.vector.tensor_tensor(
@@ -145,30 +144,29 @@ def tile_teacher_student_logits_s9_kernel(tc, u, gain, w, c, teacher_words, teac
         def x_quant(m):
             quantize(x_q[m], x_grp[m], E4M3)
 
-        def staging(key, shift):
-            step = 2 * key[0] + key[1] + shift
-            tag = "stage%d" % (step % 3) if step >= 0 else "first%d" % (step % 3)
+        def staging(tag):
             return keep.tile([P, 4 * G], BF16, name="staged", tag=tag, align_bytes=64)
 
         wk_grp = {}
 
+        def wk_stage(key, tag):
+            wk_grp[key] = staging(tag)
+
         def wk_views(key, first, last):
-            if key not in wk_grp:
-                wk_grp[key] = staging(key, -2)
             dst = wk_grp[key][:, 4 * first : 4 * last].rearrange("p (n i j) -> p n j i", j=4, i=4)
             src = w_raw[key][:, :, first:last].rearrange("p j (n i) -> p n j i", i=4)
             return dst, src
 
-        def wk_vector(key, split):
-            dst, src = wk_views(key, 0, split)
+        def wk_vector(key, first, last):
+            dst, src = wk_views(key, first, last)
             nc.vector.tensor_copy(out=dst, in_=src)
 
-        def wk_scalar(key, split):
-            dst, src = wk_views(key, split, G)
+        def wk_scalar(key, first, last):
+            dst, src = wk_views(key, first, last)
             nc.scalar.copy(out=dst, in_=src)
 
-        def wk_gpsimd(key, split):
-            dst, src = [view.rearrange("p n j i -> p n i j") for view in wk_views(key, 0, split)]
+        def wk_gpsimd(key, first, last):
+            dst, src = [view.rearrange("p n j i -> p n i j") for view in wk_views(key, first, last)]
             nc.gpsimd.tensor_scalar(out=dst, in0=src, scalar1=1.0, scalar2=0.0, op0=MULT, op1=ADD)
 
         def wk_quant(key):
@@ -185,11 +183,11 @@ def tile_teacher_student_logits_s9_kernel(tc, u, gain, w, c, teacher_words, teac
                 for half in range(2):
                     nc.tensor.transpose(wn_ps[key, h][:, 2 * j + half, :], words[:, half:256:2], ident[:])
 
-        def wn_copy(key, h):
+        def wn_copy(key, h, tag=None, move=nc.scalar.copy):
             if h == 0:
-                wn_grp[key] = staging(key, 0)
+                wn_grp[key] = staging(tag)
             dst = wn_grp[key][:].bitcast(F32)[:, G * h : G * (h + 1)]
-            nc.scalar.copy(
+            move(
                 out=dst.rearrange("q (j p u) -> q j p u", j=2, u=2),
                 in_=wn_ps[key, h][:].rearrange("q (j u) p -> q j p u", u=2),
             )
@@ -233,7 +231,12 @@ def tile_teacher_student_logits_s9_kernel(tc, u, gain, w, c, teacher_words, teac
         def zs_out_of_psum(b):
             g = b // MT
             zs[b] = work.tile([P, G], F32, name="zs", bufs=8)
-            nc.vector.tensor_tensor(out=zs[b][:], in0=ps_s[b][:], in1=c_all[:, G * g : G * (g + 1)], op=MULT)
+            nc.vector.tensor_tensor(
+                out=zs[b][:].rearrange("m (p u e) -> m p u e", u=2, e=2),
+                in0=ps_s[b][:].rearrange("m (p u e) -> m p u e", u=2, e=2),
+                in1=c_sorted[:, G * g : G * (g + 1)].rearrange("m (u p e) -> m p u e", u=2, e=2),
+                op=MULT,
+            )
             nc.sync.dma_start(out=out_block(zs_out, b), in_=zs[b][:])
 
         def zt_out_of_psum(b):
@@ -242,30 +245,43 @@ def tile_teacher_student_logits_s9_kernel(tc, u, gain, w, c, teacher_words, teac
             nc.sync.dma_start(out=out_block(zt_out, b), in_=zt[:])
 
         def subtract(b):
-            diff[b] = work.tile([P, G], F32, name="diff", bufs=4, align_bytes=64)
+            i, h = divmod(b, 2)
+            if h == 0:
+                diff[i] = keep.tile([P, 2, G], F32, name="diff", tag="diff%d" % (i if i % 2 else i % 4), align_bytes=64)
             nc.vector.tensor_tensor(
-                out=diff[b][:].rearrange("m (u p e) -> m u p e", u=2, e=2),
+                out=diff[i][:, h, :].rearrange("m (u p e) -> m u p e", u=2, e=2),
                 in0=zs[b][:].rearrange("m (p u e) -> m u p e", u=2, e=2),
                 in1=ps_t[b][:].rearrange("m (p u e) -> m u p e", u=2, e=2),
                 op=SUB,
             )
 
-        def d_scale(eng, b, tile=None):
-            g = b // MT
-            d_bf[b] = work.tile([P, G], BF16, name="d_bf", bufs=6, align_bytes=64) if tile is None else tile
-            eng.tensor_tensor(out=d_bf[b][:, 0:G], in0=diff[b][:], in1=c_sorted[:, G * g : G * (g + 1)], op=MULT)
+        def d_stage(i, tag):
+            d_bf[i] = staging(tag)
+
+        def d_scale(eng, i, first, last, factors):
+            n = last - first
+            out = d_bf[i][:, G * first : G * last].rearrange("m (h n) -> m h n", n=G)
+            eng.tensor_tensor(out=out, in0=diff[i][:, first:last, :], in1=factors.unsqueeze(1).to_broadcast([P, n, G]), op=MULT)
+
+        def d_gpsimd(i, tag):
+            d_stage(i, tag)
+            d_scale(nc.gpsimd, i, 0, 2, c_sorted[:, G * (i // 2) : G * (i // 2 + 1)])
+
+        def d_vector(i, first, last, c_late):
+            g = i // 2 - 2
+            d_scale(nc.vector, i, first, last, c_late[:].rearrange("q j p -> q (j p)").bitcast(BF16)[:, G * g : G * (g + 1)])
 
         def d_turn(i, bank):
             ps = psum.tile([P, 4, P], F32, name="ps_d", tag=bank)
             for h in range(2):
-                words = d_bf[2 * i + h][:, 0:G].bitcast(F32)
+                words = d_bf[i][:, G * h : G * (h + 1)].bitcast(F32)
                 for half in range(2):
                     nc.tensor.transpose(ps[:, 2 * h + half, :], words[:, P * half : P * (half + 1)], ident[:])
             return ps
 
-        def d_copy(i, ps):
-            d_grp[i] = work.tile([P, 2 * G], BF16, name="d_grp", bufs=3, align_bytes=64)
-            nc.scalar.copy(
+        def d_copy(i, ps, move=nc.scalar.copy):
+            d_grp[i] = work.tile([P, 2 * G], BF16, name="d_grp", bufs=4, align_bytes=64)
+            move(
                 out=d_grp[i][:].bitcast(F32).rearrange("p (h m u) -> p h m u", h=2, u=2),
                 in_=ps[:].rearrange("p (h u) m -> p h m u", u=2),
             )
@@ -273,12 +289,14 @@ def tile_teacher_student_logits_s9_kernel(tc, u, gain, w, c, teacher_words, teac
         def d_quant(i):
             quantize(d_q[i], d_grp[i], E5M2)
 
-        dx = {}
+        dx, passes = {}, {}
 
         def mx_back(m, kg, groups, tag):
             if (m, kg) not in dx:
                 dx[m, kg] = psum.tile([P, G], F32, name="ps_dx", tag=tag)
+                passes[m, kg] = 0
             for g in groups:
+                passes[m, kg] += 1
                 codes, scales = d_q[2 * g + m // 2]
                 cols = slice(P * (m % 2), P * (m % 2 + 1))
                 nc.tensor.matmul_mx(
@@ -287,8 +305,8 @@ def tile_teacher_student_logits_s9_kernel(tc, u, gain, w, c, teacher_words, teac
                     lhsT_scale=scales[:, cols],
                     rhs=wn_q[g, kg][0][:].bitcast(E4M3),
                     rhs_scale=wn_q[g, kg][1][:],
-                    start=(g == 0),
-                    stop=(g == NG - 1),
+                    start=(passes[m, kg] == 1),
+                    stop=(passes[m, kg] == NG),
                 )
 
         def du_out_of_psum(m, kg):
@@ -301,144 +319,169 @@ def tile_teacher_student_logits_s9_kernel(tc, u, gain, w, c, teacher_words, teac
             )
             nc.sync.dma_start(out=du_out[m * P : (m + 1) * P, G * kg : G * (kg + 1)], in_=du[:])
 
-        def unit(i):
-            return (i // 2 + 1, i % 2)
-
-        x_turn(0, "x")
-        c_ps = [c_turn(h, "t%d" % h) for h in range(2)]
-        x_scale(0)
-        c_copy(0, c_ps[0])
-        wk_vector((0, 0), HEAD_SPLIT)
-        wk_scalar((0, 0), HEAD_SPLIT)
-        c_copy(1, c_ps[1])
-        x_quant(0)
-        wk_quant((0, 0))
-        wn_turn((0, 0), 0, "w0")
-        x_turn(1, "d")
-        wn_turn((0, 0), 1, "w1")
-        wn_copy((0, 0), 0)
-        x_scale(1)
-        wk_vector((0, 1), SECOND)
-        wk_scalar((0, 1), SECOND)
-        wn_copy((0, 0), 1)
-        x_quant(1)
-        wk_quant((0, 1))
-        for h in range(2):
-            wn_turn((0, 1), h, "t%d" % h)
-            wn_copy((0, 1), h)
-        x_turn(2, "x")
-        x_turn(3, "d")
-        mx_student(0)
-        mx_student(1)
-        wn_quant((0, 0))
-        sort_c()
-        wk_gpsimd(unit(0), THIRD)
-        wk_scalar(unit(0), THIRD)
-        x_scale(2)
-        x_scale(3)
-        zs_out_of_psum(0)
-        zs_out_of_psum(1)
-        for h in range(2):
-            wn_turn(unit(0), h, "w%d" % h)
-            wn_copy(unit(0), h)
-        mx_teacher(0)
-        mx_teacher(1)
-        zt_out_of_psum(0)
-        zt_out_of_psum(1)
-        x_quant(2)
-        x_quant(3)
-        wk_quant(unit(0))
-        wn_quant((0, 1))
-        mx_student(2)
-        mx_student(3)
-
-        banks = {(0, 0): "w1", (0, 1): "x", (1, 0): "w0", (1, 1): "s0", (2, 0): "t0", (2, 1): "t1", (3, 0): "s1", (3, 1): "d"}
 
         def back(key, groups):
             mx_back(*key, groups, banks[key])
 
-        for i in range(1, PAIRS - 2):
-            a, b = 2 * i, 2 * i + 1
-            if i in (3, 5):
-                back((0, 1), [i // 2 - 1])
-            wk_gpsimd(unit(i), LOOP_SPLIT)
-            wk_scalar(unit(i), LOOP_SPLIT)
-            wn_turn(unit(i), 0, "w0")
-            wn_copy(unit(i), 0)
-            subtract(a - 2)
-            subtract(b - 2)
-            d_scale(nc.gpsimd, a - 2)
-            mx_teacher(a)
-            mx_teacher(b)
-            zs_out_of_psum(a)
-            zt_out_of_psum(a)
-            zs_out_of_psum(b)
-            zt_out_of_psum(b)
-            d_scale(nc.vector, b - 2)
-            wn_turn(unit(i), 1, "w1")
-            wn_copy(unit(i), 1)
-            d_copy(i - 1, d_turn(i - 1, "d"))
-            wk_quant(unit(i))
-            if i >= 2:
-                d_quant(i - 2)
-            wn_quant(unit(i - 1))
-            mx_student(a + 2)
-            mx_student(b + 2)
+        def ring(n):
+            return "ring%d" % (n % 4)
 
-        back((1, 0), (0, 1))
-        subtract(10)
-        subtract(11)
-        d_scale(nc.gpsimd, 10)
-        mx_teacher(12)
-        mx_teacher(13)
-        back((0, 0), (0, 1))
-        zs_out_of_psum(12)
-        zt_out_of_psum(12)
-        zs_out_of_psum(13)
-        zt_out_of_psum(13)
-        mx_student(14)
-        mx_student(15)
+        x_turn(0, "x")
+        c_ps = [c_turn(h, "w%d" % h) for h in range(2)]
+        x_turn(1, "d")
+        x_scale(0, ring(2))
+        wk_stage((0, 0), "k0")
+        wk_scalar((0, 0), H0, G)
+        wk_vector((0, 0), 0, H0)
+        c_copy(0, c_ps[0])
+        c_copy(1, c_ps[1])
+        x_quant(0)
+        mx_teacher(0)
+        x_scale(1, ring(3))
+        x_turn(2, "x")
+        wk_quant((0, 0))
+        mx_student(0, [0])
+        x_quant(1)
+        mx_teacher(1)
+        mx_student(1, [0])
+        wk_stage((0, 1), "k1")
+        wk_scalar((0, 1), H1, G)
+        wk_vector((0, 1), 0, H1)
+        x_scale(2, "k2")
+        x_turn(3, "d")
+        wn_turn((0, 0), 0, "w0")
+        wk_quant((0, 1))
+        mx_student(0, [1])
+        mx_student(1, [1])
+        x_quant(2)
+        wn_turn((0, 0), 1, "w1")
+        zt_out_of_psum(0)
+        zt_out_of_psum(1)
+        wk_stage(tile_key(2), "k2")
+        wk_gpsimd(tile_key(2), 0, H2)
+        wk_scalar(tile_key(2), H2, G)
+        wn_copy((0, 0), 0, ring(0))
+        wn_turn((0, 1), 0, "x")
+        x_scale(3, "k0")
+        x_quant(3)
+        wk_stage(tile_key(3), "k0")
+        wk_gpsimd(tile_key(3), 0, GS)
+        wn_copy((0, 0), 1)
+        wk_scalar(tile_key(3), GS, G)
+        zs_out_of_psum(0)
+        zs_out_of_psum(1)
+        subtract(0)
+        subtract(1)
+        wn_turn((0, 1), 1, "d")
+        wn_copy((0, 1), 0, ring(1))
+        wn_copy((0, 1), 1)
+        wk_quant(tile_key(2))
+        wk_quant(tile_key(3))
+
+        def pair_passes(i):
+            mx_student(2 * i)
+            mx_student(2 * i + 1)
+            mx_teacher(2 * i)
+            mx_teacher(2 * i + 1)
+
+        def pair_out(i):
+            a, b = 2 * i, 2 * i + 1
+            zt_out_of_psum(a)
+            zt_out_of_psum(b)
+            zs_out_of_psum(a)
+            zs_out_of_psum(b)
+            subtract(a)
+            subtract(b)
+
+        def turn_w(n, move=nc.scalar.copy):
+            for h in range(2):
+                wn_turn(tile_key(n), h, "w%d" % h)
+            wn_copy(tile_key(n), 0, ring(n), move)
+            wn_copy(tile_key(n), 1)
+
+        for i in range(1, 5):
+            key = tile_key(i + 3)
+            held = "k0" if i == 1 else ring(i - 2)
+            pair_passes(i)
+            if i % 2:
+                wk_stage(key, held)
+                wk_gpsimd(key, 0, GS)
+            else:
+                d_gpsimd(i - 2, held)
+            pair_out(i)
+            wk_scalar(key, GS if i % 2 else SA, G)
+            if i == 3:
+                d_copy(0, d_turn(0, "d"))
+            if i == 4:
+                c_late = c_turn(1, "x")
+            turn_w(i + 1, nc.scalar.copy if i % 2 else nc.vector.tensor_copy)
+            wk_quant(key)
+            if i == 4:
+                d_quant(0)
+            wn_quant(tile_key(i - 1))
+            if i % 2:
+                wk_stage(tile_key(i + 4), "k1")
+                wk_scalar(tile_key(i + 4), 0, SA)
+
+        banks = {(0, 0): "w0", (0, 1): "w1", (1, 0): "s0", (1, 1): "s1", (2, 0): "t0", (2, 1): "t1", (3, 0): "x", (3, 1): "w0"}
+        pair_passes(5)
+        d_gpsimd(4, ring(3))
+        pair_out(5)
+        d_copy(2, d_turn(2, "d"))
+        turn_w(6)
+        d_stage(5, "k2")
+        d_vector(5, 0, 1, c_late)
+        d_quant(2)
+        wn_quant(tile_key(4))
+
+        pair_passes(6)
+        d_gpsimd(1, ring(4))
+        pair_out(6)
+        d_copy(4, d_turn(4, "d"))
+        d_stage(6, "k0")
+        d_vector(6, 0, 1, c_late)
+        d_vector(6, 1, 2, c_late)
         d_quant(4)
-        wn_quant(unit(5))
-        d_scale(nc.gpsimd, 11, staging(unit(5), 0))
-        for key in ((0, 0), (0, 1), (1, 0)):
-            back(key, (2,))
-        subtract(12)
-        subtract(13)
-        d_scale(nc.gpsimd, 12)
-        mx_teacher(14)
-        mx_teacher(15)
-        zs_out_of_psum(14)
-        zs_out_of_psum(15)
-        subtract(14)
-        zt_out_of_psum(15)
-        zt_out_of_psum(14)
-        d_scale(nc.vector, 13)
-        subtract(15)
-        back((1, 1), (0, 1, 2))
-        turned = d_turn(5, "s1")
+        wn_quant(tile_key(6))
+        wn_quant(tile_key(5))
+        turn_w(7)
+
+        pair_passes(7)
+        d_gpsimd(3, ring(5))
+        pair_out(7)
         d_copy(6, d_turn(6, "d"))
-        d_copy(5, turned)
-        d_scale(nc.vector, 14)
-        d_scale(nc.vector, 15)
+        d_stage(7, "k1")
+        d_vector(7, 0, 1, c_late)
+        d_vector(7, 1, 2, c_late)
+        d_vector(5, 1, 2, c_late)
+        back((0, 0), (0, 1, 2))
+        back((0, 1), (0, 1, 2))
+        d_copy(1, d_turn(1, "d"))
         d_quant(6)
-        d_quant(5)
-        back((2, 0), (0, 1))
-        back((2, 1), (0, 1))
-        d_copy(7, d_turn(7, "d"))
-        for key in ((0, 0), (0, 1), (1, 0), (1, 1)):
+        wn_quant(tile_key(7))
+        d_quant(1)
+        back((1, 0), (0, 1, 2))
+        back((1, 1), (0, 1, 2))
+        turned = [d_turn(7, "d"), d_turn(3, "t0"), d_turn(5, "t1")]
+        d_copy(7, turned[0])
+        d_copy(3, turned[1])
+        d_copy(5, turned[2])
+        d_quant(7)
+        for key in ((0, 0), (1, 0), (0, 1), (1, 1)):
             back(key, (3,))
         du_out_of_psum(0, 0)
-        d_quant(7)
-        for key in ((0, 1), (1, 0), (1, 1)):
-            du_out_of_psum(*key)
-        back((2, 0), (2,))
-        back((2, 1), (2,))
-        back((3, 0), (0,))
-        for key in ((2, 0), (2, 1)):
-            back(key, (3,))
-            du_out_of_psum(*key)
-        back((3, 0), (1, 2, 3))
+        d_quant(3)
+        du_out_of_psum(1, 0)
+        back((3, 0), (0, 3))
+        back((2, 0), (0, 3))
+        d_quant(5)
+        du_out_of_psum(0, 1)
+        du_out_of_psum(1, 1)
+        back((3, 0), (1, 2))
         du_out_of_psum(3, 0)
+        back((2, 0), (1, 2))
+        du_out_of_psum(2, 0)
+        back((2, 1), range(NG))
+        du_out_of_psum(2, 1)
         back((3, 1), range(NG))
         du_out_of_psum(3, 1)

@@ -23,11 +23,11 @@ MT = M // P
 KG = K // G
 NG = N // G
 PAIRS = NG * MT // 2
-H0 = 256
-H1 = 320
-H2 = 160
-GS = 352
-SA = 256
+H0 = 288
+H1 = 288
+H3 = 128
+H4 = 224
+VS = 208
 
 
 def tile_teacher_student_logits_s9_kernel(tc, u, gain, w, c, teacher_words, teacher_scales, zs_out, zt_out, du_out):
@@ -46,7 +46,7 @@ def tile_teacher_student_logits_s9_kernel(tc, u, gain, w, c, teacher_words, teac
 
         ident = kept("ident", [P, P], F32)
         gain_t = kept("gain_t", [P, KG, 4], BF16)
-        c_t = kept("c_t", [P, NG, 4], BF16)
+        c_t = kept("c_t", [P, N // P], BF16)
         gain_all = kept("gain_all", [P, K], BF16)
         c_sorted = kept("c_sorted", [P, N], BF16)
         t_parts = [(0, G), (G, N)]
@@ -54,13 +54,39 @@ def tile_teacher_student_logits_s9_kernel(tc, u, gain, w, c, teacher_words, teac
         t_scales = [kept("t_scales%d" % a, [P, KG, b - a], U8) for a, b in t_parts]
         u_sb = [kept("u%d" % m, [P, K], BF16) for m in range(MT)]
         w_raw = {(g, kg): kept("w%d%d" % (g, kg), [P, 4, G], BF16) for g in range(NG) for kg in range(KG)}
-        x_q = [operand("x%d" % m, KG * P) for m in range(MT)]
-        wk_q = {key: operand("wk%d%d" % key, G) for key in w_raw}
-        wn_q = {key: operand("wn%d%d" % key, G) for key in w_raw}
-        d_q = [operand("d%d" % i, 2 * P) for i in range(PAIRS)]
+        x_q, wk_q, wn_q, d_q = {}, {}, {}, {}
+        x_grp, wk_grp, wn_grp, d_grp = {}, {}, {}, {}
+        waiting = {}
 
-        def quantize(dst, src, fmt):
-            nc.vector.quantize_mx(out=dst[0][:].bitcast(fmt), scales=dst[1][:], in_=src[:])
+        def stage(tag, *members):
+            total = sum(m[3] for m in members)
+            name = "q%d" % len(waiting)
+            staged = keep.tile([P, total], BF16, name="staged", tag=tag, align_bytes=64)
+            codes, scales = operand(name, total // 4)
+            first = 0
+            for views, done, key, width in members:
+                views[key] = staged[:, first : first + width]
+                cols = slice(first // 4, (first + width) // 4)
+                done[key] = (codes[:, cols], scales[:, cols])
+                first += width
+            waiting[name] = (codes, scales, staged)
+            return name
+
+        def quantize(name, fmt=E4M3):
+            codes, scales, staged = waiting[name]
+            nc.vector.quantize_mx(out=codes[:].bitcast(fmt), scales=scales[:], in_=staged[:])
+
+        def xs(m):
+            return (x_grp, x_q, m, K)
+
+        def ks(n):
+            return (wk_grp, wk_q, divmod(n, KG), 4 * G)
+
+        def ns(n):
+            return (wn_grp, wn_q, divmod(n, KG), 4 * G)
+
+        def ds(i):
+            return (d_grp, d_q, i, 2 * G)
 
         def load_u(m):
             nc.sync.dma_start(out=u_sb[m][:], in_=u[m * P : (m + 1) * P, :])
@@ -92,21 +118,23 @@ def tile_teacher_student_logits_s9_kernel(tc, u, gain, w, c, teacher_words, teac
             nc.vector.memset(plane[:].rearrange("p g n -> p (g n)").bitcast(I32), 0)
         make_identity(nc, ident[:])
         nc.scalar.dma_start(out=gain_t[:], in_=gain.rearrange("(g p t) -> p g t", g=KG, t=4))
-        nc.scalar.dma_start(out=c_t[:], in_=c.rearrange("(g p e) -> p g e", g=NG, e=4))
+        nc.scalar.dma_start(out=c_t[:], in_=c.rearrange("(p i) -> p i", p=P))
         load_u(0)
         load_w(0)
         load_u(1)
-        load_words(0)
-        load_scales(nc.sync, 0)
-        load_u(2)
         load_w(1)
+        load_u(2)
         load_u(3)
         load_w(2)
+        load_scales(nc.sync, 0)
+        load_words(0)
         load_w(3)
+        load_w(4)
         load_scales(nc.sync, 1)
         load_words(1)
-        for n in range(4, 8):
-            load_w(n)
+        load_w(5)
+        load_w(6)
+        load_w(7)
         nc.sync.dma_start(out=gain_all[:], in_=gain.partition_broadcast(P))
 
         def spread(words, tag):
@@ -115,13 +143,14 @@ def tile_teacher_student_logits_s9_kernel(tc, u, gain, w, c, teacher_words, teac
                 nc.tensor.transpose(ps[:, j, :], words[:, j : j + 1].to_broadcast([P, P]), ident[:])
             return ps
 
-        def c_turn(h, tag):
-            return spread(c_t[:].rearrange("p g e -> p (g e)").bitcast(F32)[:, 4 * h : 4 * h + 4], tag)
+        def c_turn(half, tag):
+            return spread(c_t[:].bitcast(F32)[:, half::2], tag)
 
-        def c_copy(h, ps):
-            nc.scalar.copy(out=c_sorted[:].bitcast(F32)[:, G * h : G * (h + 1)], in_=ps[:].rearrange("q j p -> q (j p)"))
+        def c_copy(half, ps):
+            dst = c_sorted[:].bitcast(F32).rearrange("q (g u r j) -> q g u r j", g=NG, u=2, j=4)[:, :, half, :, :]
+            nc.scalar.copy(out=dst, in_=ps[:].rearrange("q j (g r) -> q g r j", g=NG))
 
-        x_ps, x_grp = {}, {}
+        x_ps = {}
 
         def x_turn(m, tag):
             x_ps[m] = psum.tile([P, KG * 2, P], F32, name="ps_x", tag=tag)
@@ -130,8 +159,7 @@ def tile_teacher_student_logits_s9_kernel(tc, u, gain, w, c, teacher_words, teac
                 for half in range(2):
                     nc.tensor.transpose(x_ps[m][:, 2 * kg + half, :], words[:, 256 * kg + half : 256 * (kg + 1) : 2], ident[:])
 
-        def x_scale(m, tag):
-            x_grp[m] = staging(tag)[:, 0:K]
+        def x_scale(m):
             for kg in range(KG):
                 turned = x_ps[m][:, 2 * kg : 2 * kg + 2, :].bitcast(BF16)
                 nc.vector.tensor_tensor(
@@ -140,17 +168,6 @@ def tile_teacher_student_logits_s9_kernel(tc, u, gain, w, c, teacher_words, teac
                     in1=gain_t[:, kg, :].rearrange("p (u e) -> p u e", e=2).unsqueeze(1).to_broadcast([P, P, 2, 2]),
                     op=MULT,
                 )
-
-        def x_quant(m):
-            quantize(x_q[m], x_grp[m], E4M3)
-
-        def staging(tag):
-            return keep.tile([P, 4 * G], BF16, name="staged", tag=tag, align_bytes=64)
-
-        wk_grp = {}
-
-        def wk_stage(key, tag):
-            wk_grp[key] = staging(tag)
 
         def wk_views(key, first, last):
             dst = wk_grp[key][:, 4 * first : 4 * last].rearrange("p (n i j) -> p n j i", j=4, i=4)
@@ -169,11 +186,6 @@ def tile_teacher_student_logits_s9_kernel(tc, u, gain, w, c, teacher_words, teac
             dst, src = [view.rearrange("p n j i -> p n i j") for view in wk_views(key, first, last)]
             nc.gpsimd.tensor_scalar(out=dst, in0=src, scalar1=1.0, scalar2=0.0, op0=MULT, op1=ADD)
 
-        def wk_quant(key):
-            quantize(wk_q[key], wk_grp[key], E4M3)
-
-        wn_grp = {}
-
         wn_ps = {}
 
         def wn_turn(key, h, bank):
@@ -183,19 +195,14 @@ def tile_teacher_student_logits_s9_kernel(tc, u, gain, w, c, teacher_words, teac
                 for half in range(2):
                     nc.tensor.transpose(wn_ps[key, h][:, 2 * j + half, :], words[:, half:256:2], ident[:])
 
-        def wn_copy(key, h, tag=None, move=nc.scalar.copy):
-            if h == 0:
-                wn_grp[key] = staging(tag)
+        def wn_copy(key, h, move=nc.scalar.copy):
             dst = wn_grp[key][:].bitcast(F32)[:, G * h : G * (h + 1)]
             move(
                 out=dst.rearrange("q (j p u) -> q j p u", j=2, u=2),
                 in_=wn_ps[key, h][:].rearrange("q (j u) p -> q j p u", u=2),
             )
 
-        def wn_quant(key):
-            quantize(wn_q[key], wn_grp[key], E4M3)
-
-        ps_s, ps_t, zs, diff, d_bf, d_grp = {}, {}, {}, {}, {}, {}
+        ps_s, ps_t, zs, diff, d_bf, d_half = {}, {}, {}, {}, {}, {}
 
         def logits(ps, m, codes, scales, groups):
             for kg in groups:
@@ -247,7 +254,7 @@ def tile_teacher_student_logits_s9_kernel(tc, u, gain, w, c, teacher_words, teac
         def subtract(b):
             i, h = divmod(b, 2)
             if h == 0:
-                diff[i] = keep.tile([P, 2, G], F32, name="diff", tag="diff%d" % (i if i % 2 else i % 4), align_bytes=64)
+                diff[i] = keep.tile([P, 2, G], F32, name="diff", tag="diff%d" % (i % 3), align_bytes=64)
             nc.vector.tensor_tensor(
                 out=diff[i][:, h, :].rearrange("m (u p e) -> m u p e", u=2, e=2),
                 in0=zs[b][:].rearrange("m (p u e) -> m u p e", u=2, e=2),
@@ -256,38 +263,43 @@ def tile_teacher_student_logits_s9_kernel(tc, u, gain, w, c, teacher_words, teac
             )
 
         def d_stage(i, tag):
-            d_bf[i] = staging(tag)
+            tile = keep.tile([P, 2 * G], BF16, name="d_bf", tag=tag, align_bytes=64)
+            d_bf[i] = tile
+            d_half[2 * i], d_half[2 * i + 1] = tile[:, 0:G], tile[:, G : 2 * G]
+
+        def d_stage_block(b, tag):
+            d_half[b] = keep.tile([P, G], BF16, name="d_bf", tag=tag, align_bytes=64)[:, 0:G]
 
         def d_scale(eng, i, first, last, factors):
             n = last - first
             out = d_bf[i][:, G * first : G * last].rearrange("m (h n) -> m h n", n=G)
             eng.tensor_tensor(out=out, in0=diff[i][:, first:last, :], in1=factors.unsqueeze(1).to_broadcast([P, n, G]), op=MULT)
 
+        def d_block(eng, b):
+            i, h = divmod(b, 2)
+            eng.tensor_tensor(out=d_half[b], in0=diff[i][:, h, :], in1=c_sorted[:, G * (i // 2) : G * (i // 2 + 1)], op=MULT)
+
         def d_gpsimd(i, tag):
             d_stage(i, tag)
             d_scale(nc.gpsimd, i, 0, 2, c_sorted[:, G * (i // 2) : G * (i // 2 + 1)])
 
-        def d_vector(i, first, last, c_late):
-            g = i // 2 - 2
-            d_scale(nc.vector, i, first, last, c_late[:].rearrange("q j p -> q (j p)").bitcast(BF16)[:, G * g : G * (g + 1)])
+        def d_vector(i, tag):
+            d_stage(i, tag)
+            d_scale(nc.vector, i, 0, 2, c_sorted[:, G * (i // 2) : G * (i // 2 + 1)])
 
         def d_turn(i, bank):
             ps = psum.tile([P, 4, P], F32, name="ps_d", tag=bank)
             for h in range(2):
-                words = d_bf[i][:, G * h : G * (h + 1)].bitcast(F32)
+                words = d_half[2 * i + h].bitcast(F32)
                 for half in range(2):
                     nc.tensor.transpose(ps[:, 2 * h + half, :], words[:, P * half : P * (half + 1)], ident[:])
             return ps
 
         def d_copy(i, ps, move=nc.scalar.copy):
-            d_grp[i] = work.tile([P, 2 * G], BF16, name="d_grp", bufs=4, align_bytes=64)
             move(
                 out=d_grp[i][:].bitcast(F32).rearrange("p (h m u) -> p h m u", h=2, u=2),
                 in_=ps[:].rearrange("p (h u) m -> p h m u", u=2),
             )
-
-        def d_quant(i):
-            quantize(d_q[i], d_grp[i], E5M2)
 
         dx, passes = {}, {}
 
@@ -310,7 +322,7 @@ def tile_teacher_student_logits_s9_kernel(tc, u, gain, w, c, teacher_words, teac
                 )
 
         def du_out_of_psum(m, kg):
-            du = work.tile([P, G], F32, name="du", bufs=8)
+            du = keep.tile([P, G], F32, name="du", tag="w%d%d" % (m, kg), align_bytes=64)
             nc.vector.tensor_tensor(
                 out=du[:].rearrange("m (p j) -> m p j", j=4),
                 in0=dx[m, kg][:].rearrange("m (j p) -> m p j", j=4),
@@ -320,63 +332,18 @@ def tile_teacher_student_logits_s9_kernel(tc, u, gain, w, c, teacher_words, teac
             nc.sync.dma_start(out=du_out[m * P : (m + 1) * P, G * kg : G * (kg + 1)], in_=du[:])
 
 
+        def du_by_gpsimd(m, kg, tag):
+            dx_sb = work.tile([P, G], F32, name="dx_sb")
+            nc.scalar.copy(out=dx_sb[:].rearrange("m (p j) -> m p j", j=4), in_=dx[m, kg][:].rearrange("m (j p) -> m p j", j=4))
+            du = keep.tile([P, G], F32, name="du_held", tag=tag, align_bytes=64)
+            nc.gpsimd.tensor_tensor(out=du[:], in0=dx_sb[:], in1=gain_all[:, G * kg : G * (kg + 1)], op=MULT)
+            return du
+
+        def du_store(m, kg, du):
+            nc.sync.dma_start(out=du_out[m * P : (m + 1) * P, G * kg : G * (kg + 1)], in_=du[:])
+
         def back(key, groups):
             mx_back(*key, groups, banks[key])
-
-        def ring(n):
-            return "ring%d" % (n % 4)
-
-        x_turn(0, "x")
-        c_ps = [c_turn(h, "w%d" % h) for h in range(2)]
-        x_turn(1, "d")
-        x_scale(0, ring(2))
-        wk_stage((0, 0), "k0")
-        wk_scalar((0, 0), H0, G)
-        wk_vector((0, 0), 0, H0)
-        c_copy(0, c_ps[0])
-        c_copy(1, c_ps[1])
-        x_quant(0)
-        mx_teacher(0)
-        x_scale(1, ring(3))
-        x_turn(2, "x")
-        wk_quant((0, 0))
-        mx_student(0, [0])
-        x_quant(1)
-        mx_teacher(1)
-        mx_student(1, [0])
-        wk_stage((0, 1), "k1")
-        wk_scalar((0, 1), H1, G)
-        wk_vector((0, 1), 0, H1)
-        x_scale(2, "k2")
-        x_turn(3, "d")
-        wn_turn((0, 0), 0, "w0")
-        wk_quant((0, 1))
-        mx_student(0, [1])
-        mx_student(1, [1])
-        x_quant(2)
-        wn_turn((0, 0), 1, "w1")
-        zt_out_of_psum(0)
-        zt_out_of_psum(1)
-        wk_stage(tile_key(2), "k2")
-        wk_gpsimd(tile_key(2), 0, H2)
-        wk_scalar(tile_key(2), H2, G)
-        wn_copy((0, 0), 0, ring(0))
-        wn_turn((0, 1), 0, "x")
-        x_scale(3, "k0")
-        x_quant(3)
-        wk_stage(tile_key(3), "k0")
-        wk_gpsimd(tile_key(3), 0, GS)
-        wn_copy((0, 0), 1)
-        wk_scalar(tile_key(3), GS, G)
-        zs_out_of_psum(0)
-        zs_out_of_psum(1)
-        subtract(0)
-        subtract(1)
-        wn_turn((0, 1), 1, "d")
-        wn_copy((0, 1), 0, ring(1))
-        wn_copy((0, 1), 1)
-        wk_quant(tile_key(2))
-        wk_quant(tile_key(3))
 
         def pair_passes(i):
             mx_student(2 * i)
@@ -396,92 +363,171 @@ def tile_teacher_student_logits_s9_kernel(tc, u, gain, w, c, teacher_words, teac
         def turn_w(n, move=nc.scalar.copy):
             for h in range(2):
                 wn_turn(tile_key(n), h, "w%d" % h)
-            wn_copy(tile_key(n), 0, ring(n), move)
+            wn_copy(tile_key(n), 0, move)
             wn_copy(tile_key(n), 1)
 
-        for i in range(1, 5):
-            key = tile_key(i + 3)
-            held = "k0" if i == 1 else ring(i - 2)
-            pair_passes(i)
-            if i % 2:
-                wk_stage(key, held)
-                wk_gpsimd(key, 0, GS)
-            else:
-                d_gpsimd(i - 2, held)
-            pair_out(i)
-            wk_scalar(key, GS if i % 2 else SA, G)
-            if i == 3:
-                d_copy(0, d_turn(0, "d"))
-            if i == 4:
-                c_late = c_turn(1, "x")
-            turn_w(i + 1, nc.scalar.copy if i % 2 else nc.vector.tensor_copy)
-            wk_quant(key)
-            if i == 4:
-                d_quant(0)
-            wn_quant(tile_key(i - 1))
-            if i % 2:
-                wk_stage(tile_key(i + 4), "k1")
-                wk_scalar(tile_key(i + 4), 0, SA)
+        def half_turn(j):
+            wn_turn(tile_key(j // 2), j % 2, "w%d" % (j % 2))
 
-        banks = {(0, 0): "w0", (0, 1): "w1", (1, 0): "s0", (1, 1): "s1", (2, 0): "t0", (2, 1): "t1", (3, 0): "x", (3, 1): "w0"}
-        pair_passes(5)
-        d_gpsimd(4, ring(3))
-        pair_out(5)
+        def half_copy(j):
+            wn_copy(tile_key(j // 2), j % 2)
+
+        banks = {(0, 0): "x", (0, 1): "w0", (1, 0): "w1", (1, 1): "s0", (2, 0): "s1", (2, 1): "t0", (3, 0): "t1", (3, 1): "d"}
+        x0, x1, k0, k1 = stage("b0", xs(0)), stage("b1", xs(1)), stage("b2", ks(0)), stage("b3", ks(1))
+        n = {0: stage("r0", ns(0)), 1: stage("r1", ns(1))}
+        x_turn(0, "x")
+        c_ps = [c_turn(h, "t%d" % h) for h in range(2)]
+        x_turn(1, "d")
+        x_scale(0)
+        wk_vector((0, 0), 0, H0)
+        wk_scalar((0, 0), H0, G)
+        c_copy(0, c_ps[0])
+        c_copy(1, c_ps[1])
+        quantize(x0)
+        half_turn(0)
+        half_turn(1)
+        x_scale(1)
+        quantize(k0)
+        wk_vector((0, 1), 0, H1)
+        wk_scalar((0, 1), H1, G)
+        half_copy(0)
+        half_copy(1)
+        k = {2: stage("k2", ks(2))}
+        wk_scalar(tile_key(2), 0, G)
+        quantize(x1)
+        x_turn(2, "x")
+        mx_student(0, [0])
+        mx_student(1, [0])
+        x_turn(3, "d")
+        quantize(k1)
+        mx_student(0, [1])
+        mx_student(1, [1])
+        x23 = stage("b0", xs(2), xs(3))
+        x_scale(2)
+        mx_teacher(0)
+        mx_teacher(1)
+        half_turn(2)
+        half_turn(3)
+        quantize(n[0])
+        k[3] = stage("r0", ks(3))
+        wk_gpsimd(tile_key(3), 0, H3)
+        wk_scalar(tile_key(3), H3, H4)
+        zt_out_of_psum(0)
+        zt_out_of_psum(1)
+        half_copy(2)
+        half_copy(3)
+        x_scale(3)
+        zs_out_of_psum(0)
+        zs_out_of_psum(1)
+        quantize(x23)
+        wk_scalar(tile_key(3), H4, G)
+        subtract(0)
+        subtract(1)
+        quantize(k[2])
+        def first_passes(i):
+            a, b = 2 * i, 2 * i + 1
+            mx_student(a, [0])
+            mx_student(b, [0])
+            mx_teacher(a)
+            mx_teacher(b)
+            mx_student(a, [1])
+            mx_student(b, [1])
+
+        def next_tile(t, tag):
+            k[t] = stage(tag, ks(t))
+            wk_scalar(tile_key(t), VS, G)
+            wk_vector(tile_key(t), 0, VS)
+
+        pair_passes(1)
+        d_gpsimd(0, "k2")
+        pair_out(1)
+        n23 = stage("n23", ns(2), ns(3))
+        turn_w(2)
+        quantize(k[3])
+        next_tile(4, "b1")
+        quantize(n[1])
+
+        first_passes(2)
+        d_gpsimd(1, "r1")
+        pair_out(2)
+        d0 = stage("b3", ds(0))
+        d_copy(0, d_turn(0, "d"))
+        turn_w(3)
+        next_tile(5, "b2")
+        quantize(k[4])
+
+        pair_passes(3)
+        d_gpsimd(2, "b1")
+        pair_out(3)
+        d12 = stage("b0", ds(1), ds(2))
+        d_copy(1, d_turn(1, "d"))
+        n46 = stage("n46", ns(4), ns(6))
+        turn_w(4)
+        quantize(k[5])
+        next_tile(6, "r0")
+        quantize(d0, E5M2)
+
+        first_passes(4)
+        d_gpsimd(3, "b3")
+        pair_out(4)
         d_copy(2, d_turn(2, "d"))
-        turn_w(6)
-        d_stage(5, "k2")
-        d_vector(5, 0, 1, c_late)
-        d_quant(2)
-        wn_quant(tile_key(4))
+        n57 = stage("n57", ns(5), ns(7))
+        turn_w(5)
+        next_tile(7, "b2")
+        quantize(k[6])
 
-        pair_passes(6)
-        d_gpsimd(1, ring(4))
+        pair_passes(5)
+        back((0, 0), (0,))
+        d_gpsimd(4, "r0")
+        pair_out(5)
+        d34 = stage("k2", ds(3), ds(4))
+        d_copy(3, d_turn(3, "d"))
+        turn_w(6)
+        quantize(k[7])
+        quantize(n23)
+
+        first_passes(6)
+        d_gpsimd(5, "n23")
         pair_out(6)
         d_copy(4, d_turn(4, "d"))
-        d_stage(6, "k0")
-        d_vector(6, 0, 1, c_late)
-        d_vector(6, 1, 2, c_late)
-        d_quant(4)
-        wn_quant(tile_key(6))
-        wn_quant(tile_key(5))
         turn_w(7)
+        quantize(d12, E5M2)
 
         pair_passes(7)
-        d_gpsimd(3, ring(5))
+        d_gpsimd(6, "b0")
         pair_out(7)
+        d5, d6, d7 = stage("b3", ds(5)), stage("r1", ds(6)), stage("r0", ds(7))
+        d_copy(5, d_turn(5, "d"))
+        back((0, 0), (1,))
+        back((0, 1), (0, 1))
+        back((1, 0), (0, 1))
+        quantize(d34, E5M2)
+        d_vector(7, "b1")
+        quantize(n46)
+        back((1, 1), (0, 1))
+        back((2, 0), (0,))
         d_copy(6, d_turn(6, "d"))
-        d_stage(7, "k1")
-        d_vector(7, 0, 1, c_late)
-        d_vector(7, 1, 2, c_late)
-        d_vector(5, 1, 2, c_late)
-        back((0, 0), (0, 1, 2))
-        back((0, 1), (0, 1, 2))
-        d_copy(1, d_turn(1, "d"))
-        d_quant(6)
-        wn_quant(tile_key(7))
-        d_quant(1)
-        back((1, 0), (0, 1, 2))
-        back((1, 1), (0, 1, 2))
-        turned = [d_turn(7, "d"), d_turn(3, "t0"), d_turn(5, "t1")]
-        d_copy(7, turned[0])
-        d_copy(3, turned[1])
-        d_copy(5, turned[2])
-        d_quant(7)
-        for key in ((0, 0), (1, 0), (0, 1), (1, 1)):
-            back(key, (3,))
+        back((2, 1), (0,))
+        back((3, 0), (0,))
+        for key in ((2, 0), (2, 1), (3, 0)):
+            back(key, (1,))
+        d_copy(7, d_turn(7, "d"))
+        quantize(d6, E5M2)
+        quantize(n57)
+        quantize(d5, E5M2)
+        quantize(d7, E5M2)
+        back((0, 0), (2, 3))
+        back((1, 0), (2, 3))
+        back((0, 1), (2, 3))
+        back((1, 1), (2, 3))
         du_out_of_psum(0, 0)
-        d_quant(3)
+        late = du_by_gpsimd(0, 1, "r0")
         du_out_of_psum(1, 0)
-        back((3, 0), (0, 3))
-        back((2, 0), (0, 3))
-        d_quant(5)
-        du_out_of_psum(0, 1)
         du_out_of_psum(1, 1)
-        back((3, 0), (1, 2))
-        du_out_of_psum(3, 0)
-        back((2, 0), (1, 2))
+        back((2, 0), (2, 3))
         du_out_of_psum(2, 0)
-        back((2, 1), range(NG))
-        du_out_of_psum(2, 1)
-        back((3, 1), range(NG))
-        du_out_of_psum(3, 1)
+        du_store(0, 1, late)
+        back((3, 1), (0, 1))
+        for key in ((2, 1), (3, 0), (3, 1)):
+            back(key, (2, 3))
+            du_out_of_psum(*key)

@@ -439,13 +439,13 @@ def tile_teacher_student_logits_s9_kernel(tc, u, gain, w, c, teacher_words, teac
             wk_vector(tile_key(t), 0, VS)
 
         pair_passes(1)
-        d_gpsimd(0, "k2")
+        d_gpsimd(0, "dbf0")
         pair_out(1)
         n23 = stage("n23", ns(2), ns(3))
         turn_w(2)
         quantize(k[3])
-        next_tile(4, "b1")
         quantize(n[1])
+        next_tile(4, "b1")
 
         first_passes(2)
         d_gpsimd(1, "r1")
@@ -453,8 +453,8 @@ def tile_teacher_student_logits_s9_kernel(tc, u, gain, w, c, teacher_words, teac
         d0 = stage("b3", ds(0))
         d_copy(0, d_turn(0, "d"))
         turn_w(3)
-        next_tile(5, "b2")
         quantize(k[4])
+        next_tile(5, "b2")
 
         pair_passes(3)
         d_gpsimd(2, "b1")
@@ -464,8 +464,8 @@ def tile_teacher_student_logits_s9_kernel(tc, u, gain, w, c, teacher_words, teac
         n46 = stage("n46", ns(4), ns(6))
         turn_w(4)
         quantize(k[5])
-        next_tile(6, "r0")
         quantize(d0, E5M2)
+        next_tile(6, "r0")
 
         first_passes(4)
         d_gpsimd(3, "b3")
@@ -473,25 +473,27 @@ def tile_teacher_student_logits_s9_kernel(tc, u, gain, w, c, teacher_words, teac
         d_copy(2, d_turn(2, "d"))
         n57 = stage("n57", ns(5), ns(7))
         turn_w(5)
-        next_tile(7, "b2")
         quantize(k[6])
+        next_tile(7, "b2")
 
         pair_passes(5)
         back((0, 0), (0,))
         d_gpsimd(4, "r0")
         pair_out(5)
-        d34 = stage("k2", ds(3), ds(4))
+        d3 = stage("k2", ds(3))
         d_copy(3, d_turn(3, "d"))
         turn_w(6)
         quantize(k[7])
         quantize(n23)
 
         first_passes(6)
-        d_gpsimd(5, "n23")
+        d_gpsimd(5, "b2")
         pair_out(6)
+        d4 = stage("dbf0", ds(4))
         d_copy(4, d_turn(4, "d"))
         turn_w(7)
         quantize(d12, E5M2)
+        quantize(d3, E5M2)
 
         pair_passes(7)
         d_gpsimd(6, "b0")
@@ -501,7 +503,7 @@ def tile_teacher_student_logits_s9_kernel(tc, u, gain, w, c, teacher_words, teac
         back((0, 0), (1,))
         back((0, 1), (0, 1))
         back((1, 0), (0, 1))
-        quantize(d34, E5M2)
+        quantize(d4, E5M2)
         d_vector(7, "b1")
         quantize(n46)
         back((1, 1), (0, 1))

@@ -23,11 +23,14 @@ MT = M // P
 KG = K // G
 NG = N // G
 PAIRS = NG * MT // 2
-H0 = 288
-H1 = 288
-H3 = 128
-H4 = 224
-VS = 208
+H0 = 256
+H1 = 224
+H2 = 128
+H3 = 288
+H4 = 400
+A4 = 384
+V4 = 160
+VS = 224
 
 
 def tile_teacher_student_logits_s9_kernel(tc, u, gain, w, c, teacher_words, teacher_scales, zs_out, zt_out, du_out):
@@ -382,7 +385,6 @@ def tile_teacher_student_logits_s9_kernel(tc, u, gain, w, c, teacher_words, teac
         wk_vector((0, 0), 0, H0)
         wk_scalar((0, 0), H0, G)
         c_copy(0, c_ps[0])
-        c_copy(1, c_ps[1])
         quantize(x0)
         half_turn(0)
         half_turn(1)
@@ -390,25 +392,29 @@ def tile_teacher_student_logits_s9_kernel(tc, u, gain, w, c, teacher_words, teac
         quantize(k0)
         wk_vector((0, 1), 0, H1)
         wk_scalar((0, 1), H1, G)
+        c_copy(1, c_ps[1])
         half_copy(0)
         half_copy(1)
-        k = {2: stage("k2", ks(2))}
-        wk_scalar(tile_key(2), 0, G)
         quantize(x1)
+        k = {2: stage("b1", ks(2))}
+        wk_gpsimd(tile_key(2), 0, H2)
+        wk_scalar(tile_key(2), H2, G)
         x_turn(2, "x")
+        x_turn(3, "d")
         mx_student(0, [0])
         mx_student(1, [0])
-        x_turn(3, "d")
         quantize(k1)
         mx_student(0, [1])
         mx_student(1, [1])
         x23 = stage("b0", xs(2), xs(3))
         x_scale(2)
+        x_scale(3)
         mx_teacher(0)
         mx_teacher(1)
         half_turn(2)
         half_turn(3)
         quantize(n[0])
+        quantize(x23)
         k[3] = stage("r0", ks(3))
         wk_gpsimd(tile_key(3), 0, H3)
         wk_scalar(tile_key(3), H3, H4)
@@ -416,11 +422,11 @@ def tile_teacher_student_logits_s9_kernel(tc, u, gain, w, c, teacher_words, teac
         zt_out_of_psum(1)
         half_copy(2)
         half_copy(3)
-        x_scale(3)
+        wk_scalar(tile_key(3), H4, G)
+        k[4] = stage("k2", ks(4))
+        wk_scalar(tile_key(4), A4, G)
         zs_out_of_psum(0)
         zs_out_of_psum(1)
-        quantize(x23)
-        wk_scalar(tile_key(3), H4, G)
         subtract(0)
         subtract(1)
         quantize(k[2])
@@ -445,7 +451,8 @@ def tile_teacher_student_logits_s9_kernel(tc, u, gain, w, c, teacher_words, teac
         turn_w(2)
         quantize(k[3])
         quantize(n[1])
-        next_tile(4, "b1")
+        wk_scalar(tile_key(4), V4, A4)
+        wk_vector(tile_key(4), 0, V4)
 
         first_passes(2)
         d_gpsimd(1, "r1")
@@ -457,7 +464,7 @@ def tile_teacher_student_logits_s9_kernel(tc, u, gain, w, c, teacher_words, teac
         next_tile(5, "b2")
 
         pair_passes(3)
-        d_gpsimd(2, "b1")
+        d_gpsimd(2, "k2")
         pair_out(3)
         d12 = stage("b0", ds(1), ds(2))
         d_copy(1, d_turn(1, "d"))
@@ -480,7 +487,7 @@ def tile_teacher_student_logits_s9_kernel(tc, u, gain, w, c, teacher_words, teac
         back((0, 0), (0,))
         d_gpsimd(4, "r0")
         pair_out(5)
-        d3 = stage("k2", ds(3))
+        d3 = stage("b1", ds(3))
         d_copy(3, d_turn(3, "d"))
         turn_w(6)
         quantize(k[7])
@@ -504,7 +511,7 @@ def tile_teacher_student_logits_s9_kernel(tc, u, gain, w, c, teacher_words, teac
         back((0, 1), (0, 1))
         back((1, 0), (0, 1))
         quantize(d4, E5M2)
-        d_vector(7, "b1")
+        d_vector(7, "k2")
         quantize(n46)
         back((1, 1), (0, 1))
         back((2, 0), (0,))

@@ -173,8 +173,8 @@ def tile_teacher_student_logits_s9_kernel(tc, u, gain, w, c, teacher_words, teac
                 )
 
         def wk_views(key, first, last):
-            dst = wk_grp[key][:, 4 * first : 4 * last].rearrange("p (n i j) -> p n j i", j=4, i=4)
-            src = w_raw[key][:, :, first:last].rearrange("p j (n i) -> p n j i", i=4)
+            dst = wk_grp[key][:, 4 * first : 4 * last].rearrange("p (n i j) -> p n j i", j=4, i=2)
+            src = w_raw[key][:, :, first:last].rearrange("p j (n i) -> p n j i", i=2)
             return dst, src
 
         def wk_vector(key, first, last):

@@ -28,8 +28,8 @@ H1 = 224
 H2 = 128
 H3 = 288
 H4 = 400
-A4 = 384
-V4 = 160
+A4 = 448
+V4 = 128
 VS = 224
 
 

from contextlib import ExitStack

import concourse.mybir as mybir
from concourse.masks import make_identity

M, K, N = 512, 1024, 2048
FLOPS = 3 * 2 * M * K * N
F32 = mybir.dt.float32
BF16 = mybir.dt.bfloat16
U32 = mybir.dt.uint32
I32 = mybir.dt.int32
U8 = mybir.dt.uint8
E4M3 = mybir.dt.float8_e4m3fn_x4
E5M2 = mybir.dt.float8_e5m2_x4
E2M1 = mybir.dt.float4_e2m1fn_x4
MULT = mybir.AluOpType.mult
ADD = mybir.AluOpType.add
SUB = mybir.AluOpType.subtract

P = 128
G = 512
MT = M // P
KG = K // G
NG = N // G
PAIRS = NG * MT // 2
H0 = 256
H1 = 224
H2 = 128
H3 = 288
H4 = 400
A4 = 448
V4 = 128
VS = 224


def tile_teacher_student_logits_s9_kernel(tc, u, gain, w, c, teacher_words, teacher_scales, zs_out, zt_out, du_out):
    nc = tc.nc
    with ExitStack() as ctx:
        keep = ctx.enter_context(tc.tile_pool(name="keep", bufs=1))
        work = ctx.enter_context(tc.tile_pool(name="work", bufs=2))
        psum = ctx.enter_context(tc.psum_pool(name="psum", bufs=1))
        ctx.enter_context(tc.manual_schedule())

        def kept(name, shape, dtype):
            return keep.tile(shape, dtype, name=name, align_bytes=64)

        def operand(name, width):
            return kept(name + "_codes", [P, width], U32), kept(name + "_scales", [P, width], U8)

        ident = kept("ident", [P, P], F32)
        gain_t = kept("gain_t", [P, KG, 4], BF16)
        c_t = kept("c_t", [P, N // P], BF16)
        gain_all = kept("gain_all", [P, K], BF16)
        c_sorted = kept("c_sorted", [P, N], BF16)
        t_parts = [(0, G), (G, N)]
        t_words = [kept("t_words%d" % a, [P, KG, 2 * (b - a)], U8) for a, b in t_parts]
        t_scales = [kept("t_scales%d" % a, [P, KG, b - a], U8) for a, b in t_parts]
        u_sb = [kept("u%d" % m, [P, K], BF16) for m in range(MT)]
        w_raw = {(g, kg): kept("w%d%d" % (g, kg), [P, 4, G], BF16) for g in range(NG) for kg in range(KG)}
        x_q, wk_q, wn_q, d_q = {}, {}, {}, {}
        x_grp, wk_grp, wn_grp, d_grp = {}, {}, {}, {}
        waiting = {}

        def stage(tag, *members):
            total = sum(m[3] for m in members)
            name = "q%d" % len(waiting)
            staged = keep.tile([P, total], BF16, name="staged", tag=tag, align_bytes=64)
            codes, scales = operand(name, total // 4)
            first = 0
            for views, done, key, width in members:
                views[key] = staged[:, first : first + width]
                cols = slice(first // 4, (first + width) // 4)
                done[key] = (codes[:, cols], scales[:, cols])
                first += width
            waiting[name] = (codes, scales, staged)
            return name

        def quantize(name, fmt=E4M3):
            codes, scales, staged = waiting[name]
            nc.vector.quantize_mx(out=codes[:].bitcast(fmt), scales=scales[:], in_=staged[:])

        def xs(m):
            return (x_grp, x_q, m, K)

        def ks(n):
            return (wk_grp, wk_q, divmod(n, KG), 4 * G)

        def ns(n):
            return (wn_grp, wn_q, divmod(n, KG), 4 * G)

        def ds(i):
            return (d_grp, d_q, i, 2 * G)

        def load_u(m):
            nc.sync.dma_start(out=u_sb[m][:], in_=u[m * P : (m + 1) * P, :])

        def load_w(n):
            g, kg = tile_key(n)
            nc.sync.dma_start(
                out=w_raw[g, kg][:],
                in_=w[G * kg : G * (kg + 1), G * g : G * (g + 1)].rearrange("(p j) n -> p j n", j=4),
            )

        def load_scales(queue, part):
            first, last = t_parts[part]
            for q in range(4):
                queue.dma_start(
                    out=t_scales[part][32 * q : 32 * q + 4, :, :].bitcast(I32),
                    in_=teacher_scales[:, 4 * q : 4 * q + 4, first:last].rearrange("g r n -> r g n").bitcast(I32),
                )

        def load_words(part):
            first, last = t_parts[part]
            words = teacher_words.rearrange("g p n -> p g n")[:, :, 2 * first : 2 * last]
            nc.sync.dma_start(out=t_words[part][:].bitcast(I32), in_=words.bitcast(I32))

        def tile_key(n):
            return divmod(n, KG)

        for plane in t_scales:
            nc.vector.memset(plane[:].rearrange("p g n -> p (g n)").bitcast(I32), 0)
        make_identity(nc, ident[:])
        nc.scalar.dma_start(out=gain_t[:], in_=gain.rearrange("(g p t) -> p g t", g=KG, t=4))
        nc.scalar.dma_start(out=c_t[:], in_=c.rearrange("(p i) -> p i", p=P))
        load_u(0)
        load_w(0)
        load_u(1)
        load_w(1)
        load_u(2)
        load_u(3)
        load_w(2)
        load_scales(nc.sync, 0)
        load_words(0)
        load_w(3)
        load_w(4)
        load_scales(nc.sync, 1)
        load_words(1)
        load_w(5)
        load_w(6)
        load_w(7)
        nc.sync.dma_start(out=gain_all[:], in_=gain.partition_broadcast(P))

        def spread(words, tag):
            ps = psum.tile([P, 4, P], F32, name="ps_spread", tag=tag)
            for j in range(4):
                nc.tensor.transpose(ps[:, j, :], words[:, j : j + 1].to_broadcast([P, P]), ident[:])
            return ps

        def c_turn(half, tag):
            return spread(c_t[:].bitcast(F32)[:, half::2], tag)

        def c_copy(half, ps):
            dst = c_sorted[:].bitcast(F32).rearrange("q (g u r j) -> q g u r j", g=NG, u=2, j=4)[:, :, half, :, :]
            nc.scalar.copy(out=dst, in_=ps[:].rearrange("q j (g r) -> q g r j", g=NG))

        x_ps = {}

        def x_turn(m, tag):
            x_ps[m] = psum.tile([P, KG * 2, P], F32, name="ps_x", tag=tag)
            words = u_sb[m][:].bitcast(F32)
            for kg in range(KG):
                for half in range(2):
                    nc.tensor.transpose(x_ps[m][:, 2 * kg + half, :], words[:, 256 * kg + half : 256 * (kg + 1) : 2], ident[:])

        def x_scale(m):
            for kg in range(KG):
                turned = x_ps[m][:, 2 * kg : 2 * kg + 2, :].bitcast(BF16)
                nc.vector.tensor_tensor(
                    out=x_grp[m][:, G * kg : G * (kg + 1)].rearrange("p (m u e) -> p m u e", u=2, e=2),
                    in0=turned.rearrange("p u (m e) -> p m u e", e=2),
                    in1=gain_t[:, kg, :].rearrange("p (u e) -> p u e", e=2).unsqueeze(1).to_broadcast([P, P, 2, 2]),
                    op=MULT,
                )

        def wk_views(key, first, last):
            dst = wk_grp[key][:, 4 * first : 4 * last].rearrange("p (n i j) -> p n j i", j=4, i=2)
            src = w_raw[key][:, :, first:last].rearrange("p j (n i) -> p n j i", i=2)
            return dst, src

        def wk_vector(key, first, last):
            dst, src = wk_views(key, first, last)
            nc.vector.tensor_copy(out=dst, in_=src)

        def wk_scalar(key, first, last):
            dst, src = wk_views(key, first, last)
            nc.scalar.copy(out=dst, in_=src)

        def wk_gpsimd(key, first, last):
            dst, src = [view.rearrange("p n j i -> p n i j") for view in wk_views(key, first, last)]
            nc.gpsimd.tensor_scalar(out=dst, in0=src, scalar1=1.0, scalar2=0.0, op0=MULT, op1=ADD)

        wn_ps = {}

        def wn_turn(key, h, bank):
            wn_ps[key, h] = psum.tile([P, 4, P], F32, name="ps_w", tag=bank)
            for j in range(2):
                words = w_raw[key][:, 2 * h + j, :].bitcast(F32)
                for half in range(2):
                    nc.tensor.transpose(wn_ps[key, h][:, 2 * j + half, :], words[:, half:256:2], ident[:])

        def wn_copy(key, h, move=nc.scalar.copy):
            dst = wn_grp[key][:].bitcast(F32)[:, G * h : G * (h + 1)]
            move(
                out=dst.rearrange("q (j p u) -> q j p u", j=2, u=2),
                in_=wn_ps[key, h][:].rearrange("q (j u) p -> q j p u", u=2),
            )

        ps_s, ps_t, zs, diff, d_bf, d_half = {}, {}, {}, {}, {}, {}

        def logits(ps, m, codes, scales, groups):
            for kg in groups:
                nc.tensor.matmul_mx(
                    out=ps[:],
                    lhsT=x_q[m][0][:, kg * P : (kg + 1) * P].bitcast(E4M3),
                    lhsT_scale=x_q[m][1][:, kg * P : (kg + 1) * P],
                    rhs=codes(kg),
                    rhs_scale=scales(kg),
                    start=(kg == 0),
                    stop=(kg == KG - 1),
                )

        def mx_student(b, groups=range(KG)):
            g, m = divmod(b, MT)
            if b not in ps_s:
                ps_s[b] = psum.tile([P, G], F32, name="ps_s", tag="s%d" % (b % 2))
            logits(ps_s[b], m, lambda kg: wk_q[g, kg][0][:].bitcast(E4M3), lambda kg: wk_q[g, kg][1][:], groups)

        def mx_teacher(b):
            g, m = divmod(b, MT)
            ps_t[b] = psum.tile([P, G], F32, name="ps_t", tag="t%d" % (b % 2))
            part = min(g, 1)
            first = G * (g - part)
            words = t_words[part][:, :, 2 * first : 2 * (first + G)]
            scales = t_scales[part][:, :, first : first + G]
            logits(ps_t[b], m, lambda kg: words[:, kg, :].bitcast(E2M1), lambda kg: scales[:, kg, :], range(KG))

        def out_block(out, b):
            g, m = divmod(b, MT)
            return out[m * P : (m + 1) * P, G * g : G * (g + 1)]

        def zs_out_of_psum(b):
            g = b // MT
            zs[b] = work.tile([P, G], F32, name="zs", bufs=8)
            nc.vector.tensor_tensor(
                out=zs[b][:].rearrange("m (p u e) -> m p u e", u=2, e=2),
                in0=ps_s[b][:].rearrange("m (p u e) -> m p u e", u=2, e=2),
                in1=c_sorted[:, G * g : G * (g + 1)].rearrange("m (u p e) -> m p u e", u=2, e=2),
                op=MULT,
            )
            nc.sync.dma_start(out=out_block(zs_out, b), in_=zs[b][:])

        def zt_out_of_psum(b):
            zt = work.tile([P, G], F32, name="zt", bufs=8)
            nc.scalar.copy(out=zt[:], in_=ps_t[b][:])
            nc.sync.dma_start(out=out_block(zt_out, b), in_=zt[:])

        def subtract(b):
            i, h = divmod(b, 2)
            if h == 0:
                diff[i] = keep.tile([P, 2, G], F32, name="diff", tag="diff%d" % (i % 3), align_bytes=64)
            nc.vector.tensor_tensor(
                out=diff[i][:, h, :].rearrange("m (u p e) -> m u p e", u=2, e=2),
                in0=zs[b][:].rearrange("m (p u e) -> m u p e", u=2, e=2),
                in1=ps_t[b][:].rearrange("m (p u e) -> m u p e", u=2, e=2),
                op=SUB,
            )

        def d_stage(i, tag):
            tile = keep.tile([P, 2 * G], BF16, name="d_bf", tag=tag, align_bytes=64)
            d_bf[i] = tile
            d_half[2 * i], d_half[2 * i + 1] = tile[:, 0:G], tile[:, G : 2 * G]

        def d_stage_block(b, tag):
            d_half[b] = keep.tile([P, G], BF16, name="d_bf", tag=tag, align_bytes=64)[:, 0:G]

        def d_scale(eng, i, first, last, factors):
            n = last - first
            out = d_bf[i][:, G * first : G * last].rearrange("m (h n) -> m h n", n=G)
            eng.tensor_tensor(out=out, in0=diff[i][:, first:last, :], in1=factors.unsqueeze(1).to_broadcast([P, n, G]), op=MULT)

        def d_block(eng, b):
            i, h = divmod(b, 2)
            eng.tensor_tensor(out=d_half[b], in0=diff[i][:, h, :], in1=c_sorted[:, G * (i // 2) : G * (i // 2 + 1)], op=MULT)

        def d_gpsimd(i, tag):
            d_stage(i, tag)
            d_scale(nc.gpsimd, i, 0, 2, c_sorted[:, G * (i // 2) : G * (i // 2 + 1)])

        def d_vector(i, tag):
            d_stage(i, tag)
            d_scale(nc.vector, i, 0, 2, c_sorted[:, G * (i // 2) : G * (i // 2 + 1)])

        def d_turn(i, bank):
            ps = psum.tile([P, 4, P], F32, name="ps_d", tag=bank)
            for h in range(2):
                words = d_half[2 * i + h].bitcast(F32)
                for half in range(2):
                    nc.tensor.transpose(ps[:, 2 * h + half, :], words[:, P * half : P * (half + 1)], ident[:])
            return ps

        def d_copy(i, ps, move=nc.scalar.copy):
            move(
                out=d_grp[i][:].bitcast(F32).rearrange("p (h m u) -> p h m u", h=2, u=2),
                in_=ps[:].rearrange("p (h u) m -> p h m u", u=2),
            )

        dx, passes = {}, {}

        def mx_back(m, kg, groups, tag):
            if (m, kg) not in dx:
                dx[m, kg] = psum.tile([P, G], F32, name="ps_dx", tag=tag)
                passes[m, kg] = 0
            for g in groups:
                passes[m, kg] += 1
                codes, scales = d_q[2 * g + m // 2]
                cols = slice(P * (m % 2), P * (m % 2 + 1))
                nc.tensor.matmul_mx(
                    out=dx[m, kg][:],
                    lhsT=codes[:, cols].bitcast(E5M2),
                    lhsT_scale=scales[:, cols],
                    rhs=wn_q[g, kg][0][:].bitcast(E4M3),
                    rhs_scale=wn_q[g, kg][1][:],
                    start=(passes[m, kg] == 1),
                    stop=(passes[m, kg] == NG),
                )

        def du_out_of_psum(m, kg):
            du = keep.tile([P, G], F32, name="du", tag="w%d%d" % (m, kg), align_bytes=64)
            nc.vector.tensor_tensor(
                out=du[:].rearrange("m (p j) -> m p j", j=4),
                in0=dx[m, kg][:].rearrange("m (j p) -> m p j", j=4),
                in1=gain_all[:, G * kg : G * (kg + 1)].rearrange("m (p j) -> m p j", j=4),
                op=MULT,
            )
            nc.sync.dma_start(out=du_out[m * P : (m + 1) * P, G * kg : G * (kg + 1)], in_=du[:])


        def du_by_gpsimd(m, kg, tag):
            dx_sb = work.tile([P, G], F32, name="dx_sb")
            nc.scalar.copy(out=dx_sb[:].rearrange("m (p j) -> m p j", j=4), in_=dx[m, kg][:].rearrange("m (j p) -> m p j", j=4))
            du = keep.tile([P, G], F32, name="du_held", tag=tag, align_bytes=64)
            nc.gpsimd.tensor_tensor(out=du[:], in0=dx_sb[:], in1=gain_all[:, G * kg : G * (kg + 1)], op=MULT)
            return du

        def du_store(m, kg, du):
            nc.sync.dma_start(out=du_out[m * P : (m + 1) * P, G * kg : G * (kg + 1)], in_=du[:])

        def back(key, groups):
            mx_back(*key, groups, banks[key])

        def pair_passes(i):
            mx_student(2 * i)
            mx_student(2 * i + 1)
            mx_teacher(2 * i)
            mx_teacher(2 * i + 1)

        def pair_out(i):
            a, b = 2 * i, 2 * i + 1
            zt_out_of_psum(a)
            zt_out_of_psum(b)
            zs_out_of_psum(a)
            zs_out_of_psum(b)
            subtract(a)
            subtract(b)

        def turn_w(n, move=nc.scalar.copy):
            for h in range(2):
                wn_turn(tile_key(n), h, "w%d" % h)
            wn_copy(tile_key(n), 0, move)
            wn_copy(tile_key(n), 1)

        def half_turn(j):
            wn_turn(tile_key(j // 2), j % 2, "w%d" % (j % 2))

        def half_copy(j):
            wn_copy(tile_key(j // 2), j % 2)

        banks = {(0, 0): "x", (0, 1): "w0", (1, 0): "w1", (1, 1): "s0", (2, 0): "s1", (2, 1): "t0", (3, 0): "t1", (3, 1): "d"}
        x0, x1, k0, k1 = stage("b0", xs(0)), stage("b1", xs(1)), stage("b2", ks(0)), stage("b3", ks(1))
        n = {0: stage("r0", ns(0)), 1: stage("r1", ns(1))}
        x_turn(0, "x")
        c_ps = [c_turn(h, "t%d" % h) for h in range(2)]
        x_turn(1, "d")
        x_scale(0)
        wk_vector((0, 0), 0, H0)
        wk_scalar((0, 0), H0, G)
        c_copy(0, c_ps[0])
        quantize(x0)
        half_turn(0)
        half_turn(1)
        x_scale(1)
        quantize(k0)
        wk_vector((0, 1), 0, H1)
        wk_scalar((0, 1), H1, G)
        c_copy(1, c_ps[1])
        half_copy(0)
        half_copy(1)
        quantize(x1)
        k = {2: stage("b1", ks(2))}
        wk_gpsimd(tile_key(2), 0, H2)
        wk_scalar(tile_key(2), H2, G)
        x_turn(2, "x")
        x_turn(3, "d")
        mx_student(0, [0])
        mx_student(1, [0])
        quantize(k1)
        mx_student(0, [1])
        mx_student(1, [1])
        x23 = stage("b0", xs(2), xs(3))
        x_scale(2)
        x_scale(3)
        mx_teacher(0)
        mx_teacher(1)
        half_turn(2)
        half_turn(3)
        quantize(n[0])
        quantize(x23)
        k[3] = stage("r0", ks(3))
        wk_gpsimd(tile_key(3), 0, H3)
        wk_scalar(tile_key(3), H3, H4)
        zt_out_of_psum(0)
        zt_out_of_psum(1)
        half_copy(2)
        half_copy(3)
        wk_scalar(tile_key(3), H4, G)
        k[4] = stage("k2", ks(4))
        wk_scalar(tile_key(4), A4, G)
        zs_out_of_psum(0)
        zs_out_of_psum(1)
        subtract(0)
        subtract(1)
        quantize(k[2])
        def first_passes(i):
            a, b = 2 * i, 2 * i + 1
            mx_student(a, [0])
            mx_student(b, [0])
            mx_teacher(a)
            mx_teacher(b)
            mx_student(a, [1])
            mx_student(b, [1])

        def next_tile(t, tag):
            k[t] = stage(tag, ks(t))
            wk_scalar(tile_key(t), VS, G)
            wk_vector(tile_key(t), 0, VS)

        pair_passes(1)
        d_gpsimd(0, "dbf0")
        pair_out(1)
        n23 = stage("n23", ns(2), ns(3))
        turn_w(2)
        quantize(k[3])
        quantize(n[1])
        wk_scalar(tile_key(4), V4, A4)
        wk_vector(tile_key(4), 0, V4)

        first_passes(2)
        d_gpsimd(1, "r1")
        pair_out(2)
        d0 = stage("b3", ds(0))
        d_copy(0, d_turn(0, "d"))
        turn_w(3)
        quantize(k[4])
        next_tile(5, "b2")

        pair_passes(3)
        d_gpsimd(2, "k2")
        pair_out(3)
        d12 = stage("b0", ds(1), ds(2))
        d_copy(1, d_turn(1, "d"))
        n46 = stage("n46", ns(4), ns(6))
        turn_w(4)
        quantize(k[5])
        quantize(d0, E5M2)
        next_tile(6, "r0")

        first_passes(4)
        d_gpsimd(3, "b3")
        pair_out(4)
        d_copy(2, d_turn(2, "d"))
        n57 = stage("n57", ns(5), ns(7))
        turn_w(5)
        quantize(k[6])
        next_tile(7, "b2")

        pair_passes(5)
        back((0, 0), (0,))
        d_gpsimd(4, "r0")
        pair_out(5)
        d3 = stage("b1", ds(3))
        d_copy(3, d_turn(3, "d"))
        turn_w(6)
        quantize(k[7])
        quantize(n23)

        first_passes(6)
        d_gpsimd(5, "b2")
        pair_out(6)
        d4 = stage("dbf0", ds(4))
        d_copy(4, d_turn(4, "d"))
        turn_w(7)
        quantize(d12, E5M2)
        quantize(d3, E5M2)

        pair_passes(7)
        d_gpsimd(6, "b0")
        pair_out(7)
        d5, d6, d7 = stage("b3", ds(5)), stage("r1", ds(6)), stage("r0", ds(7))
        d_copy(5, d_turn(5, "d"))
        back((0, 0), (1,))
        back((0, 1), (0, 1))
        back((1, 0), (0, 1))
        quantize(d4, E5M2)
        d_vector(7, "k2")
        quantize(n46)
        back((1, 1), (0, 1))
        back((2, 0), (0,))
        d_copy(6, d_turn(6, "d"))
        back((2, 1), (0,))
        back((3, 0), (0,))
        for key in ((2, 0), (2, 1), (3, 0)):
            back(key, (1,))
        d_copy(7, d_turn(7, "d"))
        quantize(d6, E5M2)
        quantize(n57)
        quantize(d5, E5M2)
        quantize(d7, E5M2)
        back((0, 0), (2, 3))
        back((1, 0), (2, 3))
        back((0, 1), (2, 3))
        back((1, 1), (2, 3))
        du_out_of_psum(0, 0)
        late = du_by_gpsimd(0, 1, "r0")
        du_out_of_psum(1, 0)
        du_out_of_psum(1, 1)
        back((2, 0), (2, 3))
        du_out_of_psum(2, 0)
        du_store(0, 1, late)
        back((3, 1), (0, 1))
        for key in ((2, 1), (3, 0), (3, 1)):
            back(key, (2, 3))
            du_out_of_psum(*key)
